import numpy as np, ml_dtypes
CORES = [8,136,40,168]
N = 4
BF = ml_dtypes.bfloat16
def gentries(a):
    return np.ascontiguousarray(a.reshape(8, 16, -1).transpose(0, 2, 1)).reshape(8, -1)
def gtable(e):
    e = np.asarray(e); return np.ascontiguousarray(e.reshape(8, -1, 16).transpose(0, 2, 1)).reshape(128, -1).astype(np.int32)
V, E, LB, ST, RO = 3072, 1024, 10, 4, 3
def parts(rng):
    Q = 8 * N; q = np.arange(Q)[:, None]; k = np.arange(V)[None, :]
    o = np.argsort(rng.random((Q, V)), axis=1)
    x = np.zeros((Q, V, 16), np.float32); x[q, o] = np.linspace(235.0, 20.0, V)[None, :, None]
    x = x + rng.integers(4, 48, (Q, 1, 1)).astype(np.float32) * rng.standard_normal((Q, V, 16), dtype=np.float32)
    x = np.clip(np.floor(x), 0, 255)
    top = rng.integers(40, 700, (Q, 1)); nx = k + rng.integers(1, top + 1, (Q, V))
    nx = np.where((nx >= V) | (rng.random((Q, V)) < 0.015625), k, nx)
    S = np.zeros((Q, V), np.int64); S[q, o] = o[q, nx]
    pa = rng.integers(0, V, (Q, E)); far = np.where(rng.random((Q, E)) < 0.5, rng.integers(1, V, (Q, E)), rng.integers(1, 301, (Q, E)))
    a = o[q, pa]; b = o[q, (pa + far) % V]
    sa = S[q, a]; b = np.where((rng.random((Q, E)) < 0.0625) & (sa != a), sa, b)
    ix = np.where(rng.random((Q, E)) < 0.0625, rng.integers(0, E, (Q, E)), np.arange(E)[None, :])
    return x, S, a[q, ix], b[q, ix]
def pack(x, S, a, b):
    return {"x": np.ascontiguousarray(np.asarray(x).reshape(N, 8, V, 16).transpose(0, 1, 3, 2)).reshape(N, 128, V).astype(np.float32).astype(BF),
            "succ": np.ascontiguousarray(S.reshape(N, 8, V)).astype(np.int32),
            "ea": np.stack([gtable(e) for e in a.reshape(N, 8, E)]), "eb": np.stack([gtable(e) for e in b.reshape(N, 8, E)])}
def setup_inputs(rng):
    return pack(*parts(rng))
def setup_inputs_ties(rng):
    x, S, a, b = parts(rng); Q = 8 * N
    D = np.zeros((5, 16), np.int64); D[1, :8] = 1; D[1, 8:] = -1; D[2, :9] = 1; D[2, 9:] = -1; D[3, 0] = 1; D[4, 15] = -1
    A = rng.integers(1, 255, (Q, 1, 16)); A[3::8] = rng.choice(np.array([0, 255]), (N, 1, 16))
    y = np.clip(A + D[rng.integers(0, 5, (Q, V))], 0, 255)
    y[5::8] = A[5::8]; y[7::8] = x[7::8].astype(np.int64)
    for i in range(6, Q, 8):
        S[i] = np.where(S[i] % (V - 1) == 0, np.arange(V), S[i]); S[i, 0] = 0; S[i, V - 1] = V - 1
        hit = (a[i] % (V - 1) == 0) | (b[i] % (V - 1) == 0)
        a[i] = np.where(hit, 1, a[i]); b[i] = np.where(hit, 2, b[i])
        j = int(rng.integers(0, E)); a[i, j] = 0; b[i, j] = V - 1
        y[i, 0] = np.minimum(y[i, 0], 200); y[i, V - 1] = y[i, 0]; y[i, V - 1, int(rng.integers(0, 16))] += 50
    return pack(y, S, a, b)
def setup_inputs_crowd(rng):
    x, S, a, b = parts(rng); k = np.arange(E); v = np.arange(V)
    used = np.array(sorted({(ST * n + j) % LB for n in range(RO) for j in range(1, ST)}))
    hub = rng.permutation(V)
    for i in range(8 * N):
        g = i % 8; p = rng.permutation(V)
        if g in (0, 2, 4):
            d = (1, ST + 1, int(rng.choice(used)))[g // 2]; m = k & ~(1 << d)
            a[i] = p[2 * m]; b[i] = p[2 * m + 1]; S[i] = v
        elif g == 1:
            y = rng.permutation(E); j = np.arange(E - 257)
            a[i, y[:257]] = hub[0]; b[i, y[:257]] = hub[1]
            a[i, y[257:]] = hub[2 + 2 * j]; b[i, y[257:]] = hub[3 + 2 * j]
            S[i] = v; x[i] = np.minimum(x[i], 254); x[i, hub[0]] = 255
        elif g == 3:
            a[i] = p[rng.integers(0, 8, E)]; b[i] = p[8 + rng.integers(0, V - 8, E)]; x[i, p[:8]] = 255
        elif g == 5 and i // 8 == N - 1:
            a[i] = p[2 * k]; b[i] = p[2 * k + 1]; S[i] = v
        elif g == 5:
            n = V // 8
            if (i // 8) % 2 == 0: H = int(rng.integers(0, V - n + 1)) + np.arange(n)
            else: H = 8 * np.arange(n) + int(rng.integers(0, 8))
            z = rng.permutation(np.setdiff1d(v, H)); y = rng.permutation(E); j = np.arange(E - n)
            w = np.concatenate([z[:(ST - 1) * n].reshape(ST - 1, n), rng.permutation(H)[None, :]]); z = z[(ST - 1) * n:]
            S[i] = v; S[i, w[:-1]] = w[1:]
            x[i] = rng.integers(0, 128, (V, 16)); x[i, w] += 128
            a[i, y[:n]] = w[0]; b[i, y[:n]] = rng.permutation(z)[:n]
            a[i, y[n:]] = z[2 * j]; b[i, y[n:]] = z[2 * j + 1]
        elif g == 6:
            y = rng.permutation(k[((k >> 1) & 1) == 0]); c = np.concatenate([k[((k >> 1) & 1) == 1], y[:1]]); j = np.arange(E // 2 - 1)
            a[i, c] = hub[0]; b[i, c] = hub[1 + rng.permutation(E // 2 + 1)]
            a[i, y[1:]] = hub[E + 2 * j]; b[i, y[1:]] = hub[E + 2 * j + 1]
            S[i] = v; x[i] = np.minimum(x[i], 254); x[i, hub[0]] = 255
        else:
            m = np.where(((k >> 1) & 1) == 1, k & ~8, k)
            a[i] = p[2 * m]; b[i] = p[2 * m + 1]; S[i] = v
    return pack(x, S, a, b)
def setup_inputs_chains(rng):
    Q = 8 * N; q = np.arange(Q)[:, None]; k = np.arange(V)[None, :]
    C = rng.choice(np.array([2, 3, 4, 8, 16]), (Q, 1)); o = np.argsort(rng.random((Q, V)), axis=1)
    nx = k + C; nx = np.where(nx >= V, k, nx)
    S = np.zeros((Q, V), np.int64); S[q, o] = o[q, nx]
    x = np.zeros((Q, V, 16)); x[q, o] = np.floor(np.linspace(250.0, 1.0, V)[None, :, None] + 0.0625 * np.arange(16)[None, None, :])
    pa = rng.integers(0, V - 32, (Q, E)); pb = pa + rng.integers(1, C, (Q, E)); turn = rng.random((Q, E)) < 0.5
    return pack(x, S, o[q, np.where(turn, pb, pa)], o[q, np.where(turn, pa, pb)])
def setup_inputs_ends(rng):
    x, S, a, b = parts(rng); v = np.arange(V)
    x[0::2] = rng.choice(np.array([0.0, 255.0]), (4 * N, V, 16))
    S[0::8] = rng.integers(0, V, (N, V)); S[1::8] = 0; S[2::8] = V - 1; S[3::8] = V - 1 - v; S[4::8] = (v + 1) % V
    S[5::8] = v ^ 1; b[5::8] = a[5::8] ^ 1
    x[5::16] = rng.integers(0, 64, (N // 2, V, 16)) + 64 * (3 - v % 4)[None, :, None]
    S[5::16] = v - v % 4 + (v + 1) % 4; a[5::16] = 4 * rng.integers(0, V // 4, (N // 2, E)); b[5::16] = a[5::16] + 2
    w = 2 + rng.permutation(V - 4); M = V - 4 - 2 * ST
    for i in range(6, 8 * N, 8):
        S[i] = v; S[i, w[2 * ST:]] = rng.choice(w[2 * ST:], M)
        u = rng.integers(0, M, E); a[i] = w[2 * ST + u]; b[i] = w[2 * ST + (u + rng.integers(1, M, E)) % M]
        for c, (e, low) in enumerate(((0, 1), (V - 1, V - 2))):
            way = np.append(w[c * ST:(c + 1) * ST], e)
            S[i, way[:-1]] = way[1:]; x[i, way] = 255; x[i, low] = 0
        j = rng.permutation(E)[:2]
        a[i, j] = np.array([w[0], V - 2]); b[i, j] = np.array([1, w[ST]])
    a[7::8] = V - 1; b[7::8] = rng.integers(0, V - 1, (N, E))
    return pack(x, S, a, b)
def setup_inputs_spread(rng):
    Q = 8 * N
    x = np.minimum(np.floor(np.exp2(8 * rng.random((Q, V, 1))) * rng.random((Q, V, 16))), 255)
    S = rng.integers(0, V, (Q, V)); S = np.where(rng.random((Q, V)) < 0.0625, np.arange(V)[None, :], S)
    a = rng.integers(0, V, (Q, E)); b = (a + rng.integers(1, V, (Q, E))) % V
    return pack(x, S, a, b)
def check_inputs(d):
    bad = []; v = np.asarray(d["x"]).astype(np.float32)
    if not np.all((v >= 0) & (v <= 255) & (v == np.floor(v))): bad.append("x")
    for k in ("succ", "ea", "eb"):
        if np.min(d[k]) < 0 or np.max(d[k]) > V - 1: bad.append("range of " + k)
    if np.any(np.asarray(d["ea"]) == np.asarray(d["eb"])): bad.append("an edge with equal ends")
    return bad
def above(X, a, b):
    q = np.arange(X.shape[0])[:, None]
    m = np.add.reduce(np.sign(X[q, a] - X[q, b]), axis=2)
    return (m > 0) | ((m == 0) & (a < b))
def reference(x, succ, ea, eb):
    Q = 8 * N; q = np.arange(Q)[:, None]; lane = np.arange(E)[None, :]; qq = np.broadcast_to(q, (Q, E))
    X = np.ascontiguousarray(x.astype(np.float32).astype(np.int32).reshape(Q, 16, V).transpose(0, 2, 1))
    S = np.array(succ, np.int64).reshape(Q, V)
    fa = np.concatenate([gentries(e) for e in ea]).astype(np.int64); fb = np.concatenate([gentries(e) for e in eb]).astype(np.int64)
    a, b = fa, fb
    for rnd in range(RO):
        up = above(X, a, b); h = np.where(up, a, b); l = np.where(up, b, a)
        done = np.zeros((Q, E), bool); out = np.zeros((Q, E), bool)
        for k in range(ST):
            act = ~done & ~out
            s = S[q, h]
            met = act & (s == l)
            walk = act & ~met & (s != h) & above(X, s, l)
            ask = act & ~met & ~walk
            place = q * V + h
            n = np.bincount(place[ask], minlength=Q * V)[place]
            sole = ask & (n == 1); into = sole & (s != h)
            S[qq[sole], h[sole]] = l[sole]
            done = done | met | (sole & (s == h))
            h, l = np.where(into, l, np.where(walk, s, h)), np.where(into, s, l)
            out = ask & (n > 1) & (((lane >> ((rnd * ST + k + 1) % LB)) & 1) == 1)
        X = X + np.clip(X[q, S] - X, -1, 1)
        a = np.roll(np.where(done, fa, h), 8, axis=0); b = np.roll(np.where(done, fb, l), 8, axis=0)
        fa = np.roll(fa, 8, axis=0); fb = np.roll(fb, 8, axis=0)
    return {"ys": S.reshape(N, 8, V).astype(np.float32), "yx": np.ascontiguousarray(X.transpose(0, 2, 1)).reshape(N, 128, V).astype(np.float32).astype(BF)}

@@ -1,0 +1,468 @@
+from concourse.mybir import AluOpType as A, ActivationFunctionType as F
+
+RO, ST, LB = 3, 4, 10
+BIG, ROOT, TOP = 131072.0, 3072, 3073
+BS, GP = 40, 46
+NV = 52
+DT = {"b": "bfloat16", "f": "float32", "i": "int32", "u": "uint16"}
+SCRATCH = {"BT": ("sbuf", [128, 128 * (64 - NV)], "bfloat16")}
+for _t in ("b3088 XA XB CT DG;b4112 SW;b1024 GE GS XL LD SG AT GF;b1536 DD XS SN XP XM;b8192 BB;"
+           "b64 AK2;f64 DL AKN;b128 FL0 FL1 BD IO IDP IDN IDF;b256 WR;b272 FT;i128 C1 FI EI;f128 C0 I32P I32N EF PF2;"
+           "b2048 SELS SELM SELF;b8 M2 S2P S2N;i1 PI GI QI;f1 PF GFC QF GC WS WT WF;f16 EQ;i192 UI VI LV W1 W2 W3 V1 V2 SI;"
+           "b192 D0 D1 D2 S0 S1;f192 Y2 Y3 VM VK;u192 SL16;i64 LN H OI BI;u128 ED EDN LP0 LP1 SP0 SP1;"
+           "f64 TR L D SH T1 H1 LH L1 OF SC SO T2 T3 NS UP N3 AK WK EL AB SIT G R1 R2 R3;"
+           "u64 G16 L16 S16 OF16 SC16").split(";"):
+    for _n in _t.split()[1:]:
+        SCRATCH[_n] = ("sbuf", [128, int(_t.split()[0][1:])], DT[_t[0]])
+for _n in ("pS", "pV", "pX", "pL", "pH"):
+    SCRATCH[_n] = ("psum", [128, 512], "float32")
+for _n in ("pT0", "pT1", "pF"):
+    SCRATCH[_n] = ("psum", [128, 1024], "bfloat16")
+PS = ("pS", "pV", "pX", "pL", "pH", "pT0", "pT1", "pF")
+SEMAPHORES = ["cv", "ca", "cp", "cg", "se", "s0", "s1", "re", "r0", "r1"] + ["d%d" % i for i in range(24)]
+SW = "SW SWh SWl"
+
+
+def rank_program(g, core, T, topo):
+    rank = T.rank_of(core)
+    if rank is None:
+        return
+    N = len(T.cores)
+    nxt, prv = T.cores[(rank + 1) % N], T.cores[(rank - 1) % N]
+    eng = {"v": g.vector, "a": g.scalar, "p": g.tensor, "g": g, "s": g.sync}
+    total, seen, wr_, rd_ = {}, {e: {} for e in eng}, {}, {}
+
+    def need(e, toks):
+        best = {}
+        for t in toks:
+            if t[0] not in best or best[t[0]][1] < t[1]:
+                best[t[0]] = t
+        for t in sorted(best.values(), key=lambda t: -len(t[3])):
+            if seen[e].get(t[0], 0) < t[1]:
+                eng[e].wait_ge(T.sem[t[0]], t[1])
+                seen[e][t[0]] = t[1]
+                for s, v in t[3].items():
+                    seen[e][s] = max(seen[e].get(s, 0), v)
+
+    def before(e, rd, wr):
+        toks = []
+        for k in rd:
+            toks += wr_.get(k, {}).values()
+            if k in PS:
+                toks += [t for t in rd_.get(k, {}).values() if t[2] != e]
+        for k in wr:
+            part = k[0] == "+" or (e == "p" and k in PS)
+            k = k.strip("+")
+            toks += [t for t in wr_.get(k, {}).values() if not (part and t[2] == e)]
+            toks += rd_.get(k, {}).values()
+        need(e, toks)
+
+    def after(tok, rd, wr):
+        for k in wr:
+            part = k[0] == "+"
+            k = k.strip("+")
+            if not part:
+                wr_[k] = {}
+            wr_.setdefault(k, {})[tok[0]] = tok
+            rd_[k] = {}
+        for k in rd:
+            if k not in wr:
+                rd_.setdefault(k, {})[tok[0]] = tok
+
+    def em(e, fn, rd, wr):
+        rd, wr = rd.split(), wr.split()
+        before(e, rd, wr)
+        s = "c" + e
+        total[s] = total.get(s, 0) + 1
+        fn().then_inc(T.sem[s], 1)
+        after((s, total[s], e, dict(seen[e])), rd, wr)
+
+    nd = [0]
+
+    def dma(e, out, in_, rd, wr):
+        rd, wr = rd.split(), wr.split()
+        before(e, rd, wr)
+        s = "d%d" % nd[0]
+        nd[0] += 1
+        total[s] = 16
+        eng[e].dma_start(out, in_).then_inc(T.sem[s], 16)
+        after((s, 16, "D", dict(seen[e])), rd, wr)
+
+    def send(out, in_, rs, ls, rd):
+        before("g", rd.split(), [])
+        rid, pid = topo.addr(nxt, core)
+        g.remote_dma(out, in_, T.sem[rs], T.sem[ls], pid, rid, topo.mask(core, nxt))
+        total[ls] = len(topo.engines(core, nxt))
+        total[rs] = len(topo.engines(prv, core))
+        after((ls, total[ls], "D", {}), rd.split(), [])
+
+    def landed(rs, key):
+        wr_[key] = {rs: (rs, total[rs], "N", {})}
+
+    def cp(out, in_, rd, wr):
+        em("v", lambda: g.vector.tensor_copy(out, in_), rd, wr)
+
+    def tt(out, a, b, op, rd, wr):
+        em("v", lambda: g.vector.tensor_tensor(out, a, b, op), rd, wr)
+
+    def ts(out, a, s1, op0, rd, wr, s2=None, op1=None):
+        if op1 is None:
+            em("v", lambda: g.vector.tensor_scalar(out, a, s1, None, op0), rd, wr)
+        else:
+            em("v", lambda: g.vector.tensor_scalar(out, a, s1, s2, op0, op1), rd, wr)
+
+    def t3(o, a, b, op):
+        tt(T[o][:], T[a][:], T[b][:], op, a + " " + b, o)
+
+    def ms(ap, c, wr):
+        em("v", lambda: g.vector.memset(ap, c), "", wr)
+
+    def act(out, in_, fn, rd, wr, bias=0.0, scale=1.0):
+        em("a", lambda: g.scalar.activation(out, in_, fn, bias=bias, scale=scale), rd, wr)
+
+    def mm(out, l, r, start, stop, rd, wr):
+        em("p", lambda: g.tensor.matmul(out, l, r, start, stop), rd, wr)
+
+    def tr(out, in_, rd, wr):
+        em("p", lambda: g.tensor.transpose(out, in_, T.IDP[:]), rd + " IDP", wr)
+
+    def gat(e, out, win, off, rd, wr):
+        if e == "v":
+            cp(out, win.indirect(off), rd, wr)
+        else:
+            act(out, win.indirect(off), F.Copy, rd, wr)
+
+    def ext(ps, key, sel, src, rd, start, n=64, o=0):
+        for q in range(16):
+            mm(ps[:, 0:n], T[sel][:, q * 128:(q + 1) * 128], src[:, 16 * o + q:16 * (o + n):16], start and q == 0, q == 15,
+               rd + " " + sel, key)
+
+    dma("s", T.EI[:, 0:64], T.ea[:], "", "EIa")
+    dma("a", T.EI[:, 64:128], T.eb[:], "", "EIb")
+    dma("a", T.SI[:], T.succ[:], "", "SI")
+    dma("s", T.XA[:, 0:3072], T.x[:], "", "X0a X0b X0c X0d")
+
+    def iota(ap, pat, cm, wr, **kw):
+        em("g", lambda: g.iota(ap, pat, 0, cm, **kw), "", wr)
+    iota(T.PI[:], [[1, 1]], 1, "PI")
+    iota(T.FI[:], [[1, 128]], 0, "FI")
+    iota(T.UI[:], [[1, 192]], 192, "UI")
+    iota(T.LV[:], [[16, 192]], 0, "LV")
+    iota(T.DG[:], [[0, 3088]], 0, "DG DG0 DG1", allow_small_or_imprecise_dtypes=True)
+    ms(T.GS[:], 0.0, "GS0 GS1")
+    for c in range(3):
+        act(T.SW[:, 1024 * c:1024 * c + 1024], T.GS[:], F.Copy, "GS0 GS1", "+SW +SWh +SWl")
+    ts(T.GI[:], T.PI[:], 4, A.arith_shift_right, "PI", "GI")
+    ts(T.QI[:], T.PI[:], 15, A.bitwise_and, "PI", "QI")
+    ms(T.SELM[:], 0.0, "SELM")
+    cp(T.GFC[:], T.GI[:], "GI", "GFC")
+    cp(T.QF[:], T.QI[:], "QI", "QF")
+    ts(T.C1[:], T.FI[:], 4, A.arith_shift_right, "FI", "C1")
+    ts(T.GC[:], T.GFC[:], -3072.0, A.mult, "GFC", "GC")
+    ts(T.EQ[:], T.FI[:, 0:16], T.QF[:], A.is_equal, "FI QF", "EQ")
+    ts(T.BD[:], T.C1[:], T.GFC[:], A.is_equal, "C1 GFC", "BD", 4096.0, A.mult)
+    ts(T.VI[:], T.UI[:], T.GC[:], A.add, "UI GC", "VI")
+    ts(T.VK[:], T.VI[:], -1.0, A.mult, "VI", "VK", float(ROOT), A.add)
+    tt(T.Y2[:], T.SI[:], T.VI[:], A.is_equal, "SI VI", "Y2")
+    tt(T.Y3[:], T.Y2[:], T.VK[:], A.mult, "Y2 VK", "Y3")
+    tt(T.W3[:], T.Y3[:], T.SI[:], A.add, "Y3 SI", "W3")
+    ts(T.W1[:], T.W3[:], 6, A.arith_shift_right, "W3", "W1")
+    ts(T.W2[:], T.W3[:], 63, A.bitwise_and, "W3", "W2")
+    cp(T.S0[:], T.W1[:], "W1", "S0")
+    cp(T.S1[:], T.W2[:], "W2", "S1")
+    dma("s", T.SW[0:128:16, 0:3072], T.S0[:], "S0", "SWh")
+    dma("s", T.SW[1:128:16, 0:3072], T.S1[:], "S1", "SWl")
+    cp(T.ED[:], T.EI[:], "EIa EIb", "ED")
+    send(T.EDN[:], T.ED[:], "re", "se", "ED")
+    for q in range(16):
+        cp(T.SELM[:, q * 128 + q:(q + 1) * 128:16], T.BD[:, 0:128:16], "BD", "SELM" if q == 0 else "+SELM")
+    ts(T.WS[:], T.EQ[:, 0:1], 64.0 / 4096, A.mult, "EQ", "WS")
+    cp(T.PF[:], T.PI[:], "PI", "PF")
+    for b in "AB":
+        ms(T["X" + b][:, 3072:3088], -1.0, "X%de" % (b == "B"))
+    ts(T.WT[:], T.EQ[:, 1:2], 1.0 / 4096, A.mult, "EQ WS", "WT", T.WS[:], A.add)
+    for b in "AB":
+        ms(T["X" + b][:, TOP:3088], 256.0, "X%de" % (b == "B"))
+    for nm, sc in (("IDN", -1.0), ("IDP", 1.0), ("I32N", -1.0)):
+        ts(T[nm][:], T.FI[:], T.PF[:], A.is_equal, "FI PF", nm, sc, A.mult)
+
+    def more_constants():
+        act(T.SELS[:], T.SELM[:], F.Identity, "SELM WT", "SELS", scale=T.WT[:])
+        ms(T.SW[:, 3072:3088], 0.0, "+SW")
+        ts(T.W1[:], T.VI[:], 127, A.bitwise_and, "VI", "W1")
+        ts(T.V1[:], T.VI[:], 6, A.arith_shift_right, "VI", "V1")
+        ts(T.V2[:], T.VI[:], 63, A.bitwise_and, "VI", "V2")
+        ts(T.SW[:, ROOT:ROOT + 1], T.EQ[:, 0:1], 48.0, A.mult, "EQ", "SW")
+        cp(T.D2[:], T.W1[:], "W1", "D2")
+        cp(T.D0[:], T.V1[:], "V1", "D0")
+        cp(T.D1[:], T.V2[:], "V2", "D1")
+        ts(T.SW[:, TOP:TOP + 1], T.EQ[:, 0:1], 48.0, A.mult, "EQ", "SW", T.EQ[:, 1:2], A.add)
+        ts(T.DG[:, ROOT:ROOT + 1], T.EQ[:, 0:1], 48.0, A.mult, "EQ", "DG")
+        dma("s", T.DG[0:128:16, 0:3072], T.D0[:], "D0", "DG0")
+        dma("s", T.DG[1:128:16, 0:3072], T.D1[:], "D1", "DG1")
+
+    def late_constants():
+        ms(T.WR[:, 0:128], 1.0, "+WR")
+        ms(T.WR[:, 128:256], 2048.0, "+WR")
+        ms(T.CT[:, 3072:3088], 0.0, "+CT +CTl")
+        for k in range(12):
+            ts(T.CT[:, 256 * k:256 * k + 256], T.WR[:], T.EQ[:, k:k + 1], A.mult, "WR EQ", "+CT +CTl")
+        dma("s", T.CT[12:128:16, 0:3072], T.D2[:], "D2", "CTl")
+        cp(T.M2[:], T.BD[:, 0:128:16], "BD", "M2")
+        ts(T.S2P[:], T.BD[:, 0:128:16], T.WT[:], A.mult, "BD WT", "S2P")
+        ts(T.S2N[:], T.BD[:, 0:128:16], T.WT[:], A.mult, "BD WT", "S2N", -1.0, A.mult)
+        cp(T.IO[:], T.FI[:], "FI", "IO")
+
+    def last_constants():
+        ts(T.LN[:], T.LV[:, 0:64], T.QF[:], A.add, "LV QF", "LN")
+        ts(T.WF[:], T.QF[:], 11.5, A.is_lt, "QF", "WF", -BIG / 4096, A.mult)
+        for nm, sc in (("IDF", 4096.0), ("I32P", 1.0)):
+            ts(T[nm][:], T.FI[:], T.PF[:], A.is_equal, "FI PF", nm, sc, A.mult)
+        ts(T.TR[:], T.LN[:], 3088.0, A.add, "LN", "TR")
+        ms(T.FT[:, 256:272], 0.0, "FT")
+        ts(T.VM[:], T.LV[:], T.QF[:], A.add, "LV QF", "VM", -float(ROOT), A.add)
+        act(T.SELF[:], T.SELM[:], F.Identity, "SELM WF", "SELF", scale=T.WF[:])
+
+    def signs(X, xk, lst, lk):
+        m = 16 * BS
+        tt(T.DD[:, 0:m], X[:].indirect(lst[:, 0:BS]), T.XL[:, 0:m], A.subtract, xk + " XL0 XL1 " + lk, "DDa")
+        gat("a", T.XS[:, 0:1024 - m], X[:], lst[:, BS:64], xk + " " + lk, "XS0")
+        mm(T.pH[:, 0:1024 - m], T.IDN[:], T.XL[:, m:1024], True, False, "IDN XL0 XL1", "pH")
+        mm(T.pH[:, 0:1024 - m], T.IDP[:], T.XS[:, 0:1024 - m], False, True, "IDP XS0", "pH")
+        act(T.SG[:, m:1024], T.pH[:, 0:1024 - m], F.Sign, "pH", "SG1")
+
+    def clip():
+        ts(T.SG[:, 0:16 * BS], T.DD[:, 0:16 * BS], 1.0, A.min, "DDa", "SG0", -1.0, A.max)
+
+    def own_x(X, xk):
+        gat("a", T.XL[:], X[:], T.L16[:], xk + " L16", "XL0 XL1")
+
+    def digits(e):
+        gat("a", T.GE[:, 0:512], T.CT[:], T.G16[:, 0:32], "CT CTl G16", "GE0")
+        gat(e, T.GE[:, 512:1024], T.CT[:], T.G16[:, 32:64], "CT CTl G16", "GE1")
+        for c in range(8):
+            tr(T["pT%d" % (c // 4)][:, 128 * (c % 4):128 * (c % 4) + 128], T.GE[:, 128 * c:128 * c + 128],
+               "GE%d" % (c // 4), "pT%d" % (c // 4))
+
+    def turned():
+        act(T.AT[:, 512:1024], T.pT1[:, 0:512], F.Copy, "pT1", "AT1")
+
+    def round_start(n, X, xk):
+        if n == 0:
+            lst, lk = T.ED, "ED"
+        else:
+            lst, lk = T["LP%d" % (n - 1)], "LP%d" % (n - 1)
+            landed("r%d" % (n - 1), lk)
+        gat("v", T.XL[:, 0:512], X[:], lst[:, 64:96], xk + " " + lk, "XL0")
+        gat("a", T.XL[:, 512:1024], X[:], lst[:, 96:128], xk + " " + lk, "XL1")
+        signs(X, xk, lst, lk)
+        clip()
+        cp(T.PF2[:], lst[:], lk, "PF2")
+        tt(T.D[:], T.PF2[:, 0:64], T.PF2[:, 64:128], A.subtract, "PF2", "D")
+        mm(T.pV[:, 0:64], T.I32N[:], T.D[:], True, False, "I32N D", "pV")
+        ext(T.pV, "pV", "SELM", T.SG, "SG0 SG1", False)
+        ms(T.SIT[:], 0.0, "SIT")
+        if n == 0:
+            more_constants()
+        if n < 2:
+            if n == 1:
+                landed("re", "EDN")
+            e = T.ED if n == 0 else T.EDN
+            cp(T.EF[:], e[:], "ED" if n == 0 else "EDN", "EF")
+        ts(T.UP[:], T.pV[:, 0:64], 0.0, A.is_gt, "pV", "UP")
+        t3("T1", "UP", "D", A.mult)
+        tt(T.L[:], T.PF2[:, 0:64], T.T1[:], A.subtract, "T1 PF2", "L")
+        tt(T.H[:], T.T1[:], T.PF2[:, 64:128], A.add, "T1 PF2", "H")
+        cp(T.L16[:], T.L[:], "L", "L16")
+        cp(T.G16[:], T.H[:], "H", "G16")
+        own_x(X, xk)
+
+    def step(n, k, X, xk):
+        last = k == ST - 1
+        final = last and n == RO - 1
+        if k == 0:
+            gat("v", T.GS[:], T.SW[:, 0:3088], T.G16[:], SW + " G16", "GS0 GS1")
+            if n == 0:
+                late_constants()
+            else:
+                digits("v")
+        else:
+            gat("v", T.GS[:, 0:512], T.SW[:, 0:3088], T.G16[:, 0:32], SW + " G16", "GS0")
+            gat("a", T.GS[:, 512:1024], T.SW[:, 0:3088], T.G16[:, 32:64], SW + " G16", "GS1")
+        ext(T.pS, "pS", "SELS", T.GS, "GS0 GS1", True)
+        gat("v", T.LD[:, 0:512], T.DG[:], T.L16[:, 0:32], "DG DG0 DG1 L16", "LD0")
+        gat("a", T.LD[:, 512:1024], T.DG[:], T.L16[:, 32:64], "DG DG0 DG1 L16", "LD1")
+        cp(T.S16[:], T.pS[:, 0:64], "pS", "S16")
+        signs(X, xk, T.S16, "S16")
+        if n == 0 and k == 0:
+            digits("a")
+        for c in range(8):
+            o = T.pL[:, 8 * c:8 * c + 8]
+            mm(o, T.GS[:, 128 * c:128 * c + 128], T.S2P[:], True, False, "GS0 GS1 S2P", "pL")
+            mm(o, T.LD[:, 128 * c:128 * c + 128], T.S2N[:], False, True, "LD0 LD1 S2N", "pL")
+        clip()
+        for c in range(8):
+            mm(T.pV[:, 8 * c:8 * c + 8], T.SG[:, 128 * c:128 * c + 128], T.M2[:], True, True,
+               "M2 SG%d" % (c >= BS // 8), "pV")
+        cp(T.DL[:], T.pL[:, 0:64], "pL", "DL")
+        tt(T.D[:], T.pS[:, 0:64], T.L[:], A.subtract, "pS L", "D")
+        cp(T.AT[:, 0:512], T.pT0[:, 0:512], "pT0", "AT0")
+        if k == 0:
+            turned()
+        tt(T.SH[:], T.pS[:, 0:64], T.H[:], A.subtract, "pS H", "SH")
+        for b in range(NV, 64):
+            o, w = 128 * (b % 8) + 16 * (b // 8) + 12, 128 * (b - NV)
+            act(T.BT[:, w:w + 128], T.IO[:], F.Abs, "IO AT%d" % (b % 8 // 4), "BT%d" % b, bias=T.AT[:, o:o + 1], scale=-1.0)
+        tt(T.AK2[:], T.pV[:, 0:64], T.DL[:], A.is_lt, "pV DL", "AK2")
+        act(T.AKN[:], T.AK2[:], F.Copy, "AK2", "AKN", scale=-1.0)
+        for b in range(64):
+            gr, c = b // 8, b % 8
+            o, a = 128 * c + 16 * gr + 12, 8 * c + gr
+            bb, ak = T.BB[:, 128 * b:128 * b + 128], T.AK2[:, a:a + 1]
+            if b < NV:
+                em("v", lambda: g.vector.tensor_scalar(bb, T.IO[:], T.AT[:, o:o + 1], ak, A.is_equal, A.mult),
+                   "IO AK2 AT%d" % (c // 4), "BB%d" % b)
+            else:
+                act(bb, T.BT[:, 128 * (b - NV):128 * (b - NV) + 128], F.Relu, "BT%d AK2 AKN" % b, "BB%d" % b,
+                    bias=ak, scale=T.AKN[:, a:a + 1])
+        mm(T.pV[:, 0:64], T.I32N[:], T.D[:], True, False, "I32N D", "pV")
+        ext(T.pV, "pV", "SELM", T.SG, "SG0 SG1", False)
+        for b in range(64):
+            gr, c = b // 8, b % 8
+            mm(T.pH[:, 16 * gr:16 * gr + 16], T.BB[:, 128 * b:128 * b + 128],
+               T.AT[:, 128 * c + 16 * gr:128 * c + 16 * gr + 16], c == 0, c == 7, "BB%d AT%d" % (b, c // 4), "pH")
+        ts(T.OI[:], T.H[:], 255, A.bitwise_and, "H", "OI")
+        ts(T.N3[:], T.pV[:, 0:64], 0.0, A.is_ge, "pV", "N3", 256.0, A.mult)
+        t3("OF", "OI", "N3", A.max)
+        cp(T.OF16[:], T.OF[:], "OF", "OF16")
+        if n == 0 and k == 0:
+            last_constants()
+        ts(T.C1[:], T.pH[:, 0:128], 1.0 / 2048, A.mult, "pH", "C1", -0.25, A.add)
+        ts(T.C0[:], T.C1[:], 2048.0, A.mult, "C1", "C0", 1.0, A.add)
+        ts(T.FL1[:], T.C1[:], 1.0, A.is_equal, "C1", "FL1")
+        tt(T.FL0[:], T.pH[:, 0:128], T.C0[:], A.is_equal, "pH C0", "FL0")
+        m = 16 * GP
+        mm(T.pS[:, 0:1024 - m], T.IDP[:], T.GE[:, m:1024], True, False, "IDP GE1", "pS")
+        mm(T.pX[:, 0:64], T.I32P[:], T.TR[:], True, False, "I32P TR", "pX")
+        tr(T.pF[:, 128:256], T.FL1[:], "FL1", "pF")
+        tr(T.pF[:, 0:128], T.FL0[:], "FL0", "pF")
+        cp(T.FT[:, 0:256], T.pF[:, 0:256], "pF", "FT")
+        tt(T.GF[:, 0:m], T.FT[:].indirect(T.OF16[:, 0:GP]), T.GE[:, 0:m], A.mult, "FT OF16 GE0 GE1", "GF0")
+        gat("a", T.XS[:, 512:1536 - m], T.FT[:], T.OF16[:, GP:64], "FT OF16", "XS1")
+        mm(T.pS[:, 0:1024 - m], T.IDF[:], T.XS[:, 512:1536 - m], False, True, "IDF XS1", "pS")
+        act(T.GF[:, m:1024], T.pS[:, 0:1024 - m], F.Relu, "pS", "GF1", bias=-4096.0)
+        ext(T.pX, "pX", "SELF", T.GF, "GF0 GF1", False)
+        if not final:
+            t3("WK", "N3", "SIT", A.is_gt)
+            ts(T.EL[:], T.D[:], 0.0, A.is_equal, "D", "EL", float(ROOT), A.mult)
+            t3("T1", "WK", "SH", A.mult)
+            t3("LH", "SH", "D", A.subtract)
+            t3("H1", "H", "T1", A.add)
+            t3("L1", "L", "EL", A.max)
+        if not last:
+            ts(T.BI[:], T.LN[:], (ST * n + k + 1) % LB, A.arith_shift_right, "LN", "BI", 1, A.bitwise_and)
+            ts(T.AK[:], T.N3[:], 0.0, A.is_equal, "N3", "AK", float(TOP), A.mult)
+            t3("AB", "AK", "BI", A.mult)
+        tt(T.SC[:], T.pX[:, 0:64], T.H[:], A.max, "pX H", "SC")
+        if not final:
+            ts(T.SO[:], T.pX[:, 0:64], 0.0, A.is_lt, "pX", "SO")
+        cp(T.SC16[:], T.SC[:], "SC", "SC16")
+        if not last:
+            ts(T.NS[:], T.pX[:, 0:64], 0.0, A.is_ge, "pX", "NS")
+        if not final:
+            t3("T2", "SO", "LH", A.mult)
+            t3("T3", "SO", "D", A.mult)
+            if not last:
+                t3("SIT", "AB", "NS", A.mult)
+            t3("H", "H1", "T2", A.add)
+            t3("L", "L1", "T3", A.add)
+            if not last:
+                t3("G", "H", "SIT", A.max)
+                cp(T.L16[:], T.L[:], "L", "L16")
+                cp(T.G16[:], T.G[:], "G", "G16")
+                digits("a")
+                own_x(X, xk)
+                turned()
+            else:
+                ts(T.UP[:], T.L[:], float(ROOT), A.is_equal, "L", "UP")
+                tt(T.T1[:], T.EF[:, 0:64], T.H[:], A.subtract, "EF H", "T1")
+                tt(T.T2[:], T.EF[:, 64:128], T.L[:], A.subtract, "EF L", "T2")
+                t3("SH", "T1", "UP", A.mult)
+                t3("D", "T2", "UP", A.mult)
+                t3("H1", "SH", "H", A.add)
+                t3("T3", "D", "L", A.add)
+                sp = "SP%d" % n
+                cp(T[sp][:, 0:64], T.H1[:], "H1", "+" + sp)
+                cp(T[sp][:, 64:128], T.T3[:], "T3", "+" + sp)
+                send(T["LP%d" % n][:], T[sp][:], "r%d" % n, "s%d" % n, sp)
+        em("v", lambda: g.vector.tensor_copy(T.SW[:].indirect(T.SC16[:]), T.LD[:]), "SC16 LD0 LD1", SW)
+        if last:
+            act(T.XP[:], X[:, 0:1536], F.Identity, xk, "XP", bias=1.0)
+            act(T.XM[:], X[:, 0:1536], F.Identity, xk, "XM", bias=-1.0)
+
+    def round_end(n, X, xk, Y, yk):
+        final = n == RO - 1
+        if final:
+            dma("s", T.D0[:], T.SW[0:128:16, 0:3072], SW, "D0")
+            dma("s", T.D1[:], T.SW[1:128:16, 0:3072], SW, "D1")
+        bank = ("pH", "pL", "pX")
+        for c in (1, 2, 0):
+            mm(T[bank[c]][:], T.IDN[:], X[:, 1536 + 512 * c:2048 + 512 * c], True, False, "IDN " + xk, bank[c])
+
+        def lists(ps, o, key):
+            ts(T.R1[:], T[ps][:, 0:64], float(ROOT), A.is_equal, ps, "R1")
+            tt(T.R2[:], T.R1[:], T.VM[:, o:o + 64], A.mult, "R1 VM", "R2")
+            tt(T.R3[:], T[ps][:, 0:64], T.R2[:], A.add, ps + " R2", "R3")
+            cp(T.SL16[:, o:o + 64], T.R3[:], "R3", key)
+        ext(T.pS, "pS", "SELS", T.SW, SW, True, 64, 128)
+        lists("pS", 128, "SLc")
+        ext(T.pV, "pV", "SELS", T.SW, SW, True, 64, 0)
+        lists("pV", 0, "SLa")
+        ext(T.pS, "pS", "SELS", T.SW, SW, True, 64, 64)
+        tt(T.DD[:, 0:1024], X[:].indirect(T.SL16[:, 0:64]), T.XP[:, 0:1024], A.min, xk + " SLa XP", "DDa")
+        lists("pS", 64, "SLb")
+        mm(T.pV[:], T.IDP[:], T.XM[:, 0:512], True, True, "IDP XM", "pV")
+        mm(T.pS[:], T.IDP[:], T.XM[:, 512:1024], True, True, "IDP XM", "pS")
+
+        def ga(c):
+            gat("a", T.XS[:, 512 * c:512 * c + 512], X[:], T.SL16[:, 96 + 32 * c:128 + 32 * c],
+                xk + (" SLc" if c else " SLb"), "XS%d" % c)
+            mm(T[bank[c]][:], T.IDP[:], T.XS[:, 512 * c:512 * c + 512], False, True, "IDP XS%d" % c, bank[c])
+
+        def sg(c):
+            act(T.SN[:, 512 * c:512 * c + 512], T[bank[c]][:], F.Sign, bank[c], "SN%d" % c)
+            o = 1536 + 512 * c
+            mm(T[bank[c]][:], T.IDP[:], X[:, o:o + 512], True, False, "IDP " + xk, bank[c])
+            mm(T[bank[c]][:], T.IDP[:], T.SN[:, 512 * c:512 * c + 512], False, True, "IDP SN%d" % c, bank[c])
+
+        def ev(c):
+            o = 1536 + 512 * c
+            act(Y[:, o:o + 512], T[bank[c]][:], F.Copy, bank[c], "+" + yk + ("b" if c else "d"))
+        ga(1), ga(2), sg(1), ga(0), sg(2), ev(1), sg(0), ev(2), ev(0)
+        tt(Y[:, 0:512], T.DD[:, 0:512], T.pV[:], A.max, "DDa pV", "+" + yk + "a")
+        tt(Y[:, 512:1024], T.DD[:, 512:1024], T.pS[:], A.max, "DDa pS", "+" + yk + "a")
+        tt(T.DD[:, 1024:1536], X[:].indirect(T.SL16[:, 64:96]), T.XP[:, 1024:1536], A.min, xk + " SLb XP", "DDb")
+        tt(Y[:, 1024:1536], T.DD[:, 1024:1536], T.XM[:, 1024:1536], A.max, "DDb XM", yk + "c")
+        if final:
+            dma("s", T.yx[:, 0:1024], Y[:, 0:1024], yk + "a", "oxa")
+            ts(T.Y2[:], T.D0[:], 64.0, A.mult, "D0", "Y2")
+            tt(T.Y3[:], T.Y2[:], T.D1[:], A.add, "Y2 D1", "Y3")
+            ts(T.Y2[:], T.Y3[:], float(ROOT), A.is_equal, "Y3", "Y2")
+            tt(T.Y2[:], T.Y2[:], T.VK[:], A.mult, "Y2 VK", "Y2")
+            tt(T.Y3[:], T.Y3[:], T.Y2[:], A.subtract, "Y3 Y2", "Y3")
+            dma("s", T.yx[:, 1024:1536], Y[:, 1024:1536], yk + "c", "oxc")
+            dma("s", T.ys[:], T.Y3[:], "Y3", "oy")
+            dma("s", T.yx[:, 2048:3072], Y[:, 2048:3072], yk + "b", "oxb")
+            dma("s", T.yx[:, 1536:2048], Y[:, 1536:2048], yk + "d", "oxd")
+
+    X, Y, xk, yk = T.XA, T.XB, "X0", "X1"
+    for n in range(RO):
+        xr = " ".join(xk + c for c in "abcde")
+        round_start(n, X, xr)
+        for k in range(ST):
+            step(n, k, X, xr)
+        round_end(n, X, xr, Y, yk)
+        X, Y, xk, yk = Y, X, yk, xk
+    for s, v in total.items():
+        if seen["g"].get(s, 0) < v:
+            g.wait_ge(T.sem[s], v)

@@ -1,26 +1,30 @@
 from concourse.mybir import AluOpType as A, ActivationFunctionType as F
 
 RO, ST, LB = 3, 4, 10
-BIG, ROOT, TOP = 131072.0, 3072, 3073
-BS, GP = 40, 46
-NV = 52
+ROOT, TOP, SIT = 3072, 3073, 8192.0
+MAGIC = 3.0 * 2 ** 33
+PIECES = (("v", 0, 2, "pA"), ("v", 2, 4, "pB"), ("a", 4, 8, "pC"))
+GP = 46
+NA = 10
+RS = 36
+RE = (24, 28, 28)
+PB, PC, VB, VC = 4, 12, 14, 28
 DT = {"b": "bfloat16", "f": "float32", "i": "int32", "u": "uint16"}
-SCRATCH = {"BT": ("sbuf", [128, 128 * (64 - NV)], "bfloat16")}
-for _t in ("b3088 XA XB CT DG;b4112 SW;b1024 GE GS XL LD SG AT GF;b1536 DD XS SN XP XM;b8192 BB;"
-           "b64 AK2;f64 DL AKN;b128 FL0 FL1 BD IO IDP IDN IDF;b256 WR;b272 FT;i128 C1 FI EI;f128 C0 I32P I32N EF PF2;"
-           "b2048 SELS SELM SELF;b8 M2 S2P S2N;i1 PI GI QI;f1 PF GFC QF GC WS WT WF;f16 EQ;i192 UI VI LV W1 W2 W3 V1 V2 SI;"
-           "b192 D0 D1 D2 S0 S1;f192 Y2 Y3 VM VK;u192 SL16;i64 LN H OI BI;u128 ED EDN LP0 LP1 SP0 SP1;"
-           "f64 TR L D SH T1 H1 LH L1 OF SC SO T2 T3 NS UP N3 AK WK EL AB SIT G R1 R2 R3;"
-           "u64 G16 L16 S16 OF16 SC16").split(";"):
+SCRATCH = {"BT": ("sbuf", [128, 128 * max(NA, 1)], "bfloat16")}
+for _t in ("b3088 XA XB CT DG;b4112 SW;b1024 GE GS XL LD SG AT GF;b1536 XS SN;b3072 DD XP XM;b8192 BB;b512 GN;"
+           "b64 AK2 S2N;f64 AKN;b128 FL0 FL1 IO IDP IDN NEG;b256 WR FT IH IL B2;i128 EI;f128 RR EF PF2;"
+           "b2048 SELS SELM SELT;b8 M2 S2P;i1 PI GI QI;f1 PF GFC QF GC WT WU EH EO N12 N13;f16 EQ EC GQ KB;i4 BI;f4 BC;"
+           "i192 UI VI W1 W2 SI;b192 D0 D1 S0 S1;f192 Y2 Y3 NEW BASE DV;u192 SL16;i64 LV H OI GX;"
+           "u128 ED EDN LP0 LP1 SP0 SP1 GL16;f256 BW;"
+           "f64 D DS K HT GA E1 E2 S2 EL UP T1;u64 S16 OF16 SC16").split(";"):
     for _n in _t.split()[1:]:
         SCRATCH[_n] = ("sbuf", [128, int(_t.split()[0][1:])], DT[_t[0]])
-for _n in ("pS", "pV", "pX", "pL", "pH"):
+PS = ("pS", "pA", "pB", "pC", "pD", "pH", "pW", "pT")
+for _n in PS[:-1]:
     SCRATCH[_n] = ("psum", [128, 512], "float32")
-for _n in ("pT0", "pT1", "pF"):
-    SCRATCH[_n] = ("psum", [128, 1024], "bfloat16")
-PS = ("pS", "pV", "pX", "pL", "pH", "pT0", "pT1", "pF")
+SCRATCH["pT"] = ("psum", [128, 1024], "bfloat16")
 SEMAPHORES = ["cv", "ca", "cp", "cg", "se", "s0", "s1", "re", "r0", "r1"] + ["d%d" % i for i in range(24)]
-SW = "SW SWh SWl"
+SW = "SW SW0 SW1 SW2 SW3"
 
 
 def rank_program(g, core, T, topo):
@@ -132,120 +136,118 @@ def rank_program(g, core, T, topo):
         else:
             act(out, win.indirect(off), F.Copy, rd, wr)
 
-    def ext(ps, key, sel, src, rd, start, n=64, o=0):
+    def ext(key, sel, src, rd, o=0):
         for q in range(16):
-            mm(ps[:, 0:n], T[sel][:, q * 128:(q + 1) * 128], src[:, 16 * o + q:16 * (o + n):16], start and q == 0, q == 15,
+            mm(T[key][:, 0:64], T[sel][:, q * 128:(q + 1) * 128], src[:, 16 * o + q:16 * (o + 64):16], q == 0, q == 15,
                rd + " " + sel, key)
 
-    dma("s", T.EI[:, 0:64], T.ea[:], "", "EIa")
-    dma("a", T.EI[:, 64:128], T.eb[:], "", "EIb")
-    dma("a", T.SI[:], T.succ[:], "", "SI")
-    dma("s", T.XA[:, 0:3072], T.x[:], "", "X0a X0b X0c X0d")
+    def iota(nm, pat, cm, a=0, b=None):
+        kw = {} if SCRATCH[nm][2] == "int32" else {"allow_small_or_imprecise_dtypes": True}
+        em("g", lambda: g.iota(T[nm][:, a:b or SCRATCH[nm][1][1]], pat, 0, cm, **kw), "", "+" + nm)
 
-    def iota(ap, pat, cm, wr, **kw):
-        em("g", lambda: g.iota(ap, pat, 0, cm, **kw), "", wr)
-    iota(T.PI[:], [[1, 1]], 1, "PI")
-    iota(T.FI[:], [[1, 128]], 0, "FI")
-    iota(T.UI[:], [[1, 192]], 192, "UI")
-    iota(T.LV[:], [[16, 192]], 0, "LV")
-    iota(T.DG[:], [[0, 3088]], 0, "DG DG0 DG1", allow_small_or_imprecise_dtypes=True)
-    ms(T.GS[:], 0.0, "GS0 GS1")
-    for c in range(3):
-        act(T.SW[:, 1024 * c:1024 * c + 1024], T.GS[:], F.Copy, "GS0 GS1", "+SW +SWh +SWl")
-    ts(T.GI[:], T.PI[:], 4, A.arith_shift_right, "PI", "GI")
+    GN_, LN_ = T.NEW[:, 64:128], T.NEW[:, 128:192]
+
+    dma("s", T.SI[:], T.succ[:], "", "SI")
+    dma("a", T.EI[:, 0:64], T.ea[:], "", "EIa")
+    dma("a", T.EI[:, 64:128], T.eb[:], "", "EIb")
+    dma("s", T.XA[:, 0:3072], T.x[:], "", "X0a X0b X0c X0d X0f X0g")
+
+    iota("PI", [[1, 1]], 1)
+    iota("IO", [[1, 128]], 0)
+    iota("UI", [[1, 192]], 192)
+    iota("IH", [[1, 4], [0, 64]], 0)
+    iota("IL", [[0, 4], [1, 64]], 0)
+    ms(T.SW[:, 0:3088], 0.0, SW)
+    ts(T.GI[:], T.PI[:], 112, A.bitwise_and, "PI", "GI")
     ts(T.QI[:], T.PI[:], 15, A.bitwise_and, "PI", "QI")
-    ms(T.SELM[:], 0.0, "SELM")
+    cp(T.PF[:], T.PI[:], "PI", "PF")
     cp(T.GFC[:], T.GI[:], "GI", "GFC")
     cp(T.QF[:], T.QI[:], "QI", "QF")
-    ts(T.C1[:], T.FI[:], 4, A.arith_shift_right, "FI", "C1")
-    ts(T.GC[:], T.GFC[:], -3072.0, A.mult, "GFC", "GC")
-    ts(T.EQ[:], T.FI[:, 0:16], T.QF[:], A.is_equal, "FI QF", "EQ")
-    ts(T.BD[:], T.C1[:], T.GFC[:], A.is_equal, "C1 GFC", "BD", 4096.0, A.mult)
-    ts(T.VI[:], T.UI[:], T.GC[:], A.add, "UI GC", "VI")
-    ts(T.VK[:], T.VI[:], -1.0, A.mult, "VI", "VK", float(ROOT), A.add)
-    tt(T.Y2[:], T.SI[:], T.VI[:], A.is_equal, "SI VI", "Y2")
-    tt(T.Y3[:], T.Y2[:], T.VK[:], A.mult, "Y2 VK", "Y3")
-    tt(T.W3[:], T.Y3[:], T.SI[:], A.add, "Y3 SI", "W3")
-    ts(T.W1[:], T.W3[:], 6, A.arith_shift_right, "W3", "W1")
-    ts(T.W2[:], T.W3[:], 63, A.bitwise_and, "W3", "W2")
-    cp(T.S0[:], T.W1[:], "W1", "S0")
-    cp(T.S1[:], T.W2[:], "W2", "S1")
-    dma("s", T.SW[0:128:16, 0:3072], T.S0[:], "S0", "SWh")
-    dma("s", T.SW[1:128:16, 0:3072], T.S1[:], "S1", "SWl")
-    cp(T.ED[:], T.EI[:], "EIa EIb", "ED")
-    send(T.EDN[:], T.ED[:], "re", "se", "ED")
-    for q in range(16):
-        cp(T.SELM[:, q * 128 + q:(q + 1) * 128:16], T.BD[:, 0:128:16], "BD", "SELM" if q == 0 else "+SELM")
-    ts(T.WS[:], T.EQ[:, 0:1], 64.0 / 4096, A.mult, "EQ", "WS")
-    cp(T.PF[:], T.PI[:], "PI", "PF")
     for b in "AB":
         ms(T["X" + b][:, 3072:3088], -1.0, "X%de" % (b == "B"))
-    ts(T.WT[:], T.EQ[:, 1:2], 1.0 / 4096, A.mult, "EQ WS", "WT", T.WS[:], A.add)
+    ts(T.GQ[:], T.IO[:, 0:16], T.GFC[:], A.add, "IO GFC", "GQ")
+    ts(T.EQ[:], T.IO[:, 0:16], T.QF[:], A.is_equal, "IO QF", "EQ")
+    ts(T.GC[:], T.GFC[:], -192.0, A.mult, "GFC", "GC")
     for b in "AB":
         ms(T["X" + b][:, TOP:3088], 256.0, "X%de" % (b == "B"))
-    for nm, sc in (("IDN", -1.0), ("IDP", 1.0), ("I32N", -1.0)):
-        ts(T[nm][:], T.FI[:], T.PF[:], A.is_equal, "FI PF", nm, sc, A.mult)
+    tt(T.EH[:], T.EQ[:, 0:1], T.EQ[:, 2:3], A.add, "EQ", "EH")
+    tt(T.EO[:], T.EQ[:, 1:2], T.EQ[:, 3:4], A.add, "EQ", "EO")
+    ts(T.VI[:], T.UI[:], T.GC[:], A.add, "UI GC", "VI")
+    ts(T.WT[:], T.EQ[:, 0:1], 64.0, A.mult, "EQ", "WT", T.EQ[:, 1:2], A.add)
+    ts(T.WU[:], T.EQ[:, 2:3], 64.0, A.mult, "EQ", "WU", T.EQ[:, 3:4], A.add)
+    ts(T.WR[:], T.IH[:], T.EH[:], A.mult, "IH EH", "WR")
+    ts(T.FT[:], T.IL[:], T.EO[:], A.mult, "IL EO", "FT")
+    ts(T.KB[:], T.IO[:, 0:16], T.EH[:], A.mult, "IO EH", "KB", 4.0, A.mult)
+    tt(T.B2[:], T.WR[:], T.FT[:], A.add, "WR FT", "B2")
+    for k in range(13):
+        w = 256 if k < 12 else 16
+        act(T.DG[:, 256 * k:256 * k + w], T.B2[:, 0:w], F.Identity, "B2 KB", "+DG", bias=T.KB[:, k:k + 1])
+    for q in range(16):
+        ts(T.SELM[:, q * 128:(q + 1) * 128], T.IO[:], T.GQ[:, q:q + 1], A.is_equal, "IO GQ", "+SELM")
+    act(T.SELS[:], T.SELM[:], F.Identity, "SELM WT", "SELS", scale=T.WT[:])
+    tt(T.Y2[:], T.SI[:], T.VI[:], A.not_equal, "SI VI", "Y2")
+    ts(T.W1[:], T.SI[:], 6, A.arith_shift_right, "SI", "W1")
+    ts(T.W2[:], T.SI[:], 63, A.bitwise_and, "SI", "W2")
+    ts(T.Y3[:], T.Y2[:], -48.0, A.mult, "Y2", "Y3", 48.0, A.add)
+    tt(T.S1[:], T.W2[:], T.Y2[:], A.mult, "W2 Y2", "S1")
+    dma("s", T.SW[1:128:16, 0:3072], T.S1[:], "S1", "SW1")
+    tt(T.S0[:], T.W1[:], T.Y3[:], A.max, "W1 Y3", "S0")
+    dma("s", T.SW[0:128:16, 0:3072], T.S0[:], "S0", "SW0")
+    cp(T.ED[:], T.EI[:], "EIa EIb", "ED")
+    send(T.EDN[:], T.ED[:], "re", "se", "ED")
+    iota("LV", [[16, 64]], 0)
+    for i, b in enumerate((1, 2, 3, 5)):
+        iota("BW", [[0, 32 >> b], [int(SIT), 2], [0, 1 << b]], 0, 64 * i, 64 * i + 64)
+    cp(T.D0[:], T.W1[:], "W1", "D0")
+    cp(T.D1[:], T.W2[:], "W2", "D1")
+    dma("s", T.SW[2:128:16, 0:3072], T.D0[:], "D0", "SW2")
+    dma("s", T.SW[3:128:16, 0:3072], T.D1[:], "D1", "SW3")
+    for nm, sc in (("IDN", -1.0), ("IDP", 1.0)):
+        ts(T[nm][:], T.IO[:], T.PF[:], A.is_equal, "IO PF", nm, sc, A.mult)
+    ts(T.N12[:], T.EQ[:, 12:13], -1.0, A.mult, "EQ", "N12", 1.0, A.add)
+    ts(T.N13[:], T.EQ[:, 12:13], -2048.0, A.mult, "EQ", "N13", 2048.0, A.add)
+    ts(T.EC[:], T.EQ[:], T.EQ[:, 12:13], A.max, "EQ", "EC")
+    ts(T.WR[:, 0:128], T.IO[:], T.EQ[:, 12:13], A.mult, "IO EQ N12", "WR", T.N12[:], A.add)
+    ts(T.WR[:, 128:256], T.IO[:], T.EQ[:, 12:13], A.mult, "IO EQ N13", "+WR", T.N13[:], A.add)
+    ms(T.CT[:, 3072:3088], 0.0, "+CT")
+    for k in range(12):
+        if k < 6:
+            ts(T.CT[:, 256 * k:256 * k + 256], T.WR[:], T.EC[:, k:k + 1], A.mult, "WR EC", "+CT")
+        else:
+            act(T.CT[:, 256 * k:256 * k + 256], T.WR[:], F.Identity, "WR EC", "+CT", scale=T.EC[:, k:k + 1])
 
     def more_constants():
-        act(T.SELS[:], T.SELM[:], F.Identity, "SELM WT", "SELS", scale=T.WT[:])
-        ms(T.SW[:, 3072:3088], 0.0, "+SW")
-        ts(T.W1[:], T.VI[:], 127, A.bitwise_and, "VI", "W1")
-        ts(T.V1[:], T.VI[:], 6, A.arith_shift_right, "VI", "V1")
-        ts(T.V2[:], T.VI[:], 63, A.bitwise_and, "VI", "V2")
-        ts(T.SW[:, ROOT:ROOT + 1], T.EQ[:, 0:1], 48.0, A.mult, "EQ", "SW")
-        cp(T.D2[:], T.W1[:], "W1", "D2")
-        cp(T.D0[:], T.V1[:], "V1", "D0")
-        cp(T.D1[:], T.V2[:], "V2", "D1")
-        ts(T.SW[:, TOP:TOP + 1], T.EQ[:, 0:1], 48.0, A.mult, "EQ", "SW", T.EQ[:, 1:2], A.add)
-        ts(T.DG[:, ROOT:ROOT + 1], T.EQ[:, 0:1], 48.0, A.mult, "EQ", "DG")
-        dma("s", T.DG[0:128:16, 0:3072], T.D0[:], "D0", "DG0")
-        dma("s", T.DG[1:128:16, 0:3072], T.D1[:], "D1", "DG1")
-
-    def late_constants():
-        ms(T.WR[:, 0:128], 1.0, "+WR")
-        ms(T.WR[:, 128:256], 2048.0, "+WR")
-        ms(T.CT[:, 3072:3088], 0.0, "+CT +CTl")
-        for k in range(12):
-            ts(T.CT[:, 256 * k:256 * k + 256], T.WR[:], T.EQ[:, k:k + 1], A.mult, "WR EQ", "+CT +CTl")
-        dma("s", T.CT[12:128:16, 0:3072], T.D2[:], "D2", "CTl")
-        cp(T.M2[:], T.BD[:, 0:128:16], "BD", "M2")
-        ts(T.S2P[:], T.BD[:, 0:128:16], T.WT[:], A.mult, "BD WT", "S2P")
-        ts(T.S2N[:], T.BD[:, 0:128:16], T.WT[:], A.mult, "BD WT", "S2N", -1.0, A.mult)
-        cp(T.IO[:], T.FI[:], "FI", "IO")
+        cp(T.SW[:, ROOT:ROOT + 2], T.DG[:, ROOT:ROOT + 2], "DG", "SW")
+        ms(T.S2N[:], 0.0, "S2N")
+        ms(T.NEG[:], -1.0, "NEG")
+        sel = T.SELM[:, 0:128:16]
+        ts(T.M2[:], sel, 4096.0, A.mult, "SELM", "M2")
+        ts(T.S2P[:], sel, T.WT[:], A.mult, "SELM WT", "S2P")
+        ts(T.S2N[:, 0:8], sel, T.WT[:], A.mult, "SELM WT", "S2N", -1.0, A.mult)
 
     def last_constants():
-        ts(T.LN[:], T.LV[:, 0:64], T.QF[:], A.add, "LV QF", "LN")
-        ts(T.WF[:], T.QF[:], 11.5, A.is_lt, "QF", "WF", -BIG / 4096, A.mult)
-        for nm, sc in (("IDF", 4096.0), ("I32P", 1.0)):
-            ts(T[nm][:], T.FI[:], T.PF[:], A.is_equal, "FI PF", nm, sc, A.mult)
-        ts(T.TR[:], T.LN[:], 3088.0, A.add, "LN", "TR")
-        ms(T.FT[:, 256:272], 0.0, "FT")
-        ts(T.VM[:], T.LV[:], T.QF[:], A.add, "LV QF", "VM", -float(ROOT), A.add)
-        act(T.SELF[:], T.SELM[:], F.Identity, "SELM WF", "SELF", scale=T.WF[:])
-
-    def signs(X, xk, lst, lk):
-        m = 16 * BS
-        tt(T.DD[:, 0:m], X[:].indirect(lst[:, 0:BS]), T.XL[:, 0:m], A.subtract, xk + " XL0 XL1 " + lk, "DDa")
-        gat("a", T.XS[:, 0:1024 - m], X[:], lst[:, BS:64], xk + " " + lk, "XS0")
-        mm(T.pH[:, 0:1024 - m], T.IDN[:], T.XL[:, m:1024], True, False, "IDN XL0 XL1", "pH")
-        mm(T.pH[:, 0:1024 - m], T.IDP[:], T.XS[:, 0:1024 - m], False, True, "IDP XS0", "pH")
-        act(T.SG[:, m:1024], T.pH[:, 0:1024 - m], F.Sign, "pH", "SG1")
-
-    def clip():
-        ts(T.SG[:, 0:16 * BS], T.DD[:, 0:16 * BS], 1.0, A.min, "DDa", "SG0", -1.0, A.max)
-
-    def own_x(X, xk):
-        gat("a", T.XL[:], X[:], T.L16[:], xk + " L16", "XL0 XL1")
+        for u in range(4):
+            ts(T.BI[:, u:u + 1], T.QI[:], u, A.arith_shift_right, "QI", "+BI", 1, A.bitwise_and)
+        ts(T.BASE[:, 0:64], T.LV[:], T.QF[:], A.add, "LV QF", "TR", 3088.0, A.add)
+        ts(T.BC[:], T.BI[:], SIT, A.mult, "BI", "BC")
 
     def digits(e):
-        gat("a", T.GE[:, 0:512], T.CT[:], T.G16[:, 0:32], "CT CTl G16", "GE0")
-        gat(e, T.GE[:, 512:1024], T.CT[:], T.G16[:, 32:64], "CT CTl G16", "GE1")
-        for c in range(8):
-            tr(T["pT%d" % (c // 4)][:, 128 * (c % 4):128 * (c % 4) + 128], T.GE[:, 128 * c:128 * c + 128],
-               "GE%d" % (c // 4), "pT%d" % (c // 4))
+        gat("a", T.GE[:, 0:512], T.CT[:], T.GL16[:, 0:32], "CT GL16", "GE0")
+        gat(e, T.GE[:, 512:1024], T.CT[:], T.GL16[:, 32:64], "CT GL16", "GE1")
 
-    def turned():
-        act(T.AT[:, 512:1024], T.pT1[:, 0:512], F.Copy, "pT1", "AT1")
+    def turn():
+        for c in range(8):
+            tr(T.pT[:, 128 * c:128 * c + 128], T.GE[:, 128 * c:128 * c + 128], "GE%d" % (c // 4), "pT")
+
+    def turned(e, h):
+        o, i = T.AT[:, 512 * h:512 * h + 512], T.pT[:, 512 * h:512 * h + 512]
+        if e == "v":
+            cp(o, i, "pT", "AT%d" % h)
+        else:
+            act(o, i, F.Copy, "pT", "AT%d" % h)
+
+    def own_x(e, X, xk, a, b, key):
+        gat(e, T.XL[:, 16 * a:16 * b], X[:], T.GL16[:, 64 + a:64 + b], xk + " GL16", key)
 
     def round_start(n, X, xk):
         if n == 0:
@@ -253,15 +255,19 @@ def rank_program(g, core, T, topo):
         else:
             lst, lk = T["LP%d" % (n - 1)], "LP%d" % (n - 1)
             landed("r%d" % (n - 1), lk)
-        gat("v", T.XL[:, 0:512], X[:], lst[:, 64:96], xk + " " + lk, "XL0")
-        gat("a", T.XL[:, 512:1024], X[:], lst[:, 96:128], xk + " " + lk, "XL1")
-        signs(X, xk, lst, lk)
-        clip()
+        m, w = 16 * RS, 1024 - 16 * RS
+        gat("v", T.XL[:, 0:m], X[:], lst[:, 64:64 + RS], xk + " " + lk, "XL0")
+        gat("a", T.XL[:, m:1024], X[:], lst[:, 64 + RS:128], xk + " " + lk, "XL1")
+        mm(T.pD[:, 0:w], T.IDN[:], T.XL[:, m:1024], True, False, "IDN XL1", "pD")
+        gat("a", T.XS[:, 0:w], X[:], lst[:, RS:64], xk + " " + lk, "XS0")
+        mm(T.pD[:, 0:w], T.IDP[:], T.XS[:, 0:w], False, True, "IDP XS0", "pD")
+        act(T.SG[:, m:1024], T.pD[:, 0:w], F.Sign, "pD", "SGpC")
+        tt(T.DD[:, 0:m], X[:].indirect(lst[:, 0:RS]), T.XL[:, 0:m], A.subtract, xk + " XL0 " + lk, "DDpA DDpB")
+        ts(T.SG[:, 0:m], T.DD[:, 0:m], 1.0, A.min, "DDpA DDpB", "SGpA SGpB", -1.0, A.max)
+        ext("pA", "SELM", T.SG, "SGpA SGpB SGpC")
         cp(T.PF2[:], lst[:], lk, "PF2")
         tt(T.D[:], T.PF2[:, 0:64], T.PF2[:, 64:128], A.subtract, "PF2", "D")
-        mm(T.pV[:, 0:64], T.I32N[:], T.D[:], True, False, "I32N D", "pV")
-        ext(T.pV, "pV", "SELM", T.SG, "SG0 SG1", False)
-        ms(T.SIT[:], 0.0, "SIT")
+        ts(T.DS[:], T.D[:], 1.0 / 4096, A.mult, "D", "DS")
         if n == 0:
             more_constants()
         if n < 2:
@@ -269,195 +275,269 @@ def rank_program(g, core, T, topo):
                 landed("re", "EDN")
             e = T.ED if n == 0 else T.EDN
             cp(T.EF[:], e[:], "ED" if n == 0 else "EDN", "EF")
-        ts(T.UP[:], T.pV[:, 0:64], 0.0, A.is_gt, "pV", "UP")
-        t3("T1", "UP", "D", A.mult)
-        tt(T.L[:], T.PF2[:, 0:64], T.T1[:], A.subtract, "T1 PF2", "L")
-        tt(T.H[:], T.T1[:], T.PF2[:, 64:128], A.add, "T1 PF2", "H")
-        cp(T.L16[:], T.L[:], "L", "L16")
-        cp(T.G16[:], T.H[:], "H", "G16")
-        own_x(X, xk)
+        tt(T.UP[:], T.pA[:, 0:64], T.DS[:], A.is_gt, "pA DS", "UP")
+        tt(T.pW[:, 0:64], T.UP[:], T.D[:], A.mult, "UP D", "pW")
+        tt(GN_, T.pW[:, 0:64], T.PF2[:, 64:128], A.add, "pW PF2", "+NEW")
+        tt(LN_, T.PF2[:, 0:64], T.pW[:, 0:64], A.subtract, "pW PF2", "+NEW")
+        cp(T.GL16[:], T.NEW[:, 64:192], "NEW", "GL16")
 
     def step(n, k, X, xk):
         last = k == ST - 1
         final = last and n == RO - 1
+        sa = 128 * PIECES[2][1]
+        gat("v", T.GS[:, 0:512], T.SW[:, 0:3088], T.GL16[:, 0:32], SW + " GL16", "GS0")
+        gat("a", T.GS[:, 512:1024], T.SW[:, 0:3088], T.GL16[:, 32:64], SW + " GL16", "GS1")
+        ext("pS", "SELS", T.GS, "GS0 GS1")
         if k == 0:
-            gat("v", T.GS[:], T.SW[:, 0:3088], T.G16[:], SW + " G16", "GS0 GS1")
-            if n == 0:
-                late_constants()
-            else:
-                digits("v")
+            own_x("v", X, xk, 0, sa // 16, "XL0")
+            gat("a", T.LD[:, 0:512], T.DG[:], T.GL16[:, 64:96], "DG GL16", "LD0")
+            own_x("a", X, xk, sa // 16, 64, "XL1")
+            mm(T.pD[:, 0:1024 - sa], T.IDN[:], T.XL[:, sa:1024], True, False, "IDN XL1", "pD")
         else:
-            gat("v", T.GS[:, 0:512], T.SW[:, 0:3088], T.G16[:, 0:32], SW + " G16", "GS0")
-            gat("a", T.GS[:, 512:1024], T.SW[:, 0:3088], T.G16[:, 32:64], SW + " G16", "GS1")
-        ext(T.pS, "pS", "SELS", T.GS, "GS0 GS1", True)
-        gat("v", T.LD[:, 0:512], T.DG[:], T.L16[:, 0:32], "DG DG0 DG1 L16", "LD0")
-        gat("a", T.LD[:, 512:1024], T.DG[:], T.L16[:, 32:64], "DG DG0 DG1 L16", "LD1")
+            gat("v", T.LD[:, 0:512], T.DG[:], T.GL16[:, 64:96], "DG GL16", "LD0")
+            gat("a", T.LD[:, 512:1024], T.DG[:], T.GL16[:, 96:128], "DG GL16", "LD1")
+            turned("v", 0)
         cp(T.S16[:], T.pS[:, 0:64], "pS", "S16")
-        signs(X, xk, T.S16, "S16")
-        if n == 0 and k == 0:
-            digits("a")
-        for c in range(8):
-            o = T.pL[:, 8 * c:8 * c + 8]
-            mm(o, T.GS[:, 128 * c:128 * c + 128], T.S2P[:], True, False, "GS0 GS1 S2P", "pL")
-            mm(o, T.LD[:, 128 * c:128 * c + 128], T.S2N[:], False, True, "LD0 LD1 S2N", "pL")
-        clip()
-        for c in range(8):
-            mm(T.pV[:, 8 * c:8 * c + 8], T.SG[:, 128 * c:128 * c + 128], T.M2[:], True, True,
-               "M2 SG%d" % (c >= BS // 8), "pV")
-        cp(T.DL[:], T.pL[:, 0:64], "pL", "DL")
-        tt(T.D[:], T.pS[:, 0:64], T.L[:], A.subtract, "pS L", "D")
-        cp(T.AT[:, 0:512], T.pT0[:, 0:512], "pT0", "AT0")
+
+        def ties(bank, a, b):
+            for c in range(a, b):
+                w = 8 * (b - a) if c == a else 8
+                mm(T[bank][:, 8 * (c - a):8 * (c - a) + w], T.GS[:, 128 * c:128 * c + 128], T.S2N[:, 0:w], c == a, False,
+                   "GS%d S2N" % (c // 4), bank)
+            for c in range(a, b):
+                mm(T[bank][:, 8 * (c - a):8 * (c - a) + 8], T.LD[:, 128 * c:128 * c + 128], T.S2P[:], False, False,
+                   "LD%d S2P" % (c // 4), bank)
+
+        def diff(bank, a, b):
+            tt(T.DD[:, 128 * a:128 * b], X[:].indirect(T.S16[:, 8 * a:8 * b]), T.XL[:, 128 * a:128 * b], A.subtract,
+               xk + " XL0 S16", "DD" + bank)
+
+        def clip(bank, a, b):
+            ts(T.SG[:, 128 * a:128 * b], T.DD[:, 128 * a:128 * b], 1.0, A.min, "DD" + bank, "SG" + bank, -1.0, A.max)
+
+        def votes(bank, a, b):
+            for c in range(a, b):
+                mm(T[bank][:, 8 * (c - a):8 * (c - a) + 8], T.SG[:, 128 * c:128 * c + 128], T.M2[:], False, c == b - 1,
+                   "M2 SG" + bank, bank)
+
+        def asks(bank, a, b):
+            ts(T.AK2[:, 8 * a:8 * b], T[bank][:, 0:8 * (b - a)], 0.0, A.is_lt, bank, "AK" + bank)
+
+        p0, p1, p2 = [(p[3], p[1], p[2]) for p in PIECES]
+        diff(*p0)
+        gat("a", T.XS[:, 0:1024 - sa], X[:], T.S16[:, sa // 16:64], xk + " S16", "XS0")
         if k == 0:
-            turned()
-        tt(T.SH[:], T.pS[:, 0:64], T.H[:], A.subtract, "pS H", "SH")
-        for b in range(NV, 64):
-            o, w = 128 * (b % 8) + 16 * (b // 8) + 12, 128 * (b - NV)
-            act(T.BT[:, w:w + 128], T.IO[:], F.Abs, "IO AT%d" % (b % 8 // 4), "BT%d" % b, bias=T.AT[:, o:o + 1], scale=-1.0)
-        tt(T.AK2[:], T.pV[:, 0:64], T.DL[:], A.is_lt, "pV DL", "AK2")
-        act(T.AKN[:], T.AK2[:], F.Copy, "AK2", "AKN", scale=-1.0)
-        for b in range(64):
-            gr, c = b // 8, b % 8
-            o, a = 128 * c + 16 * gr + 12, 8 * c + gr
-            bb, ak = T.BB[:, 128 * b:128 * b + 128], T.AK2[:, a:a + 1]
-            if b < NV:
-                em("v", lambda: g.vector.tensor_scalar(bb, T.IO[:], T.AT[:, o:o + 1], ak, A.is_equal, A.mult),
-                   "IO AK2 AT%d" % (c // 4), "BB%d" % b)
-            else:
-                act(bb, T.BT[:, 128 * (b - NV):128 * (b - NV) + 128], F.Relu, "BT%d AK2 AKN" % b, "BB%d" % b,
-                    bias=ak, scale=T.AKN[:, a:a + 1])
-        mm(T.pV[:, 0:64], T.I32N[:], T.D[:], True, False, "I32N D", "pV")
-        ext(T.pV, "pV", "SELM", T.SG, "SG0 SG1", False)
-        for b in range(64):
-            gr, c = b // 8, b % 8
-            mm(T.pH[:, 16 * gr:16 * gr + 16], T.BB[:, 128 * b:128 * b + 128],
-               T.AT[:, 128 * c + 16 * gr:128 * c + 16 * gr + 16], c == 0, c == 7, "BB%d AT%d" % (b, c // 4), "pH")
-        ts(T.OI[:], T.H[:], 255, A.bitwise_and, "H", "OI")
-        ts(T.N3[:], T.pV[:, 0:64], 0.0, A.is_ge, "pV", "N3", 256.0, A.mult)
-        t3("OF", "OI", "N3", A.max)
-        cp(T.OF16[:], T.OF[:], "OF", "OF16")
-        if n == 0 and k == 0:
-            last_constants()
-        ts(T.C1[:], T.pH[:, 0:128], 1.0 / 2048, A.mult, "pH", "C1", -0.25, A.add)
-        ts(T.C0[:], T.C1[:], 2048.0, A.mult, "C1", "C0", 1.0, A.add)
-        ts(T.FL1[:], T.C1[:], 1.0, A.is_equal, "C1", "FL1")
-        tt(T.FL0[:], T.pH[:, 0:128], T.C0[:], A.is_equal, "pH C0", "FL0")
+            digits("a")
+        ties(*p0)
+        if k:
+            ties(*p1), ties(*p2)
+        clip(*p0)
+        votes(*p0)
+        if k == 0:
+            gat("v", T.LD[:, 512:1024], T.DG[:], T.GL16[:, 96:128], "DG GL16", "LD1")
+            ties(*p1)
+        mm(T.pD[:, 0:1024 - sa], T.IDP[:], T.XS[:, 0:1024 - sa], False, True, "IDP XS0", "pD")
+        if k == 0:
+            mm(T.pH[:, 0:128], T.IDP[:], T.NEG[:], True, False, "IDP NEG", "pH")
+            ties(*p2)
+        diff(*p1)
+        asks(*p0)
+        clip(*p1)
+        if k == 0:
+            votes(*p1)
+            turn()
+            turned("v", 0)
+        act(T.SG[:, sa:1024], T.pD[:, 0:1024 - sa], F.Sign, "pD", "SGpC")
+        if k == 0:
+            turned("a", 1)
+        act(T.K[:], GN_, F.Abs, "NEW", "K", bias=-SIT)
+
+        def where(b):
+            c, gr = b // 8, b % 8
+            bank = [p[3] for p in PIECES if p[1] <= c < p[2]][0]
+            return c, gr, 128 * c + 16 * gr, bank
+
+        for b in range(64 - NA, 64):
+            c, gr, o, bank = where(b)
+            w = 128 * (b - 64 + NA)
+            act(T.BT[:, w:w + 128], T.IO[:], F.Abs, "IO AT%d" % (c // 4), "BT%d" % b, bias=T.AT[:, o + 12:o + 13], scale=-1.0)
         m = 16 * GP
-        mm(T.pS[:, 0:1024 - m], T.IDP[:], T.GE[:, m:1024], True, False, "IDP GE1", "pS")
-        mm(T.pX[:, 0:64], T.I32P[:], T.TR[:], True, False, "I32P TR", "pX")
-        tr(T.pF[:, 128:256], T.FL1[:], "FL1", "pF")
-        tr(T.pF[:, 0:128], T.FL0[:], "FL0", "pF")
-        cp(T.FT[:, 0:256], T.pF[:, 0:256], "pF", "FT")
-        tt(T.GF[:, 0:m], T.FT[:].indirect(T.OF16[:, 0:GP]), T.GE[:, 0:m], A.mult, "FT OF16 GE0 GE1", "GF0")
-        gat("a", T.XS[:, 512:1536 - m], T.FT[:], T.OF16[:, GP:64], "FT OF16", "XS1")
-        mm(T.pS[:, 0:1024 - m], T.IDF[:], T.XS[:, 512:1536 - m], False, True, "IDF XS1", "pS")
-        act(T.GF[:, m:1024], T.pS[:, 0:1024 - m], F.Relu, "pS", "GF1", bias=-4096.0)
-        ext(T.pX, "pX", "SELF", T.GF, "GF0 GF1", False)
-        if not final:
-            t3("WK", "N3", "SIT", A.is_gt)
-            ts(T.EL[:], T.D[:], 0.0, A.is_equal, "D", "EL", float(ROOT), A.mult)
-            t3("T1", "WK", "SH", A.mult)
-            t3("LH", "SH", "D", A.subtract)
-            t3("H1", "H", "T1", A.add)
-            t3("L1", "L", "EL", A.max)
-        if not last:
-            ts(T.BI[:], T.LN[:], (ST * n + k + 1) % LB, A.arith_shift_right, "LN", "BI", 1, A.bitwise_and)
-            ts(T.AK[:], T.N3[:], 0.0, A.is_equal, "N3", "AK", float(TOP), A.mult)
-            t3("AB", "AK", "BI", A.mult)
-        tt(T.SC[:], T.pX[:, 0:64], T.H[:], A.max, "pX H", "SC")
-        if not final:
-            ts(T.SO[:], T.pX[:, 0:64], 0.0, A.is_lt, "pX", "SO")
-        cp(T.SC16[:], T.SC[:], "SC", "SC16")
-        if not last:
-            ts(T.NS[:], T.pX[:, 0:64], 0.0, A.is_ge, "pX", "NS")
-        if not final:
-            t3("T2", "SO", "LH", A.mult)
-            t3("T3", "SO", "D", A.mult)
-            if not last:
-                t3("SIT", "AB", "NS", A.mult)
-            t3("H", "H1", "T2", A.add)
-            t3("L", "L1", "T3", A.add)
-            if not last:
-                t3("G", "H", "SIT", A.max)
-                cp(T.L16[:], T.L[:], "L", "L16")
-                cp(T.G16[:], T.G[:], "G", "G16")
-                digits("a")
-                own_x(X, xk)
-                turned()
+
+        def early():
+            cp(T.GX[:], GN_, "NEW", "GX")
+            tt(T.D[:], T.pS[:, 0:64], LN_, A.subtract, "pS NEW", "D")
+            if not final:
+                tt(T.S2[:], T.pS[:, 0:64], T.K[:], A.min, "pS K", "S2")
+            ts(T.H[:], T.GX[:], 4095, A.bitwise_and, "GX", "H")
+            ts(T.OI[:], T.GX[:], 255, A.bitwise_and, "GX", "OI")
+            ts(T.DS[:], T.D[:], 1.0 / 4096, A.mult, "D", "DS")
+            tt(T.HT[:], T.H[:], T.BASE[:, 0:64], A.subtract, "H TR", "HT")
+            cp(T.OF16[:], T.OI[:], "OI", "OF16")
+            if final:
+                return
+            u = (ST * n + k + 1) % LB
+            if last:
+                cp(T.GA[:], T.H[:], "H", "GA")
+            elif u < 4:
+                ts(T.GA[:], T.H[:], T.BC[:, u:u + 1], A.add, "H BC", "GA")
             else:
-                ts(T.UP[:], T.L[:], float(ROOT), A.is_equal, "L", "UP")
-                tt(T.T1[:], T.EF[:, 0:64], T.H[:], A.subtract, "EF H", "T1")
-                tt(T.T2[:], T.EF[:, 64:128], T.L[:], A.subtract, "EF L", "T2")
-                t3("SH", "T1", "UP", A.mult)
-                t3("D", "T2", "UP", A.mult)
-                t3("H1", "SH", "H", A.add)
-                t3("T3", "D", "L", A.add)
-                sp = "SP%d" % n
-                cp(T[sp][:, 0:64], T.H1[:], "H1", "+" + sp)
-                cp(T[sp][:, 64:128], T.T3[:], "T3", "+" + sp)
-                send(T["LP%d" % n][:], T[sp][:], "r%d" % n, "s%d" % n, sp)
+                i = (5, 6, 7, 9).index(u)
+                tt(T.GA[:], T.H[:], T.BW[:, 64 * i:64 * i + 64], A.add, "H BW", "GA")
+            ts(T.EL[:], T.D[:], 0.0, A.is_equal, "D", "EL", float(ROOT), A.mult)
+
+        def later():
+            if not final:
+                tt(T.E1[:], LN_, T.GA[:], A.subtract, "NEW GA", "E1")
+                t3("E2", "GA", "S2", A.subtract)
+
+        for b in range(64):
+            c, gr, o, bank = where(b)
+            if b == PB and k > 0:
+                votes(*p1)
+            if b == VB:
+                asks(*p1)
+            if b == PC:
+                votes(*p2)
+            if b == VC:
+                asks(*p2)
+                if NA:
+                    act(T.AKN[:, 8 * p2[1]:64], T.AK2[:, 8 * p2[1]:64], F.Copy, "AKpC", "AKN", scale=-1.0)
+                    for b2 in range(64 - NA, 64):
+                        w = 128 * (b2 - 64 + NA)
+                        act(T.BB[:, 128 * b2:128 * b2 + 128], T.BT[:, w:w + 128], F.Relu, "BT%d AKpC AKN" % b2, "BB%d" % b2,
+                            bias=T.AK2[:, b2:b2 + 1], scale=T.AKN[:, b2:b2 + 1])
+            if b < 64 - NA:
+                bb = T.BB[:, 128 * b:128 * b + 128]
+                ts(bb, T.IO[:], T.AT[:, o + 12:o + 13], A.is_equal, "IO AK%s AT%d" % (bank, c // 4), "BB%d" % b,
+                   T.AK2[:, b:b + 1], A.mult)
+            if b == 63 - NA:
+                if n == 0 and k == 0:
+                    last_constants()
+                early()
+            mm(T.pH[:, 16 * gr:16 * gr + 12], T.BB[:, 128 * b:128 * b + 128], T.AT[:, o:o + 12], False, b == 63,
+               "BB%d AT%d" % (b, c // 4), "pH")
+        act(T.GN[:, 0:1024 - m], T.GE[:, m:1024], F.Sign, "GE1", "GN")
+        if n == 0 and k == 0:
+            act(T.SELT[:], T.SELM[:], F.Identity, "SELM WU", "SELT", scale=T.WU[:])
+        ts(T.RR[:], T.pH[:, 0:128], MAGIC, A.add, "pH", "RR", MAGIC, A.subtract)
+        ts(T.FL1[:], T.pH[:, 0:128], MAGIC, A.add, "pH", "FL1", MAGIC + 2048, A.is_equal)
+        tt(T.FL0[:], T.pH[:, 0:128], T.RR[:], A.is_equal, "pH RR", "FL0")
+        mm(T.pD[:, 0:1024 - m], T.IDP[:], T.GN[:, 0:1024 - m], True, False, "IDP GN", "pD")
+        tr(T.pT[:, 128:256], T.FL1[:], "FL1", "pT")
+        tr(T.pT[:, 0:128], T.FL0[:], "FL0", "pT")
+        ext("pA", "SELM", T.SG, "SGpA SGpB SGpC")
+        later()
+        cp(T.FT[:], T.pT[:, 0:256], "pT", "FT")
+        tt(T.GF[:, 0:m], T.FT[:].indirect(T.OF16[:, 0:GP]), T.GE[:, 0:m], A.min, "FT OF16 GE0 GE1", "GF0")
+        gat("a", T.XS[:, 512:1536 - m], T.FT[:], T.OF16[:, GP:64], "FT OF16", "XS1")
+        mm(T.pD[:, 0:1024 - m], T.IDP[:], T.XS[:, 512:1536 - m], False, True, "IDP XS1", "pD")
+        act(T.GF[:, m:1024], T.pD[:, 0:1024 - m], F.Relu, "pD", "GF1", bias=-1.0)
+        ext("pS", "SELM", T.GF, "GF0 GF1")
+        AK = T.pW[:, 192:256]
+        tt(AK, T.pA[:, 0:64], T.DS[:], A.is_lt, "pA DS", "pW")
+        if not final:
+            tt(T.BASE[:, 128:192], LN_, T.EL[:], A.max, "NEW EL", "BL")
+        tt(T.DV[:, 0:64], AK, T.HT[:], A.mult, "pW HT", "+DV")
+        w = 64 if final else 192
+        if not final:
+            tt(T.T1[:], AK, T.E2[:], A.mult, "pW E2", "T1")
+            tt(T.DV[:, 64:128], AK, T.E1[:], A.mult, "pW E1", "+DV")
+            tt(T.DV[:, 128:192], AK, T.D[:], A.mult, "pW D", "+DV")
+            tt(T.BASE[:, 64:128], T.T1[:], T.S2[:], A.add, "T1 S2", "BG")
+        for o in range(0, w, 64):
+            tt(T.pW[:, o:o + 64], T.pS[:, 0:64], T.DV[:, o:o + 64], A.mult, "pS DV", "+pW")
+        tt(T.NEW[:, 0:w], T.pW[:, 0:w], T.BASE[:, 0:w], A.add, "pW TR BG BL", "NEW")
+        if not last:
+            ts(T.GL16[:], T.NEW[:, 64:192], float(TOP), A.min, "NEW", "GL16")
+        cp(T.SC16[:], T.NEW[:, 0:64], "NEW", "SC16")
+        if not last:
+            digits("a")
+            turn()
+            mm(T.pH[:, 0:128], T.IDP[:], T.NEG[:], True, False, "IDP NEG", "pH")
+            own_x("a", X, xk, 0, 64, "XL0 XL1")
+            mm(T.pD[:, 0:1024 - sa], T.IDN[:], T.XL[:, sa:1024], True, False, "IDN XL1", "pD")
+            turned("a", 1)
         em("v", lambda: g.vector.tensor_copy(T.SW[:].indirect(T.SC16[:]), T.LD[:]), "SC16 LD0 LD1", SW)
-        if last:
-            act(T.XP[:], X[:, 0:1536], F.Identity, xk, "XP", bias=1.0)
-            act(T.XM[:], X[:, 0:1536], F.Identity, xk, "XM", bias=-1.0)
+
+    def pass_on(n):
+        ts(T.UP[:], LN_, float(ROOT), A.is_equal, "NEW", "UP")
+        tt(T.PF2[:], T.EF[:], T.NEW[:, 64:192], A.subtract, "EF NEW", "PF2")
+        tt(T.pW[:, 0:64], T.PF2[:, 0:64], T.UP[:], A.mult, "PF2 UP", "pW")
+        tt(T.pW[:, 64:128], T.PF2[:, 64:128], T.UP[:], A.mult, "PF2 UP", "+pW")
+        tt(T.RR[:], T.pW[:, 0:128], T.NEW[:, 64:192], A.add, "pW NEW", "RR")
+        sp = "SP%d" % n
+        cp(T[sp][:], T.RR[:], "RR", sp)
+        send(T["LP%d" % n][:], T[sp][:], "r%d" % n, "s%d" % n, sp)
 
     def round_end(n, X, xk, Y, yk):
         final = n == RO - 1
+        lb, db = ("pS", "pA", "pS"), ("pB", "pC", "pD")
+        cut = [1024 * (c + 1) - 16 * RE[c] for c in range(3)]
+        for c in range(3):
+            a, b = 1024 * c, cut[c]
+            act(T.XP[:, a:b], X[:, a:b], F.Identity, xk, "+XP", bias=1.0)
+            act(T.XM[:, a:b], X[:, a:b], F.Identity, xk, "+XM", bias=-1.0)
+            mm(T[db[c]][:, 0:16 * RE[c]], T.IDN[:], X[:, b:1024 * (c + 1)], True, False, "IDN " + xk, db[c])
+        mm(T.pH[:, 0:16 * RE[0]], T.IDP[:], X[:, cut[0]:1024], True, False, "IDP " + xk, "pH")
         if final:
-            dma("s", T.D0[:], T.SW[0:128:16, 0:3072], SW, "D0")
-            dma("s", T.D1[:], T.SW[1:128:16, 0:3072], SW, "D1")
-        bank = ("pH", "pL", "pX")
-        for c in (1, 2, 0):
-            mm(T[bank[c]][:], T.IDN[:], X[:, 1536 + 512 * c:2048 + 512 * c], True, False, "IDN " + xk, bank[c])
+            dma("s", T.D0[:], T.SW[2:128:16, 0:3072], SW, "D0")
+            dma("s", T.D1[:], T.SW[3:128:16, 0:3072], SW, "D1")
 
-        def lists(ps, o, key):
-            ts(T.R1[:], T[ps][:, 0:64], float(ROOT), A.is_equal, ps, "R1")
-            tt(T.R2[:], T.R1[:], T.VM[:, o:o + 64], A.mult, "R1 VM", "R2")
-            tt(T.R3[:], T[ps][:, 0:64], T.R2[:], A.add, ps + " R2", "R3")
-            cp(T.SL16[:, o:o + 64], T.R3[:], "R3", key)
-        ext(T.pS, "pS", "SELS", T.SW, SW, True, 64, 128)
-        lists("pS", 128, "SLc")
-        ext(T.pV, "pV", "SELS", T.SW, SW, True, 64, 0)
-        lists("pV", 0, "SLa")
-        ext(T.pS, "pS", "SELS", T.SW, SW, True, 64, 64)
-        tt(T.DD[:, 0:1024], X[:].indirect(T.SL16[:, 0:64]), T.XP[:, 0:1024], A.min, xk + " SLa XP", "DDa")
-        lists("pS", 64, "SLb")
-        mm(T.pV[:], T.IDP[:], T.XM[:, 0:512], True, True, "IDP XM", "pV")
-        mm(T.pS[:], T.IDP[:], T.XM[:, 512:1024], True, True, "IDP XM", "pS")
+        def lists(c):
+            ext(lb[c], "SELT", T.SW, SW, 64 * c)
+
+        def listed(c):
+            cp(T.SL16[:, 64 * c:64 * c + 64], T[lb[c]][:, 0:64], lb[c], "SL%d" % c)
+
+        def lo(c):
+            a, b = 1024 * c, cut[c]
+            tt(T.DD[:, a:b], X[:].indirect(T.SL16[:, a // 16:b // 16]), T.XP[:, a:b], A.min, xk + " XP SL%d" % c,
+               "DDpA DDpB" if c == 0 else "DD%d" % c)
+
+        def hi(c):
+            a, b = 1024 * c, cut[c]
+            tt(Y[:, a:b], T.DD[:, a:b], T.XM[:, a:b], A.max, "XM " + ("DDpA DDpB" if c == 0 else "DD%d" % c), yk + "abc"[c])
+            if final:
+                dma("s", T.yx[:, a:b], Y[:, a:b], yk + "abc"[c], "ox" + "abc"[c])
 
         def ga(c):
-            gat("a", T.XS[:, 512 * c:512 * c + 512], X[:], T.SL16[:, 96 + 32 * c:128 + 32 * c],
-                xk + (" SLc" if c else " SLb"), "XS%d" % c)
-            mm(T[bank[c]][:], T.IDP[:], T.XS[:, 512 * c:512 * c + 512], False, True, "IDP XS%d" % c, bank[c])
+            w = 16 * RE[c]
+            gat("a", T.XS[:, 512 * c:512 * c + w], X[:], T.SL16[:, cut[c] // 16:64 * (c + 1)], xk + " SL%d" % c, "XS%d" % c)
+
+        def gd(c):
+            w = 16 * RE[c]
+            mm(T[db[c]][:, 0:w], T.IDP[:], T.XS[:, 512 * c:512 * c + w], False, True, "IDP XS%d" % c, db[c])
 
         def sg(c):
-            act(T.SN[:, 512 * c:512 * c + 512], T[bank[c]][:], F.Sign, bank[c], "SN%d" % c)
-            o = 1536 + 512 * c
-            mm(T[bank[c]][:], T.IDP[:], X[:, o:o + 512], True, False, "IDP " + xk, bank[c])
-            mm(T[bank[c]][:], T.IDP[:], T.SN[:, 512 * c:512 * c + 512], False, True, "IDP SN%d" % c, bank[c])
+            w = 16 * RE[c]
+            act(T.SN[:, 512 * c:512 * c + w], T[db[c]][:, 0:w], F.Sign, db[c], "SN%d" % c)
+
+        def ad(c):
+            w, bank = 16 * RE[c], ("pH", "pB", "pC")[c]
+            if c:
+                mm(T[bank][:, 0:w], T.IDP[:], X[:, cut[c]:1024 * (c + 1)], True, False, "IDP " + xk, bank)
+            mm(T[bank][:, 0:w], T.IDP[:], T.SN[:, 512 * c:512 * c + w], False, True, "IDP SN%d" % c, bank)
 
         def ev(c):
-            o = 1536 + 512 * c
-            act(Y[:, o:o + 512], T[bank[c]][:], F.Copy, bank[c], "+" + yk + ("b" if c else "d"))
-        ga(1), ga(2), sg(1), ga(0), sg(2), ev(1), sg(0), ev(2), ev(0)
-        tt(Y[:, 0:512], T.DD[:, 0:512], T.pV[:], A.max, "DDa pV", "+" + yk + "a")
-        tt(Y[:, 512:1024], T.DD[:, 512:1024], T.pS[:], A.max, "DDa pS", "+" + yk + "a")
-        tt(T.DD[:, 1024:1536], X[:].indirect(T.SL16[:, 64:96]), T.XP[:, 1024:1536], A.min, xk + " SLb XP", "DDb")
-        tt(Y[:, 1024:1536], T.DD[:, 1024:1536], T.XM[:, 1024:1536], A.max, "DDb XM", yk + "c")
+            w, bank = 16 * RE[c], ("pH", "pB", "pC")[c]
+            a, b = cut[c], 1024 * (c + 1)
+            act(Y[:, a:b], T[bank][:, 0:w], F.Copy, bank, yk + "dfg"[c])
+            if final:
+                dma("a", T.yx[:, a:b], Y[:, a:b], yk + "dfg"[c], "ox" + "dfg"[c])
+        lists(0)
+        if not final:
+            pass_on(n)
+        listed(0), lists(1), ga(0), lo(0), listed(1), lists(2), gd(0), ga(1), sg(0), hi(0), listed(2), gd(1), ad(0)
+        ga(2), sg(1), lo(1), gd(2), ad(1), ev(0), sg(2), ad(2), hi(1), lo(2), ev(1), ev(2)
         if final:
-            dma("s", T.yx[:, 0:1024], Y[:, 0:1024], yk + "a", "oxa")
             ts(T.Y2[:], T.D0[:], 64.0, A.mult, "D0", "Y2")
             tt(T.Y3[:], T.Y2[:], T.D1[:], A.add, "Y2 D1", "Y3")
-            ts(T.Y2[:], T.Y3[:], float(ROOT), A.is_equal, "Y3", "Y2")
-            tt(T.Y2[:], T.Y2[:], T.VK[:], A.mult, "Y2 VK", "Y2")
-            tt(T.Y3[:], T.Y3[:], T.Y2[:], A.subtract, "Y3 Y2", "Y3")
-            dma("s", T.yx[:, 1024:1536], Y[:, 1024:1536], yk + "c", "oxc")
             dma("s", T.ys[:], T.Y3[:], "Y3", "oy")
-            dma("s", T.yx[:, 2048:3072], Y[:, 2048:3072], yk + "b", "oxb")
-            dma("s", T.yx[:, 1536:2048], Y[:, 1536:2048], yk + "d", "oxd")
+        hi(2)
 
     X, Y, xk, yk = T.XA, T.XB, "X0", "X1"
     for n in range(RO):
-        xr = " ".join(xk + c for c in "abcde")
+        xr = " ".join(xk + c for c in "abcdefg")
         round_start(n, X, xr)
         for k in range(ST):
             step(n, k, X, xr)

@@ -1,30 +1,33 @@
 from concourse.mybir import AluOpType as A, ActivationFunctionType as F
 
 RO, ST, LB = 3, 4, 10
-ROOT, TOP, SIT = 3072, 3073, 8192.0
+TOP, ROOT, SELF, SIT = 3072, 3073, 3136, 8192.0
 MAGIC = 3.0 * 2 ** 33
-PIECES = (("v", 0, 2, "pA"), ("v", 2, 4, "pB"), ("a", 4, 8, "pC"))
-GP = 46
-NA = 10
+W = 120
+PIECES = ((0, 2, "pA"), (2, 4, "pB"), (4, 8, "pC"))
+GP = 50
+ND = 4
 RS = 36
-RE = (24, 28, 28)
-PB, PC, VB, VC = 4, 12, 14, 28
+AT0 = (0, 5, 0, 2, 2, 12, 20, 30, 40, 56)
+ATK = (4, 6, 2, 2, 2, 12, 12, 24, 34, 43)
+SEG = ((0, 512, "a", "pA"), (512, 1024, "v", "pW"), (1024, 1536, "a", "pB"), (1536, 2048, "a", "pC"),
+       (2048, 2560, "v", "pH"), (2560, 3072, "a", "pD"))
 DT = {"b": "bfloat16", "f": "float32", "i": "int32", "u": "uint16"}
-SCRATCH = {"BT": ("sbuf", [128, 128 * max(NA, 1)], "bfloat16")}
-for _t in ("b3088 XA XB CT DG;b4112 SW;b1024 GE GS XL LD SG AT GF;b1536 XS SN;b3072 DD XP XM;b8192 BB;b512 GN;"
-           "b64 AK2 S2N;f64 AKN;b128 FL0 FL1 IO IDP IDN NEG;b256 WR FT IH IL B2;i128 EI;f128 RR EF PF2;"
-           "b2048 SELS SELM SELT;b8 M2 S2P;i1 PI GI QI;f1 PF GFC QF GC WT WU EH EO N12 N13;f16 EQ EC GQ KB;i4 BI;f4 BC;"
-           "i192 UI VI W1 W2 SI;b192 D0 D1 S0 S1;f192 Y2 Y3 NEW BASE DV;u192 SL16;i64 LV H OI GX;"
+SCRATCH = {}
+for _t in ("b6208 XA XB;b3088 DG;b4112 SW;b1024 GS XL LD SG AT GF;b3072 DD XP XS;b7680 BB BT;b512 GN;"
+           "b64 AK2 S2G;b128 IO IDP IDN ID6 NEG FL0 FL1;b256 WR IH IL B2 FT;i128 EI;f128 RR EF PF2 P3 P4;"
+           "b2048 SELS SELM SELF;b8 M2 S2L;i1 PI GI QI;f1 PF GFC QF GC WT N1 N2;f16 EQ EC GQ KB E4 LO;"
+           "i4 BI;f4 BC;i192 UI W1 W2 SI;b192 D0 D1 D2;f192 Y3 NEW BASE DV;u192 SL16;i64 LV Q;"
            "u128 ED EDN LP0 LP1 SP0 SP1 GL16;f256 BW;"
-           "f64 D DS K HT GA E1 E2 S2 EL UP T1;u64 S16 OF16 SC16").split(";"):
+           "f64 D K HT E1 E2 S2 UP OF;u64 S16 OF16 SC16").split(";"):
     for _n in _t.split()[1:]:
         SCRATCH[_n] = ("sbuf", [128, int(_t.split()[0][1:])], DT[_t[0]])
 PS = ("pS", "pA", "pB", "pC", "pD", "pH", "pW", "pT")
 for _n in PS[:-1]:
     SCRATCH[_n] = ("psum", [128, 512], "float32")
 SCRATCH["pT"] = ("psum", [128, 1024], "bfloat16")
-SEMAPHORES = ["cv", "ca", "cp", "cg", "se", "s0", "s1", "re", "r0", "r1"] + ["d%d" % i for i in range(24)]
-SW = "SW SW0 SW1 SW2 SW3"
+SEMAPHORES = ["cv", "ca", "cp", "cg", "se", "s0", "s1", "re", "r0", "r1"] + ["d%d" % i for i in range(48)]
+SW = "SW SW0 SW1"
 
 
 def rank_program(g, core, T, topo):
@@ -90,7 +93,7 @@ def rank_program(g, core, T, topo):
         nd[0] += 1
         total[s] = 16
         eng[e].dma_start(out, in_).then_inc(T.sem[s], 16)
-        after((s, 16, "D", dict(seen[e])), rd, wr)
+        after((s, 16, e if e == "s" else "D", dict(seen[e])), rd, wr)
 
     def send(out, in_, rs, ls, rd):
         before("g", rd.split(), [])
@@ -115,9 +118,6 @@ def rank_program(g, core, T, topo):
         else:
             em("v", lambda: g.vector.tensor_scalar(out, a, s1, s2, op0, op1), rd, wr)
 
-    def t3(o, a, b, op):
-        tt(T[o][:], T[a][:], T[b][:], op, a + " " + b, o)
-
     def ms(ap, c, wr):
         em("v", lambda: g.vector.memset(ap, c), "", wr)
 
@@ -126,9 +126,6 @@ def rank_program(g, core, T, topo):
 
     def mm(out, l, r, start, stop, rd, wr):
         em("p", lambda: g.tensor.matmul(out, l, r, start, stop), rd, wr)
-
-    def tr(out, in_, rd, wr):
-        em("p", lambda: g.tensor.transpose(out, in_, T.IDP[:]), rd + " IDP", wr)
 
     def gat(e, out, win, off, rd, wr):
         if e == "v":
@@ -146,6 +143,7 @@ def rank_program(g, core, T, topo):
         em("g", lambda: g.iota(T[nm][:, a:b or SCRATCH[nm][1][1]], pat, 0, cm, **kw), "", "+" + nm)
 
     GN_, LN_ = T.NEW[:, 64:128], T.NEW[:, 128:192]
+    AK, H, GA, TQ, S = [T.pW[:, 192 + 64 * i:256 + 64 * i] for i in range(5)]
 
     dma("s", T.SI[:], T.succ[:], "", "SI")
     dma("a", T.EI[:, 0:64], T.ea[:], "", "EIa")
@@ -157,87 +155,68 @@ def rank_program(g, core, T, topo):
     iota("UI", [[1, 192]], 192)
     iota("IH", [[1, 4], [0, 64]], 0)
     iota("IL", [[0, 4], [1, 64]], 0)
-    ms(T.SW[:, 0:3088], 0.0, SW)
-    ts(T.GI[:], T.PI[:], 112, A.bitwise_and, "PI", "GI")
+    for b in "AB":
+        ms(T["X" + b][:, 3072:SELF], -1.0, "X%de" % (b == "B"))
+    ms(T.SW[:, 3072:3088], 0.0, "SW")
+    ms(T.S2G[:], 0.0, "S2G")
+    ms(T.NEG[:], -1.0, "NEG")
     ts(T.QI[:], T.PI[:], 15, A.bitwise_and, "PI", "QI")
+    ts(T.GI[:], T.PI[:], 112, A.bitwise_and, "PI", "GI")
     cp(T.PF[:], T.PI[:], "PI", "PF")
-    cp(T.GFC[:], T.GI[:], "GI", "GFC")
+    for b in "AB":
+        ms(T["X" + b][:, TOP:TOP + 1], 256.0, "X%de" % (b == "B"))
     cp(T.QF[:], T.QI[:], "QI", "QF")
-    for b in "AB":
-        ms(T["X" + b][:, 3072:3088], -1.0, "X%de" % (b == "B"))
-    ts(T.GQ[:], T.IO[:, 0:16], T.GFC[:], A.add, "IO GFC", "GQ")
+    cp(T.GFC[:], T.GI[:], "GI", "GFC")
+    for nm, sc in (("IDN", -1.0), ("IDP", 1.0), ("ID6", 64.0)):
+        ts(T[nm][:], T.IO[:], T.PF[:], A.is_equal, "IO PF", nm, sc, A.mult)
     ts(T.EQ[:], T.IO[:, 0:16], T.QF[:], A.is_equal, "IO QF", "EQ")
+    ts(T.GQ[:], T.IO[:, 0:16], T.GFC[:], A.add, "IO GFC", "GQ")
     ts(T.GC[:], T.GFC[:], -192.0, A.mult, "GFC", "GC")
-    for b in "AB":
-        ms(T["X" + b][:, TOP:3088], 256.0, "X%de" % (b == "B"))
-    tt(T.EH[:], T.EQ[:, 0:1], T.EQ[:, 2:3], A.add, "EQ", "EH")
-    tt(T.EO[:], T.EQ[:, 1:2], T.EQ[:, 3:4], A.add, "EQ", "EO")
-    ts(T.VI[:], T.UI[:], T.GC[:], A.add, "UI GC", "VI")
-    ts(T.WT[:], T.EQ[:, 0:1], 64.0, A.mult, "EQ", "WT", T.EQ[:, 1:2], A.add)
-    ts(T.WU[:], T.EQ[:, 2:3], 64.0, A.mult, "EQ", "WU", T.EQ[:, 3:4], A.add)
-    ts(T.WR[:], T.IH[:], T.EH[:], A.mult, "IH EH", "WR")
-    ts(T.FT[:], T.IL[:], T.EO[:], A.mult, "IL EO", "FT")
-    ts(T.KB[:], T.IO[:, 0:16], T.EH[:], A.mult, "IO EH", "KB", 4.0, A.mult)
-    tt(T.B2[:], T.WR[:], T.FT[:], A.add, "WR FT", "B2")
+    for u in range(4):
+        ts(T.BI[:, u:u + 1], T.QI[:], u, A.arith_shift_right, "QI", "+BI", 1, A.bitwise_and)
+    ts(T.N1[:], T.EQ[:, 15:16], -1.0, A.mult, "EQ", "N1", 1.0, A.add)
+    ts(T.N2[:], T.EQ[:, 15:16], -2048.0, A.mult, "EQ", "N2", 2048.0, A.add)
+    ts(T.EC[:], T.EQ[:], T.EQ[:, 15:16], A.max, "EQ", "EC")
+    ts(T.B2[:], T.IH[:], T.EQ[:, 0:1], A.mult, "IH EQ", "B2")
+    ts(T.FT[:], T.IL[:], T.EQ[:, 1:2], A.mult, "IL EQ", "FT")
+    ts(T.WR[:, 0:W], T.IO[:, 0:W], T.EQ[:, 15:16], A.mult, "IO EQ N1", "WR", T.N1[:], A.add)
+    ts(T.WR[:, W:2 * W], T.IO[:, 0:W], T.EQ[:, 15:16], A.mult, "IO EQ N2", "+WR", T.N2[:], A.add)
+    ts(T.KB[:], T.IO[:, 0:16], T.EQ[:, 0:1], A.mult, "IO EQ", "KB", 4.0, A.mult)
+    ts(T.pW[:, 0:192], T.UI[:], T.GC[:], A.add, "UI GC pW", "wT")
+    tt(T.B2[:], T.B2[:], T.FT[:], A.add, "B2 FT", "B2")
     for k in range(13):
         w = 256 if k < 12 else 16
         act(T.DG[:, 256 * k:256 * k + w], T.B2[:, 0:w], F.Identity, "B2 KB", "+DG", bias=T.KB[:, k:k + 1])
-    for q in range(16):
-        ts(T.SELM[:, q * 128:(q + 1) * 128], T.IO[:], T.GQ[:, q:q + 1], A.is_equal, "IO GQ", "+SELM")
-    act(T.SELS[:], T.SELM[:], F.Identity, "SELM WT", "SELS", scale=T.WT[:])
-    tt(T.Y2[:], T.SI[:], T.VI[:], A.not_equal, "SI VI", "Y2")
-    ts(T.W1[:], T.SI[:], 6, A.arith_shift_right, "SI", "W1")
+    for k in range(13):
+        a, w = 2 * W * k, min(2 * W, 3072 - 2 * W * k)
+        ts(T.SW[:, a:a + w], T.WR[:, 0:w], T.EC[:, k + 2:k + 3], A.mult, "WR EC", "+SW0 +SW1")
+    tt(T.Y3[:], T.pW[:, 0:192], T.SI[:], A.is_equal, "SI wT pW", "Y3")
     ts(T.W2[:], T.SI[:], 63, A.bitwise_and, "SI", "W2")
-    ts(T.Y3[:], T.Y2[:], -48.0, A.mult, "Y2", "Y3", 48.0, A.add)
-    tt(T.S1[:], T.W2[:], T.Y2[:], A.mult, "W2 Y2", "S1")
-    dma("s", T.SW[1:128:16, 0:3072], T.S1[:], "S1", "SW1")
-    tt(T.S0[:], T.W1[:], T.Y3[:], A.max, "W1 Y3", "S0")
-    dma("s", T.SW[0:128:16, 0:3072], T.S0[:], "S0", "SW0")
+    ts(T.W1[:], T.SI[:], 6, A.arith_shift_right, "SI", "W1")
+    ts(T.pW[:, 192:384], T.Y3[:], SELF / 64, A.mult, "Y3 pW", "wAK wH wGA")
+    cp(T.D1[:], T.W2[:], "W2", "D1")
+    dma("s", T.SW[1:128:16, 0:3072], T.D1[:], "D1", "SW1")
+    tt(T.D0[:], T.pW[:, 192:384], T.W1[:], A.add, "W1 wAK pW", "D0")
+    dma("s", T.SW[0:128:16, 0:3072], T.D0[:], "D0", "SW0")
     cp(T.ED[:], T.EI[:], "EIa EIb", "ED")
     send(T.EDN[:], T.ED[:], "re", "se", "ED")
     iota("LV", [[16, 64]], 0)
     for i, b in enumerate((1, 2, 3, 5)):
         iota("BW", [[0, 32 >> b], [int(SIT), 2], [0, 1 << b]], 0, 64 * i, 64 * i + 64)
-    cp(T.D0[:], T.W1[:], "W1", "D0")
-    cp(T.D1[:], T.W2[:], "W2", "D1")
-    dma("s", T.SW[2:128:16, 0:3072], T.D0[:], "D0", "SW2")
-    dma("s", T.SW[3:128:16, 0:3072], T.D1[:], "D1", "SW3")
-    for nm, sc in (("IDN", -1.0), ("IDP", 1.0)):
-        ts(T[nm][:], T.IO[:], T.PF[:], A.is_equal, "IO PF", nm, sc, A.mult)
-    ts(T.N12[:], T.EQ[:, 12:13], -1.0, A.mult, "EQ", "N12", 1.0, A.add)
-    ts(T.N13[:], T.EQ[:, 12:13], -2048.0, A.mult, "EQ", "N13", 2048.0, A.add)
-    ts(T.EC[:], T.EQ[:], T.EQ[:, 12:13], A.max, "EQ", "EC")
-    ts(T.WR[:, 0:128], T.IO[:], T.EQ[:, 12:13], A.mult, "IO EQ N12", "WR", T.N12[:], A.add)
-    ts(T.WR[:, 128:256], T.IO[:], T.EQ[:, 12:13], A.mult, "IO EQ N13", "+WR", T.N13[:], A.add)
-    ms(T.CT[:, 3072:3088], 0.0, "+CT")
-    for k in range(12):
-        if k < 6:
-            ts(T.CT[:, 256 * k:256 * k + 256], T.WR[:], T.EC[:, k:k + 1], A.mult, "WR EC", "+CT")
-        else:
-            act(T.CT[:, 256 * k:256 * k + 256], T.WR[:], F.Identity, "WR EC", "+CT", scale=T.EC[:, k:k + 1])
+    ts(T.E4[:], T.EQ[:], 1.0 / 4096, A.mult, "EQ", "E4")
+    for q in range(16):
+        ts(T.SELM[:, q * 128:(q + 1) * 128], T.IO[:], T.GQ[:, q:q + 1], A.is_equal, "IO GQ", "+SELM", 4096.0, A.mult)
+    ts(T.WT[:], T.E4[:, 0:1], 64.0, A.mult, "E4", "WT", T.E4[:, 1:2], A.add)
+    ts(T.BC[:], T.BI[:], SIT, A.mult, "BI", "BC")
 
     def more_constants():
-        cp(T.SW[:, ROOT:ROOT + 2], T.DG[:, ROOT:ROOT + 2], "DG", "SW")
-        ms(T.S2N[:], 0.0, "S2N")
-        ms(T.NEG[:], -1.0, "NEG")
         sel = T.SELM[:, 0:128:16]
-        ts(T.M2[:], sel, 4096.0, A.mult, "SELM", "M2")
-        ts(T.S2P[:], sel, T.WT[:], A.mult, "SELM WT", "S2P")
-        ts(T.S2N[:, 0:8], sel, T.WT[:], A.mult, "SELM WT", "S2N", -1.0, A.mult)
-
-    def last_constants():
-        for u in range(4):
-            ts(T.BI[:, u:u + 1], T.QI[:], u, A.arith_shift_right, "QI", "+BI", 1, A.bitwise_and)
+        cp(T.SW[:, TOP:TOP + 1], T.DG[:, TOP:TOP + 1], "DG", "SW")
+        ts(T.DG[:, ROOT:ROOT + 1], T.EQ[:, 0:1], 127.0, A.mult, "EQ", "DG")
+        ts(T.M2[:], sel, -2.0 ** -17, A.mult, "SELM", "M2")
+        ts(T.S2L[:], sel, T.WT[:], A.mult, "SELM WT", "S2L", -2.0 ** -17, A.mult)
+        ts(T.S2G[:, 0:8], sel, T.WT[:], A.mult, "SELM WT", "S2G", 2.0 ** -17, A.mult)
         ts(T.BASE[:, 0:64], T.LV[:], T.QF[:], A.add, "LV QF", "TR", 3088.0, A.add)
-        ts(T.BC[:], T.BI[:], SIT, A.mult, "BI", "BC")
-
-    def digits(e):
-        gat("a", T.GE[:, 0:512], T.CT[:], T.GL16[:, 0:32], "CT GL16", "GE0")
-        gat(e, T.GE[:, 512:1024], T.CT[:], T.GL16[:, 32:64], "CT GL16", "GE1")
-
-    def turn():
-        for c in range(8):
-            tr(T.pT[:, 128 * c:128 * c + 128], T.GE[:, 128 * c:128 * c + 128], "GE%d" % (c // 4), "pT")
 
     def turned(e, h):
         o, i = T.AT[:, 512 * h:512 * h + 512], T.pT[:, 512 * h:512 * h + 512]
@@ -246,8 +225,20 @@ def rank_program(g, core, T, topo):
         else:
             act(o, i, F.Copy, "pT", "AT%d" % h)
 
-    def own_x(e, X, xk, a, b, key):
-        gat(e, T.XL[:, 16 * a:16 * b], X[:], T.GL16[:, 64 + a:64 + b], xk + " GL16", key)
+    def own_x(e, X, xk, h):
+        gat(e, T.XL[:, 512 * h:512 * h + 512], X[:, 0:3088], T.GL16[:, 64 + 32 * h:96 + 32 * h], xk + " L16", "XL%d" % h)
+
+    def minus_own():
+        mm(T.pD[:], T.IDN[:], T.XL[:, 512:1024], True, False, "IDN XL1", "pD")
+
+    def own_digits(e, h):
+        gat(e, T.LD[:, 512 * h:512 * h + 512], T.DG[:], T.GL16[:, 64 + 32 * h:96 + 32 * h], "DG L16", "LD%d" % h)
+
+    def clear_counts():
+        mm(T.pH[:, 0:128], T.IDP[:], T.NEG[:], True, False, "IDP NEG", "pH")
+
+    def unsit():
+        act(T.K[:], GN_, F.Abs, "NG", "K", bias=-SIT)
 
     def round_start(n, X, xk):
         if n == 0:
@@ -255,285 +246,370 @@ def rank_program(g, core, T, topo):
         else:
             lst, lk = T["LP%d" % (n - 1)], "LP%d" % (n - 1)
             landed("r%d" % (n - 1), lk)
-        m, w = 16 * RS, 1024 - 16 * RS
-        gat("v", T.XL[:, 0:m], X[:], lst[:, 64:64 + RS], xk + " " + lk, "XL0")
-        gat("a", T.XL[:, m:1024], X[:], lst[:, 64 + RS:128], xk + " " + lk, "XL1")
+        m, w, X = 16 * RS, 1024 - 16 * RS, X[:, 0:3088]
+        gat("v", T.XL[:, 0:m], X, lst[:, 64:64 + RS], xk + " " + lk, "XL0")
+        gat("a", T.XL[:, m:1024], X, lst[:, 64 + RS:128], xk + " " + lk, "XL1")
         mm(T.pD[:, 0:w], T.IDN[:], T.XL[:, m:1024], True, False, "IDN XL1", "pD")
-        gat("a", T.XS[:, 0:w], X[:], lst[:, RS:64], xk + " " + lk, "XS0")
-        mm(T.pD[:, 0:w], T.IDP[:], T.XS[:, 0:w], False, True, "IDP XS0", "pD")
+        gat("a", T.XS[:, 0:w], X, lst[:, RS:64], xk + " " + lk, "XSa")
+        mm(T.pD[:, 0:w], T.IDP[:], T.XS[:, 0:w], False, True, "IDP XSa", "pD")
         act(T.SG[:, m:1024], T.pD[:, 0:w], F.Sign, "pD", "SGpC")
-        tt(T.DD[:, 0:m], X[:].indirect(lst[:, 0:RS]), T.XL[:, 0:m], A.subtract, xk + " XL0 " + lk, "DDpA DDpB")
+        cp(T.PF2[:], lst[:], lk, "PF2")
+        tt(T.DD[:, 0:m], X.indirect(lst[:, 0:RS]), T.XL[:, 0:m], A.subtract, xk + " XL0 " + lk, "DDpA DDpB")
+        tt(T.D[:], T.PF2[:, 0:64], T.PF2[:, 64:128], A.subtract, "PF2", "D")
         ts(T.SG[:, 0:m], T.DD[:, 0:m], 1.0, A.min, "DDpA DDpB", "SGpA SGpB", -1.0, A.max)
         ext("pA", "SELM", T.SG, "SGpA SGpB SGpC")
-        cp(T.PF2[:], lst[:], lk, "PF2")
-        tt(T.D[:], T.PF2[:, 0:64], T.PF2[:, 64:128], A.subtract, "PF2", "D")
-        ts(T.DS[:], T.D[:], 1.0 / 4096, A.mult, "D", "DS")
+        clear_counts()
         if n == 0:
+            act(T.SELS[:], T.SELM[:], F.Identity, "SELM WT", "SELS", scale=T.WT[:])
             more_constants()
         if n < 2:
             if n == 1:
                 landed("re", "EDN")
             e = T.ED if n == 0 else T.EDN
             cp(T.EF[:], e[:], "ED" if n == 0 else "EDN", "EF")
-        tt(T.UP[:], T.pA[:, 0:64], T.DS[:], A.is_gt, "pA DS", "UP")
-        tt(T.pW[:, 0:64], T.UP[:], T.D[:], A.mult, "UP D", "pW")
-        tt(GN_, T.pW[:, 0:64], T.PF2[:, 64:128], A.add, "pW PF2", "+NEW")
-        tt(LN_, T.PF2[:, 0:64], T.pW[:, 0:64], A.subtract, "pW PF2", "+NEW")
-        cp(T.GL16[:], T.NEW[:, 64:192], "NEW", "GL16")
+        tt(AK, T.pA[:, 0:64], T.D[:], A.is_gt, "pA D pW", "wAK")
+        tt(T.pW[:, 0:64], AK, T.D[:], A.mult, "wAK D pW", "wT")
+        tt(GN_, T.pW[:, 0:64], T.PF2[:, 64:128], A.add, "wT PF2 pW", "NG")
+        tt(LN_, T.PF2[:, 0:64], T.pW[:, 0:64], A.subtract, "wT PF2 pW", "NL")
+        cp(T.GL16[:, 0:64], GN_, "NG", "G16")
+        cp(T.GL16[:, 64:128], LN_, "NL", "L16")
 
     def step(n, k, X, xk):
+        t = ST * n + k
         last = k == ST - 1
         final = last and n == RO - 1
-        sa = 128 * PIECES[2][1]
-        gat("v", T.GS[:, 0:512], T.SW[:, 0:3088], T.GL16[:, 0:32], SW + " GL16", "GS0")
-        gat("a", T.GS[:, 512:1024], T.SW[:, 0:3088], T.GL16[:, 32:64], SW + " GL16", "GS1")
-        ext("pS", "SELS", T.GS, "GS0 GS1")
-        if k == 0:
-            own_x("v", X, xk, 0, sa // 16, "XL0")
-            gat("a", T.LD[:, 0:512], T.DG[:], T.GL16[:, 64:96], "DG GL16", "LD0")
-            own_x("a", X, xk, sa // 16, 64, "XL1")
-            mm(T.pD[:, 0:1024 - sa], T.IDN[:], T.XL[:, sa:1024], True, False, "IDN XL1", "pD")
-        else:
-            gat("v", T.LD[:, 0:512], T.DG[:], T.GL16[:, 64:96], "DG GL16", "LD0")
-            gat("a", T.LD[:, 512:1024], T.DG[:], T.GL16[:, 96:128], "DG GL16", "LD1")
-            turned("v", 0)
-        cp(T.S16[:], T.pS[:, 0:64], "pS", "S16")
+        p0, p1, p2 = PIECES
+        n1, n2, nb, cl, pb, vb, pc, vc, j1, j2 = AT0 if k == 0 else ATK
+        s1, s2 = list(range(32 - n1, 32)), list(range(64 - n2, 64))
+        XW = X[:, 0:3088]
 
-        def ties(bank, a, b):
+        def ties(a, b, bank):
             for c in range(a, b):
                 w = 8 * (b - a) if c == a else 8
-                mm(T[bank][:, 8 * (c - a):8 * (c - a) + w], T.GS[:, 128 * c:128 * c + 128], T.S2N[:, 0:w], c == a, False,
-                   "GS%d S2N" % (c // 4), bank)
-            for c in range(a, b):
-                mm(T[bank][:, 8 * (c - a):8 * (c - a) + 8], T.LD[:, 128 * c:128 * c + 128], T.S2P[:], False, False,
-                   "LD%d S2P" % (c // 4), bank)
+                mm(T[bank][:, 8 * (c - a):8 * (c - a) + w], T.GS[:, 128 * c:128 * c + 128], T.S2G[:, 0:w], c == a, False,
+                   "GS%d S2G" % (c // 4), bank)
 
-        def diff(bank, a, b):
-            tt(T.DD[:, 128 * a:128 * b], X[:].indirect(T.S16[:, 8 * a:8 * b]), T.XL[:, 128 * a:128 * b], A.subtract,
+        def ties2(a, b, bank):
+            for c in range(a, b):
+                mm(T[bank][:, 8 * (c - a):8 * (c - a) + 8], T.LD[:, 128 * c:128 * c + 128], T.S2L[:], False, False,
+                   "LD%d S2L" % (c // 4), bank)
+
+        def diff(a, b, bank):
+            tt(T.DD[:, 128 * a:128 * b], XW.indirect(T.S16[:, 8 * a:8 * b]), T.XL[:, 128 * a:128 * b], A.subtract,
                xk + " XL0 S16", "DD" + bank)
 
-        def clip(bank, a, b):
+        def clip(a, b, bank):
             ts(T.SG[:, 128 * a:128 * b], T.DD[:, 128 * a:128 * b], 1.0, A.min, "DD" + bank, "SG" + bank, -1.0, A.max)
 
-        def votes(bank, a, b):
+        def votes(a, b, bank):
             for c in range(a, b):
                 mm(T[bank][:, 8 * (c - a):8 * (c - a) + 8], T.SG[:, 128 * c:128 * c + 128], T.M2[:], False, c == b - 1,
                    "M2 SG" + bank, bank)
 
-        def asks(bank, a, b):
-            ts(T.AK2[:, 8 * a:8 * b], T[bank][:, 0:8 * (b - a)], 0.0, A.is_lt, bank, "AK" + bank)
+        def asks(a, b, bank):
+            ts(T.AK2[:, 8 * a:8 * b], T[bank][:, 0:8 * (b - a)], 0.0, A.is_gt, bank, "AK" + bank)
 
-        p0, p1, p2 = [(p[3], p[1], p[2]) for p in PIECES]
-        diff(*p0)
-        gat("a", T.XS[:, 0:1024 - sa], X[:], T.S16[:, sa // 16:64], xk + " S16", "XS0")
-        if k == 0:
-            digits("a")
-        ties(*p0)
-        if k:
-            ties(*p1), ties(*p2)
-        clip(*p0)
-        votes(*p0)
-        if k == 0:
-            gat("v", T.LD[:, 512:1024], T.DG[:], T.GL16[:, 96:128], "DG GL16", "LD1")
-            ties(*p1)
-        mm(T.pD[:, 0:1024 - sa], T.IDP[:], T.XS[:, 0:1024 - sa], False, True, "IDP XS0", "pD")
-        if k == 0:
-            mm(T.pH[:, 0:128], T.IDP[:], T.NEG[:], True, False, "IDP NEG", "pH")
-            ties(*p2)
-        diff(*p1)
-        asks(*p0)
-        clip(*p1)
-        if k == 0:
-            votes(*p1)
-            turn()
-            turned("v", 0)
-        act(T.SG[:, sa:1024], T.pD[:, 0:1024 - sa], F.Sign, "pD", "SGpC")
-        if k == 0:
-            turned("a", 1)
-        act(T.K[:], GN_, F.Abs, "NEW", "K", bias=-SIT)
+        def patch():
+            for r in (0, 1):
+                dma("s", T.GS[r:128:16, :], T.LD[r:128:16, :], "LD0 LD1", "+GS0 +GS1")
+
+        def o_h():
+            tt(H, GN_, T.K[:], A.min, "NG K pW", "wH")
+
+        def o_q():
+            ts(T.Q[:], GN_, 1.0 / (2 * W), A.mult, "NG", "Q", 0.25 / W - 0.5, A.add)
+
+        def o_tq():
+            ts(TQ, T.Q[:], -2.0 * W, A.mult, "Q pW", "wTQ")
+
+        def o_of():
+            tt(T.OF[:], TQ, GN_, A.add, "wTQ NG pW", "OF")
+
+        def o_of16():
+            cp(T.OF16[:], T.OF[:], "OF", "OF16")
+
+        def o_ht():
+            tt(T.HT[:], H, T.BASE[:, 0:64], A.subtract, "wH TR pW", "HT")
+
+        def o_ga():
+            u = (t + 1) % LB
+            if last:
+                pass
+            elif u < 4:
+                ts(GA, H, T.BC[:, u:u + 1], A.add, "wH BC pW", "wGA")
+            else:
+                i = (5, 6, 7, 9).index(u)
+                tt(GA, H, T.BW[:, 64 * i:64 * i + 64], A.add, "wH BW pW", "wGA")
+
+        ga, gk = (H, "wH") if last else (GA, "wGA")
+
+        def o_e1():
+            if not final:
+                tt(T.E1[:], LN_, ga, A.subtract, "NL pW " + gk, "E1")
+
+        def o_s():
+            ts(S, T.pS[:, 0:64], float(ROOT), A.min, "pS pW", "wS")
+
+        def o_d():
+            tt(T.D[:], S, LN_, A.subtract, "wS NL pW", "D")
+
+        def o_s2():
+            if not final:
+                tt(T.S2[:], S, T.K[:], A.min, "wS K pW", "S2")
+
+        def o_el():
+            if not final:
+                ts(TQ, T.D[:], 0.0, A.is_equal, "D pW", "wTQ", float(ROOT), A.mult)
+
+        def o_e2():
+            if not final:
+                tt(T.E2[:], ga, T.S2[:], A.subtract, "S2 pW " + gk, "E2")
+
+        def o_bl():
+            if not final:
+                tt(T.BASE[:, 128:192], TQ, LN_, A.max, "NL wTQ pW", "BL")
 
         def where(b):
             c, gr = b // 8, b % 8
-            bank = [p[3] for p in PIECES if p[1] <= c < p[2]][0]
-            return c, gr, 128 * c + 16 * gr, bank
+            bank = [p[2] for p in PIECES if p[0] <= c < p[1]][0]
+            return c, gr, 128 * c + 16 * gr + 15, bank
 
-        for b in range(64 - NA, 64):
+        def far(b):
             c, gr, o, bank = where(b)
-            w = 128 * (b - 64 + NA)
-            act(T.BT[:, w:w + 128], T.IO[:], F.Abs, "IO AT%d" % (c // 4), "BT%d" % b, bias=T.AT[:, o + 12:o + 13], scale=-1.0)
-        m = 16 * GP
+            act(T.BT[:, W * b:W * b + W], T.IO[:, 0:W], F.Abs, "IO AT%d" % (c // 4), "BT%d" % b,
+                bias=T.AT[:, o:o + 1], scale=-1.0)
 
-        def early():
-            cp(T.GX[:], GN_, "NEW", "GX")
-            tt(T.D[:], T.pS[:, 0:64], LN_, A.subtract, "pS NEW", "D")
-            if not final:
-                tt(T.S2[:], T.pS[:, 0:64], T.K[:], A.min, "pS K", "S2")
-            ts(T.H[:], T.GX[:], 4095, A.bitwise_and, "GX", "H")
-            ts(T.OI[:], T.GX[:], 255, A.bitwise_and, "GX", "OI")
-            ts(T.DS[:], T.D[:], 1.0 / 4096, A.mult, "D", "DS")
-            tt(T.HT[:], T.H[:], T.BASE[:, 0:64], A.subtract, "H TR", "HT")
-            cp(T.OF16[:], T.OI[:], "OI", "OF16")
-            if final:
-                return
-            u = (ST * n + k + 1) % LB
-            if last:
-                cp(T.GA[:], T.H[:], "H", "GA")
-            elif u < 4:
-                ts(T.GA[:], T.H[:], T.BC[:, u:u + 1], A.add, "H BC", "GA")
-            else:
-                i = (5, 6, 7, 9).index(u)
-                tt(T.GA[:], T.H[:], T.BW[:, 64 * i:64 * i + 64], A.add, "H BW", "GA")
-            ts(T.EL[:], T.D[:], 0.0, A.is_equal, "D", "EL", float(ROOT), A.mult)
+        def hit(b):
+            act(T.BB[:, W * b:W * b + W], T.BT[:, W * b:W * b + W], F.Relu, "BT%d AK%s" % (b, where(b)[3]), "BB%d" % b,
+                bias=T.AK2[:, b:b + 1], scale=-1.0)
 
-        def later():
-            if not final:
-                tt(T.E1[:], LN_, T.GA[:], A.subtract, "NEW GA", "E1")
-                t3("E2", "GA", "S2", A.subtract)
+        done = []
 
-        for b in range(64):
+        def count(b):
             c, gr, o, bank = where(b)
-            if b == PB and k > 0:
-                votes(*p1)
-            if b == VB:
-                asks(*p1)
-            if b == PC:
-                votes(*p2)
-            if b == VC:
-                asks(*p2)
-                if NA:
-                    act(T.AKN[:, 8 * p2[1]:64], T.AK2[:, 8 * p2[1]:64], F.Copy, "AKpC", "AKN", scale=-1.0)
-                    for b2 in range(64 - NA, 64):
-                        w = 128 * (b2 - 64 + NA)
-                        act(T.BB[:, 128 * b2:128 * b2 + 128], T.BT[:, w:w + 128], F.Relu, "BT%d AKpC AKN" % b2, "BB%d" % b2,
-                            bias=T.AK2[:, b2:b2 + 1], scale=T.AKN[:, b2:b2 + 1])
-            if b < 64 - NA:
-                bb = T.BB[:, 128 * b:128 * b + 128]
-                ts(bb, T.IO[:], T.AT[:, o + 12:o + 13], A.is_equal, "IO AK%s AT%d" % (bank, c // 4), "BB%d" % b,
-                   T.AK2[:, b:b + 1], A.mult)
-            if b == 63 - NA:
-                if n == 0 and k == 0:
-                    last_constants()
-                early()
-            mm(T.pH[:, 16 * gr:16 * gr + 12], T.BB[:, 128 * b:128 * b + 128], T.AT[:, o:o + 12], False, b == 63,
+            done.append(b)
+            mm(T.pH[0:W, 16 * gr + 2:16 * gr + 15], T.BB[:, W * b:W * b + W], T.AT[:, o - 13:o], False, len(done) == 64,
                "BB%d AT%d" % (b, c // 4), "pH")
-        act(T.GN[:, 0:1024 - m], T.GE[:, m:1024], F.Sign, "GE1", "GN")
-        if n == 0 and k == 0:
-            act(T.SELT[:], T.SELM[:], F.Identity, "SELM WU", "SELT", scale=T.WU[:])
-        ts(T.RR[:], T.pH[:, 0:128], MAGIC, A.add, "pH", "RR", MAGIC, A.subtract)
-        ts(T.FL1[:], T.pH[:, 0:128], MAGIC, A.add, "pH", "FL1", MAGIC + 2048, A.is_equal)
-        tt(T.FL0[:], T.pH[:, 0:128], T.RR[:], A.is_equal, "pH RR", "FL0")
-        mm(T.pD[:, 0:1024 - m], T.IDP[:], T.GN[:, 0:1024 - m], True, False, "IDP GN", "pD")
-        tr(T.pT[:, 128:256], T.FL1[:], "FL1", "pT")
-        tr(T.pT[:, 0:128], T.FL0[:], "FL0", "pT")
-        ext("pA", "SELM", T.SG, "SGpA SGpB SGpC")
-        later()
-        cp(T.FT[:], T.pT[:, 0:256], "pT", "FT")
-        tt(T.GF[:, 0:m], T.FT[:].indirect(T.OF16[:, 0:GP]), T.GE[:, 0:m], A.min, "FT OF16 GE0 GE1", "GF0")
-        gat("a", T.XS[:, 512:1536 - m], T.FT[:], T.OF16[:, GP:64], "FT OF16", "XS1")
-        mm(T.pD[:, 0:1024 - m], T.IDP[:], T.XS[:, 512:1536 - m], False, True, "IDP XS1", "pD")
-        act(T.GF[:, m:1024], T.pD[:, 0:1024 - m], F.Relu, "pD", "GF1", bias=-1.0)
-        ext("pS", "SELM", T.GF, "GF0 GF1")
-        AK = T.pW[:, 192:256]
-        tt(AK, T.pA[:, 0:64], T.DS[:], A.is_lt, "pA DS", "pW")
-        if not final:
-            tt(T.BASE[:, 128:192], LN_, T.EL[:], A.max, "NEW EL", "BL")
-        tt(T.DV[:, 0:64], AK, T.HT[:], A.mult, "pW HT", "+DV")
-        w = 64 if final else 192
-        if not final:
-            tt(T.T1[:], AK, T.E2[:], A.mult, "pW E2", "T1")
-            tt(T.DV[:, 64:128], AK, T.E1[:], A.mult, "pW E1", "+DV")
-            tt(T.DV[:, 128:192], AK, T.D[:], A.mult, "pW D", "+DV")
-            tt(T.BASE[:, 64:128], T.T1[:], T.S2[:], A.add, "T1 S2", "BG")
-        for o in range(0, w, 64):
-            tt(T.pW[:, o:o + 64], T.pS[:, 0:64], T.DV[:, o:o + 64], A.mult, "pS DV", "+pW")
-        tt(T.NEW[:, 0:w], T.pW[:, 0:w], T.BASE[:, 0:w], A.add, "pW TR BG BL", "NEW")
-        if not last:
-            ts(T.GL16[:], T.NEW[:, 64:192], float(TOP), A.min, "NEW", "GL16")
-        cp(T.SC16[:], T.NEW[:, 0:64], "NEW", "SC16")
-        if not last:
-            digits("a")
-            turn()
-            mm(T.pH[:, 0:128], T.IDP[:], T.NEG[:], True, False, "IDP NEG", "pH")
-            own_x("a", X, xk, 0, 64, "XL0 XL1")
-            mm(T.pD[:, 0:1024 - sa], T.IDN[:], T.XL[:, sa:1024], True, False, "IDN XL1", "pD")
+
+        gat("v", T.GS[:, 0:512], T.SW[:, 0:3088], T.GL16[:, 0:32], SW + " G16", "GS0")
+        gat("a", T.GS[:, 512:1024], T.SW[:, 0:3088], T.GL16[:, 32:64], SW + " G16", "GS1")
+        ext("pS", "SELS", T.GS, "GS0 GS1")
+        for c in range(8):
+            em("p", lambda: g.tensor.transpose(T.pT[:, 128 * c:128 * c + 128], T.GS[:, 128 * c:128 * c + 128], T.IDP[:]),
+               "IDP GS%d" % (c // 4), "pT")
+        if k == 0:
+            own_x("v", X, xk, 0)
+            own_digits("a", 0)
+            unsit()
+            own_x("a", X, xk, 1)
+            o_q()
+        else:
+            own_x("a", X, xk, 1)
+            o_h(), o_q()
+            o_ht(), o_ga(), o_tq()
+            o_e1(), o_of()
+        ts(T.S16[:], T.pS[:, 0:64], float(ROOT), A.min, "pS", "S16")
+        o_s()
+        if k:
+            o_of16()
+        else:
+            o_tq()
+        ties(*p0), ties2(*p0), ties(*p1), ties2(*p1), ties(*p2)
+        if k:
+            ties2(*p2)
+            patch()
+            minus_own()
+        diff(*p0)
+        gat("a", T.XS[:, 0:512], XW, T.S16[:, 32:64], xk + " S16", "XSa")
+        turned("v", 0)
+        cp(T.LO[:, 0:ND], T.pT[:, 15:16 * ND:16], "pT", "LO")
+        clip(*p0)
+        votes(*p0)
+        diff(*p1)
+        if k:
             turned("a", 1)
-        em("v", lambda: g.vector.tensor_copy(T.SW[:].indirect(T.SC16[:]), T.LD[:]), "SC16 LD0 LD1", SW)
+            mm(T.pD[:], T.IDP[:], T.XS[:, 0:512], False, True, "IDP XSa", "pD")
+            for b in (s1 + s2)[:nb]:
+                far(b)
+            act(T.SG[:, 512:1024], T.pD[:], F.Sign, "pD", "SGpC")
+            for b in (s1 + s2)[nb:]:
+                far(b)
+        else:
+            own_digits("a", 1)
+        o_d(), o_s2()
+        asks(*p0)
+        m = 16 * GP
+        mine = [b for b in range(64) if b not in s1 + s2]
+        for i, b in enumerate(mine):
+            c, gr, o, bank = where(b)
+            if i == cl:
+                clip(*p1)
+            if i == pb:
+                votes(*p1)
+                if k == 0:
+                    minus_own()
+                    mm(T.pD[:], T.IDP[:], T.XS[:, 0:512], False, True, "IDP XSa", "pD")
+                    act(T.SG[:, 512:1024], T.pD[:], F.Sign, "pD", "SGpC")
+                    turned("a", 1)
+                    for b2 in s1 + s2:
+                        far(b2)
+            if i == vb:
+                asks(*p1)
+                for b2 in s1:
+                    hit(b2)
+            if i == pc:
+                if k == 0:
+                    ties2(*p2)
+                    patch()
+                votes(*p2)
+            if i == vc:
+                asks(*p2)
+                for b2 in s2:
+                    hit(b2)
+            bb = T.BB[:, W * b:W * b + W]
+            if i < ND:
+                ts(bb, T.IO[:, 0:W], T.LO[:, b:b + 1], A.not_equal, "IO pA LO", "BB%d" % b, T.pA[:, b:b + 1], A.is_lt)
+            else:
+                ts(bb, T.IO[:, 0:W], T.AT[:, o:o + 1], A.is_equal, "IO AK%s AT%d" % (bank, c // 4), "BB%d" % b,
+                   T.AK2[:, b:b + 1], A.mult)
+            count(b)
+            for j, his in ((j1, s1), (j2, s2)):
+                if 0 <= i - j < len(his):
+                    count(his[i - j])
+        for b in s1 + s2:
+            if b not in done:
+                count(b)
+        if k == 0:
+            o_h(), o_of()
+        o_el()
+        if k == 0:
+            o_ga(), o_of16(), o_ht()
+        else:
+            o_e2()
+        ext("pA", "SELM", T.SG, "SGpA SGpB SGpC")
+        if GP < 64:
+            act(T.GN[:, 0:1024 - m], T.GS[:, m:1024], F.Sign, "GS1", "GN")
+            mm(T.pD[:, 0:1024 - m], T.IDP[:], T.GN[:, 0:1024 - m], True, False, "IDP GN", "pD")
+        if t == 0:
+            act(T.SELF[:], T.SELM[:], F.Copy, "SELM", "SELF", scale=1.0 / 4096)
+        ts(T.RR[0:W, :], T.pH[0:W, 0:128], MAGIC, A.add, "pH", "RR", MAGIC, A.subtract)
+        ts(T.FL1[0:W, :], T.pH[0:W, 0:128], MAGIC, A.add, "pH", "FL1", MAGIC + 2048, A.is_equal)
+        o_bl()
+        tt(T.FL0[0:W, :], T.pH[0:W, 0:128], T.RR[0:W, :], A.is_equal, "pH RR", "FL0")
+        for f in (1, 0):
+            em("p", lambda: g.tensor.transpose(T.pT[:, W * f:W * f + W], T["FL%d" % f][0:W, :], T.IDP[0:W, 0:W]),
+               "IDP FL%d" % f, "pT")
+        if k == 0:
+            o_e1(), o_e2()
+        tt(AK, T.pA[:, 0:64], T.D[:], A.is_lt, "pA D pW", "wAK")
+        win = T.FT[:, 0:2 * W]
+        cp(win, T.pT[:, 0:2 * W], "pT", "FT")
+        if not final:
+            tt(TQ, AK, T.E2[:], A.mult, "wAK E2 pW", "wTQ")
+        tt(T.DV[:, 0:64], AK, T.HT[:], A.mult, "wAK HT pW", "+DV")
+        tt(T.GF[:, 0:m], win.indirect(T.OF16[:, 0:GP]), T.GS[:, 0:m], A.min, "FT OF16 GS0 GS1", "GF0")
+        if GP < 64:
+            gat("a", T.XS[:, 512:1536 - m], win, T.OF16[:, GP:64], "FT OF16", "XSb")
+            mm(T.pD[:, 0:1024 - m], T.IDP[:], T.XS[:, 512:1536 - m], False, True, "IDP XSb", "pD")
+            act(T.GF[:, m:1024], T.pD[:, 0:1024 - m], F.Relu, "pD", "GF1", bias=-1.0)
+        ext("pS", "SELF", T.GF, "GF0 GF1")
+        if not final:
+            tt(T.DV[:, 64:128], AK, T.E1[:], A.mult, "wAK E1 pW", "+DV")
+            tt(T.DV[:, 128:192], AK, T.D[:], A.mult, "wAK D pW", "+DV")
+            tt(T.BASE[:, 64:128], TQ, T.S2[:], A.add, "wTQ S2 pW", "BG")
+        parts = (0,) if final else (0, 2, 1)
+        for i in parts:
+            tt(T.pW[:, 64 * i:64 * i + 64], T.pS[:, 0:64], T.DV[:, 64 * i:64 * i + 64], A.mult, "pS DV pW wT", "wT%d" % i)
+        for i in parts:
+            tt(T.NEW[:, 64 * i:64 * i + 64], T.pW[:, 64 * i:64 * i + 64], T.BASE[:, 64 * i:64 * i + 64], A.add,
+               "wT%d pW wT %s" % (i, ("TR", "BG", "BL")[i]), ("NC", "NG", "NL")[i])
+        cp(T.SC16[:], T.NEW[:, 0:64], "NC", "SC16")
+        if not last:
+            cp(T.GL16[:, 64:128], LN_, "NL", "L16")
+            ts(T.GL16[:, 0:64], GN_, float(TOP), A.min, "NG", "G16")
+            own_x("a", X, xk, 0)
+            own_digits("a", 0)
+            unsit()
+            own_digits("a", 1)
+            clear_counts()
+        if k == 0:
+            dma("s", X[:, SELF:SELF + 3072], X[:, 0:3072], xk + " SC16", xk[0:2] + "h")
+        em("v", lambda: g.vector.tensor_copy(T.SW[:].indirect(T.SC16[:]), T.GS[:]), "SC16 GS0 GS1", SW)
 
     def pass_on(n):
-        ts(T.UP[:], LN_, float(ROOT), A.is_equal, "NEW", "UP")
-        tt(T.PF2[:], T.EF[:], T.NEW[:, 64:192], A.subtract, "EF NEW", "PF2")
-        tt(T.pW[:, 0:64], T.PF2[:, 0:64], T.UP[:], A.mult, "PF2 UP", "pW")
-        tt(T.pW[:, 64:128], T.PF2[:, 64:128], T.UP[:], A.mult, "PF2 UP", "+pW")
-        tt(T.RR[:], T.pW[:, 0:128], T.NEW[:, 64:192], A.add, "pW NEW", "RR")
+        yield ts(T.UP[:], LN_, float(ROOT), A.is_equal, "NL", "UP")
+        yield tt(T.PF2[:], T.EF[:], T.NEW[:, 64:192], A.subtract, "EF NG NL", "PF2")
+        yield tt(T.P3[:, 0:64], T.PF2[:, 0:64], T.UP[:], A.mult, "PF2 UP", "+P3")
+        yield tt(T.P3[:, 64:128], T.PF2[:, 64:128], T.UP[:], A.mult, "PF2 UP", "+P3")
+        yield tt(T.P4[:], T.P3[:], T.NEW[:, 64:192], A.add, "P3 NG NL", "P4")
         sp = "SP%d" % n
-        cp(T[sp][:], T.RR[:], "RR", sp)
-        send(T["LP%d" % n][:], T[sp][:], "r%d" % n, "s%d" % n, sp)
+        cp(T[sp][:], T.P4[:], "P4", sp)
+        yield send(T["LP%d" % n][:], T[sp][:], "r%d" % n, "s%d" % n, sp)
 
     def round_end(n, X, xk, Y, yk):
         final = n == RO - 1
-        lb, db = ("pS", "pA", "pS"), ("pB", "pC", "pD")
-        cut = [1024 * (c + 1) - 16 * RE[c] for c in range(3)]
-        for c in range(3):
-            a, b = 1024 * c, cut[c]
-            act(T.XP[:, a:b], X[:, a:b], F.Identity, xk, "+XP", bias=1.0)
-            act(T.XM[:, a:b], X[:, a:b], F.Identity, xk, "+XM", bias=-1.0)
-            mm(T[db[c]][:, 0:16 * RE[c]], T.IDN[:], X[:, b:1024 * (c + 1)], True, False, "IDN " + xk, db[c])
-        mm(T.pH[:, 0:16 * RE[0]], T.IDP[:], X[:, cut[0]:1024], True, False, "IDP " + xk, "pH")
+        key, xh = "abcdfg", xk + " " + xk[0:2] + "h "
+        for a, b, e, bank in SEG:
+            if e == "v":
+                act(T.XP[:, a:b], X[:, a:b], F.Identity, xk, "+XP", bias=1.0)
+                act(T[bank][:, 0:b - a], X[:, a:b], F.Identity, xk, bank, bias=-1.0)
+            else:
+                mm(T[bank][:, 0:b - a], T.IDN[:], X[:, a:b], True, False, "IDN " + xk, bank)
         if final:
-            dma("s", T.D0[:], T.SW[2:128:16, 0:3072], SW, "D0")
-            dma("s", T.D1[:], T.SW[3:128:16, 0:3072], SW, "D1")
+            dma("s", T.D0[:], T.SW[0:128:16, 0:3072], SW, "D0")
+            dma("s", T.D1[:], T.SW[1:128:16, 0:3072], SW, "D1")
 
         def lists(c):
-            ext(lb[c], "SELT", T.SW, SW, 64 * c)
+            ext("pS", "SELS", T.SW, SW, 64 * c)
 
         def listed(c):
-            cp(T.SL16[:, 64 * c:64 * c + 64], T[lb[c]][:, 0:64], lb[c], "SL%d" % c)
+            cp(T.SL16[:, 64 * c:64 * c + 64], T.pS[:, 0:64], "pS", "SL%d" % c)
 
-        def lo(c):
-            a, b = 1024 * c, cut[c]
-            tt(T.DD[:, a:b], X[:].indirect(T.SL16[:, a // 16:b // 16]), T.XP[:, a:b], A.min, xk + " XP SL%d" % c,
-               "DDpA DDpB" if c == 0 else "DD%d" % c)
+        def lk(a, b):
+            return " ".join("SL%d" % c for c in range(a // 1024, (b - 1) // 1024 + 1))
 
-        def hi(c):
-            a, b = 1024 * c, cut[c]
-            tt(Y[:, a:b], T.DD[:, a:b], T.XM[:, a:b], A.max, "XM " + ("DDpA DDpB" if c == 0 else "DD%d" % c), yk + "abc"[c])
+        def fetch(i):
+            a, b, e, bank = SEG[i]
+            if e == "v":
+                tt(T.DD[:, a:b], X[:].indirect(T.SL16[:, a // 16:b // 16]), T.XP[:, a:b], A.min,
+                   xh + "XP " + lk(a, b), "DDpA DDpB DD" + key[i] if a < 1024 else "DD" + key[i])
+            else:
+                gat("a", T.XS[:, a:b], X[:], T.SL16[:, a // 16:b // 16], xh + lk(a, b), "XS" + key[i])
+
+        def minus(i):
+            a, b, e, bank = SEG[i]
+            mm(T[bank][:, 0:b - a], T.IDP[:], T.XS[:, a:b], False, True, "IDP XS" + key[i], bank)
+
+        def sign(i):
+            a, b, e, bank = SEG[i]
+            act(T[bank][:, 0:b - a], T[bank][:, 0:b - a], F.Sign, bank, bank)
+
+        def put(i):
+            a, b, e, bank = SEG[i]
+            if e == "v":
+                tt(Y[:, a:b], T[bank][:, 0:b - a], T.DD[:, a:b], A.max, bank + " DD" + key[i], yk + key[i])
+            else:
+                tt(Y[:, a:b], T[bank][:, 0:b - a], X[:, a:b], A.add, bank + " " + xk, yk + key[i])
             if final:
-                dma("s", T.yx[:, a:b], Y[:, a:b], yk + "abc"[c], "ox" + "abc"[c])
+                dma("s", T.yx[:, a:b], Y[:, a:b], yk + key[i], "ox" + key[i])
 
-        def ga(c):
-            w = 16 * RE[c]
-            gat("a", T.XS[:, 512 * c:512 * c + w], X[:], T.SL16[:, cut[c] // 16:64 * (c + 1)], xk + " SL%d" % c, "XS%d" % c)
+        on = iter(()) if final else pass_on(n)
 
-        def gd(c):
-            w = 16 * RE[c]
-            mm(T[db[c]][:, 0:w], T.IDP[:], T.XS[:, 512 * c:512 * c + w], False, True, "IDP XS%d" % c, db[c])
-
-        def sg(c):
-            w = 16 * RE[c]
-            act(T.SN[:, 512 * c:512 * c + w], T[db[c]][:, 0:w], F.Sign, db[c], "SN%d" % c)
-
-        def ad(c):
-            w, bank = 16 * RE[c], ("pH", "pB", "pC")[c]
-            if c:
-                mm(T[bank][:, 0:w], T.IDP[:], X[:, cut[c]:1024 * (c + 1)], True, False, "IDP " + xk, bank)
-            mm(T[bank][:, 0:w], T.IDP[:], T.SN[:, 512 * c:512 * c + w], False, True, "IDP SN%d" % c, bank)
-
-        def ev(c):
-            w, bank = 16 * RE[c], ("pH", "pB", "pC")[c]
-            a, b = cut[c], 1024 * (c + 1)
-            act(Y[:, a:b], T[bank][:, 0:w], F.Copy, bank, yk + "dfg"[c])
-            if final:
-                dma("a", T.yx[:, a:b], Y[:, a:b], yk + "dfg"[c], "ox" + "dfg"[c])
-        lists(0)
-        if not final:
-            pass_on(n)
-        listed(0), lists(1), ga(0), lo(0), listed(1), lists(2), gd(0), ga(1), sg(0), hi(0), listed(2), gd(1), ad(0)
-        ga(2), sg(1), lo(1), gd(2), ad(1), ev(0), sg(2), ad(2), hi(1), lo(2), ev(1), ev(2)
+        def go(c):
+            for _ in range(c):
+                next(on, None)
+        lists(0), go(2), listed(0), lists(1), fetch(0), go(2), fetch(1), listed(1), minus(0), lists(2), fetch(2), sign(0)
+        go(1), put(1), go(1), listed(2), minus(2), fetch(3), sign(2), fetch(4)
         if final:
-            ts(T.Y2[:], T.D0[:], 64.0, A.mult, "D0", "Y2")
-            tt(T.Y3[:], T.Y2[:], T.D1[:], A.add, "Y2 D1", "Y3")
-            dma("s", T.ys[:], T.Y3[:], "Y3", "oy")
-        hi(2)
+            ts(T.D2[:], T.D0[:], SELF / 64, A.is_ge, "D0", "D2", -SELF / 64, A.mult)
+            for i, (w, d) in enumerate((("ID6", "D0"), ("IDP", "D1"), ("ID6", "D2"))):
+                mm(T.pS[:, 0:192], T[w][:], T[d][:], i == 0, i == 2, w + " " + d, "pS")
+        minus(3), fetch(5), sign(3), minus(5)
+        if final:
+            act(T.Y3[:], T.pS[:, 0:192], F.Copy, "pS", "Y3")
+            dma("a", T.ys[:], T.Y3[:], "Y3", "oy")
+        sign(5)
+        put(0), put(4), put(2), put(3), put(5)
 
     X, Y, xk, yk = T.XA, T.XB, "X0", "X1"
     for n in range(RO):

@@ -4,19 +4,29 @@ RO, ST, LB = 3, 4, 10
 TOP, ROOT, SELF, SIT = 3072, 3073, 3136, 8192.0
 MAGIC = 3.0 * 2 ** 33
 W = 120
-PIECES = ((0, 2, "pA"), (2, 4, "pB"), (4, 8, "pC"))
+CUT = 4
+
+
+def pieces(k):
+    cut = CUT if k else 4
+    return (0, 1, "pA", ""), (1, 2, "pB", ""), (2, cut, "pS", "pC"), (cut, 8, "pA", "pD")
+
+
 GP = 50
-ND = 4
+HB = ("pH", "pC")
+RV = 24
+RA = 52
 RS = 36
-AT0 = (0, 5, 0, 2, 2, 12, 20, 30, 40, 56)
-ATK = (4, 6, 2, 2, 2, 12, 12, 24, 34, 43)
-SEG = ((0, 512, "a", "pA"), (512, 1024, "v", "pW"), (1024, 1536, "a", "pB"), (1536, 2048, "a", "pC"),
-       (2048, 2560, "v", "pH"), (2560, 3072, "a", "pD"))
+AT0 = (0, 6, 0, 4, 2, 12, 4, 10, 24, 40, 41)
+ATK = (0, 9, 0, 3, 1, 13, 2, 12, 29, 30, 38)
+RC = 2656
+SEG = ((0, 512, "a", "pA"), (512, 1024, "a", "pB"), (1024, 1536, "v", "pW"), (1536, 2048, "a", "pC"),
+       (2048, 2560, "v", "pH"), (2560, RC, "v", "XM"), (RC, 3072, "a", "pD"))
 DT = {"b": "bfloat16", "f": "float32", "i": "int32", "u": "uint16"}
 SCRATCH = {}
-for _t in ("b6208 XA XB;b3088 DG;b4112 SW;b1024 GS XL LD SG AT GF;b3072 DD XP XS;b7680 BB BT;b512 GN;"
+for _t in ("b6208 XA XB;b3088 DG;b4112 SW;b1024 GS XL LD SG AT GF;b3072 DD XP XS;b7680 BB BT;b512 GN XM;"
            "b64 AK2 S2G;b128 IO IDP IDN ID6 NEG FL0 FL1;b256 WR IH IL B2 FT;i128 EI;f128 RR EF PF2 P3 P4;"
-           "b2048 SELS SELM SELF;b8 M2 S2L;i1 PI GI QI;f1 PF GFC QF GC WT N1 N2;f16 EQ EC GQ KB E4 LO;"
+           "b2048 SELS SELM SELF;b8 M2 S2L;i1 PI GI QI;f1 GFC QF GC WT;b1 PF N1 N2;b16 EQ EC GQ KB;f16 E4;"
            "i4 BI;f4 BC;i192 UI W1 W2 SI;b192 D0 D1 D2;f192 Y3 NEW BASE DV;u192 SL16;i64 LV Q;"
            "u128 ED EDN LP0 LP1 SP0 SP1 GL16;f256 BW;"
            "f64 D K HT E1 E2 S2 UP OF;u64 S16 OF16 SC16").split(";"):
@@ -148,7 +158,7 @@ def rank_program(g, core, T, topo):
     dma("s", T.SI[:], T.succ[:], "", "SI")
     dma("a", T.EI[:, 0:64], T.ea[:], "", "EIa")
     dma("a", T.EI[:, 64:128], T.eb[:], "", "EIb")
-    dma("s", T.XA[:, 0:3072], T.x[:], "", "X0a X0b X0c X0d X0f X0g")
+    dma("s", T.XA[:, 0:3072], T.x[:], "", "X0a X0b X0c X0d X0f X0g X0i")
 
     iota("PI", [[1, 1]], 1)
     iota("IO", [[1, 128]], 0)
@@ -177,19 +187,26 @@ def rank_program(g, core, T, topo):
     ts(T.N1[:], T.EQ[:, 15:16], -1.0, A.mult, "EQ", "N1", 1.0, A.add)
     ts(T.N2[:], T.EQ[:, 15:16], -2048.0, A.mult, "EQ", "N2", 2048.0, A.add)
     ts(T.EC[:], T.EQ[:], T.EQ[:, 15:16], A.max, "EQ", "EC")
-    ts(T.B2[:], T.IH[:], T.EQ[:, 0:1], A.mult, "IH EQ", "B2")
-    ts(T.FT[:], T.IL[:], T.EQ[:, 1:2], A.mult, "IL EQ", "FT")
-    ts(T.WR[:, 0:W], T.IO[:, 0:W], T.EQ[:, 15:16], A.mult, "IO EQ N1", "WR", T.N1[:], A.add)
-    ts(T.WR[:, W:2 * W], T.IO[:, 0:W], T.EQ[:, 15:16], A.mult, "IO EQ N2", "+WR", T.N2[:], A.add)
     ts(T.KB[:], T.IO[:, 0:16], T.EQ[:, 0:1], A.mult, "IO EQ", "KB", 4.0, A.mult)
     ts(T.pW[:, 0:192], T.UI[:], T.GC[:], A.add, "UI GC pW", "wT")
-    tt(T.B2[:], T.B2[:], T.FT[:], A.add, "B2 FT", "B2")
-    for k in range(13):
-        w = 256 if k < 12 else 16
-        act(T.DG[:, 256 * k:256 * k + w], T.B2[:, 0:w], F.Identity, "B2 KB", "+DG", bias=T.KB[:, k:k + 1])
+    ts(T.WR[:, 0:W], T.IO[:, 0:W], T.EQ[:, 15:16], A.mult, "IO EQ N1", "WR", T.N1[:], A.add)
+    ts(T.WR[:, W:2 * W], T.IO[:, 0:W], T.EQ[:, 15:16], A.mult, "IO EQ N2", "+WR", T.N2[:], A.add)
+    ts(T.E4[:], T.EQ[:], 1.0 / 4096, A.mult, "EQ", "E4")
+    ts(T.BC[:], T.BI[:], SIT, A.mult, "BI", "BC")
+    ts(T.B2[:], T.IH[:], T.EQ[:, 0:1], A.mult, "IH EQ", "B2")
     for k in range(13):
         a, w = 2 * W * k, min(2 * W, 3072 - 2 * W * k)
         ts(T.SW[:, a:a + w], T.WR[:, 0:w], T.EC[:, k + 2:k + 3], A.mult, "WR EC", "+SW0 +SW1")
+        if k == 3:
+            ts(T.pW[:, 256:512], T.IL[:], T.EQ[:, 1:2], A.mult, "IL EQ pW", "wAK wH wGA wTQ wS")
+        if k == 5:
+            tt(T.B2[:], T.pW[:, 256:512], T.B2[:], A.add, "B2 wAK pW", "B2")
+    for k in range(13):
+        w = 256 if k < 12 else 16
+        act(T.DG[:, 256 * k:256 * k + w], T.B2[:, 0:w], F.Identity, "B2 KB", "+DG", bias=T.KB[:, k:k + 1])
+    ts(T.WT[:], T.E4[:, 0:1], 64.0, A.mult, "E4", "WT", T.E4[:, 1:2], A.add)
+    tt(T.P3[:, 0:64], T.EI[:, 0:64], T.EI[:, 64:128], A.max, "EIa EIb", "+P3")
+    tt(T.P3[:, 64:128], T.EI[:, 0:64], T.EI[:, 64:128], A.min, "EIa EIb", "+P3")
     tt(T.Y3[:], T.pW[:, 0:192], T.SI[:], A.is_equal, "SI wT pW", "Y3")
     ts(T.W2[:], T.SI[:], 63, A.bitwise_and, "SI", "W2")
     ts(T.W1[:], T.SI[:], 6, A.arith_shift_right, "SI", "W1")
@@ -198,16 +215,13 @@ def rank_program(g, core, T, topo):
     dma("s", T.SW[1:128:16, 0:3072], T.D1[:], "D1", "SW1")
     tt(T.D0[:], T.pW[:, 192:384], T.W1[:], A.add, "W1 wAK pW", "D0")
     dma("s", T.SW[0:128:16, 0:3072], T.D0[:], "D0", "SW0")
-    cp(T.ED[:], T.EI[:], "EIa EIb", "ED")
+    cp(T.ED[:], T.P3[:], "P3", "ED")
     send(T.EDN[:], T.ED[:], "re", "se", "ED")
     iota("LV", [[16, 64]], 0)
     for i, b in enumerate((1, 2, 3, 5)):
         iota("BW", [[0, 32 >> b], [int(SIT), 2], [0, 1 << b]], 0, 64 * i, 64 * i + 64)
-    ts(T.E4[:], T.EQ[:], 1.0 / 4096, A.mult, "EQ", "E4")
     for q in range(16):
         ts(T.SELM[:, q * 128:(q + 1) * 128], T.IO[:], T.GQ[:, q:q + 1], A.is_equal, "IO GQ", "+SELM", 4096.0, A.mult)
-    ts(T.WT[:], T.E4[:, 0:1], 64.0, A.mult, "E4", "WT", T.E4[:, 1:2], A.add)
-    ts(T.BC[:], T.BI[:], SIT, A.mult, "BI", "BC")
 
     def more_constants():
         sel = T.SELM[:, 0:128:16]
@@ -228,14 +242,11 @@ def rank_program(g, core, T, topo):
     def own_x(e, X, xk, h):
         gat(e, T.XL[:, 512 * h:512 * h + 512], X[:, 0:3088], T.GL16[:, 64 + 32 * h:96 + 32 * h], xk + " L16", "XL%d" % h)
 
-    def minus_own():
-        mm(T.pD[:], T.IDN[:], T.XL[:, 512:1024], True, False, "IDN XL1", "pD")
-
     def own_digits(e, h):
         gat(e, T.LD[:, 512 * h:512 * h + 512], T.DG[:], T.GL16[:, 64 + 32 * h:96 + 32 * h], "DG L16", "LD%d" % h)
 
-    def clear_counts():
-        mm(T.pH[:, 0:128], T.IDP[:], T.NEG[:], True, False, "IDP NEG", "pH")
+    def clear_counts(h):
+        mm(T[HB[h]][:, 0:64], T.IDP[:], T.NEG[:, 0:64], True, False, "IDP NEG", HB[h])
 
     def unsit():
         act(T.K[:], GN_, F.Abs, "NG", "K", bias=-SIT)
@@ -247,18 +258,28 @@ def rank_program(g, core, T, topo):
             lst, lk = T["LP%d" % (n - 1)], "LP%d" % (n - 1)
             landed("r%d" % (n - 1), lk)
         m, w, X = 16 * RS, 1024 - 16 * RS, X[:, 0:3088]
-        gat("v", T.XL[:, 0:m], X, lst[:, 64:64 + RS], xk + " " + lk, "XL0")
-        gat("a", T.XL[:, m:1024], X, lst[:, 64 + RS:128], xk + " " + lk, "XL1")
-        mm(T.pD[:, 0:w], T.IDN[:], T.XL[:, m:1024], True, False, "IDN XL1", "pD")
-        gat("a", T.XS[:, 0:w], X, lst[:, RS:64], xk + " " + lk, "XSa")
-        mm(T.pD[:, 0:w], T.IDP[:], T.XS[:, 0:w], False, True, "IDP XSa", "pD")
-        act(T.SG[:, m:1024], T.pD[:, 0:w], F.Sign, "pD", "SGpC")
+        rd = xk + " " + lk
+        vs, ss = ((0, RV, "0"), (RV, RS, "1 2")), ((RS, RA, "pC", "a"), (RA, 64, "pD", "b"))
+        gat("a", T.XL[:, m:1024], X, lst[:, 64 + RS:128], rd, "XL1")
+        for a, b, bank, key in ss:
+            mm(T[bank][:, 0:16 * (b - a)], T.IDN[:], T.XL[:, 16 * a:16 * b], True, False, "IDN XL1", bank)
+        for a, b, bank, key in ss:
+            gat("a", T.XS[:, 16 * a:16 * b], X, lst[:, a:b], rd, "XS" + key)
+            mm(T[bank][:, 0:16 * (b - a)], T.IDP[:], T.XS[:, 16 * a:16 * b], False, True, "IDP XS" + key, bank)
+        for a, b, bank, key in ss:
+            act(T.SG[:, 16 * a:16 * b], T[bank][:, 0:16 * (b - a)], F.Sign, bank, "+SG3")
+        gat("v", T.XL[:, 0:16 * RV], X, lst[:, 64:64 + RV], rd, "XL0")
+        gat("v", T.XL[:, 16 * RV:m], X, lst[:, 64 + RV:64 + RS], rd, "XL2")
+        for a, b, key in vs:
+            tt(T.DD[:, 16 * a:16 * b], X.indirect(lst[:, a:b]), T.XL[:, 16 * a:16 * b], A.subtract,
+               rd + (" XL2" if a else " XL0"), " ".join("DD" + c for c in key.split()))
+        for a, b, key in vs:
+            ts(T.SG[:, 16 * a:16 * b], T.DD[:, 16 * a:16 * b], 1.0, A.min, " ".join("DD" + c for c in key.split()),
+               " ".join("SG" + c for c in key.split()), -1.0, A.max)
+        ext("pA", "SELM", T.SG, "SG0 SG1 SG2 SG3")
         cp(T.PF2[:], lst[:], lk, "PF2")
-        tt(T.DD[:, 0:m], X.indirect(lst[:, 0:RS]), T.XL[:, 0:m], A.subtract, xk + " XL0 " + lk, "DDpA DDpB")
-        tt(T.D[:], T.PF2[:, 0:64], T.PF2[:, 64:128], A.subtract, "PF2", "D")
-        ts(T.SG[:, 0:m], T.DD[:, 0:m], 1.0, A.min, "DDpA DDpB", "SGpA SGpB", -1.0, A.max)
-        ext("pA", "SELM", T.SG, "SGpA SGpB SGpC")
-        clear_counts()
+        tt(T.D[:], T.PF2[:, 0:64], T.PF2[:, 64:128], A.add, "PF2", "D")
+        clear_counts(0)
         if n == 0:
             act(T.SELS[:], T.SELM[:], F.Identity, "SELM WT", "SELS", scale=T.WT[:])
             more_constants()
@@ -267,47 +288,67 @@ def rank_program(g, core, T, topo):
                 landed("re", "EDN")
             e = T.ED if n == 0 else T.EDN
             cp(T.EF[:], e[:], "ED" if n == 0 else "EDN", "EF")
-        tt(AK, T.pA[:, 0:64], T.D[:], A.is_gt, "pA D pW", "wAK")
-        tt(T.pW[:, 0:64], AK, T.D[:], A.mult, "wAK D pW", "wT")
-        tt(GN_, T.pW[:, 0:64], T.PF2[:, 64:128], A.add, "wT PF2 pW", "NG")
-        tt(LN_, T.PF2[:, 0:64], T.pW[:, 0:64], A.subtract, "wT PF2 pW", "NL")
+        tt(AK, T.pA[:, 0:64], T.PF2[:, 0:64], A.min, "pA PF2 pW", "wAK")
+        tt(GN_, AK, T.PF2[:, 64:128], A.max, "wAK PF2 pW", "NG")
         cp(T.GL16[:, 0:64], GN_, "NG", "G16")
-        cp(T.GL16[:, 64:128], LN_, "NL", "L16")
+        tt(LN_, T.D[:], GN_, A.subtract, "D NG", "NL")
 
     def step(n, k, X, xk):
         t = ST * n + k
         last = k == ST - 1
         final = last and n == RO - 1
-        p0, p1, p2 = PIECES
-        n1, n2, nb, cl, pb, vb, pc, vc, j1, j2 = AT0 if k == 0 else ATK
-        s1, s2 = list(range(32 - n1, 32)), list(range(64 - n2, 64))
+        n1, n2, p3, a1, v2, a2, t3, v3, a3, j1, j2 = AT0 if k == 0 else ATK
+        PIECES = pieces(k)
+        cut = 8 * PIECES[3][0]
+        s1, s2 = list(range(cut - n1, cut)), [b for b in range(cut, 64) if b % 8 >= 4][:n2]
+
+        def minus_own(p, k=0):
+            a, b, bank, db = pieces(k)[p]
+            mm(T[db][:, 0:128 * (b - a)], T.IDN[:], T.XL[:, 128 * a:128 * b], True, False, "IDN XL0 XL1", db)
+
+        mine = sorted((b for b in range(64) if b not in s1 + s2), key=lambda b: (b >= 48 and b % 8 >= 4, b))
         XW = X[:, 0:3088]
 
-        def ties(a, b, bank):
+        def ties(p):
+            a, b, bank = PIECES[p][0:3]
             for c in range(a, b):
                 w = 8 * (b - a) if c == a else 8
                 mm(T[bank][:, 8 * (c - a):8 * (c - a) + w], T.GS[:, 128 * c:128 * c + 128], T.S2G[:, 0:w], c == a, False,
                    "GS%d S2G" % (c // 4), bank)
-
-        def ties2(a, b, bank):
             for c in range(a, b):
                 mm(T[bank][:, 8 * (c - a):8 * (c - a) + 8], T.LD[:, 128 * c:128 * c + 128], T.S2L[:], False, False,
                    "LD%d S2L" % (c // 4), bank)
 
-        def diff(a, b, bank):
+        def diff(p):
+            a, b = PIECES[p][0:2]
             tt(T.DD[:, 128 * a:128 * b], XW.indirect(T.S16[:, 8 * a:8 * b]), T.XL[:, 128 * a:128 * b], A.subtract,
-               xk + " XL0 S16", "DD" + bank)
+               xk + " XL0 S16", "DD%d" % p)
 
-        def clip(a, b, bank):
-            ts(T.SG[:, 128 * a:128 * b], T.DD[:, 128 * a:128 * b], 1.0, A.min, "DD" + bank, "SG" + bank, -1.0, A.max)
+        def clip(p):
+            a, b = PIECES[p][0:2]
+            ts(T.SG[:, 128 * a:128 * b], T.DD[:, 128 * a:128 * b], 1.0, A.min, "DD%d" % p, "SG%d" % p, -1.0, A.max)
 
-        def votes(a, b, bank):
+        def fetch(p):
+            a, b = PIECES[p][0:2]
+            gat("a", T.XS[:, 128 * a:128 * b], XW, T.S16[:, 8 * a:8 * b], xk + " S16", "XS" + "ab"[p - 2])
+
+        def plus(p):
+            a, b, bank, db = PIECES[p]
+            mm(T[db][:, 0:128 * (b - a)], T.IDP[:], T.XS[:, 128 * a:128 * b], False, True, "IDP XS" + "ab"[p - 2], db)
+
+        def sign(p):
+            a, b, bank, db = PIECES[p]
+            act(T.SG[:, 128 * a:128 * b], T[db][:, 0:128 * (b - a)], F.Sign, db, "SG%d" % p)
+
+        def votes(p):
+            a, b, bank = PIECES[p][0:3]
             for c in range(a, b):
                 mm(T[bank][:, 8 * (c - a):8 * (c - a) + 8], T.SG[:, 128 * c:128 * c + 128], T.M2[:], False, c == b - 1,
-                   "M2 SG" + bank, bank)
+                   "M2 SG%d" % p, bank)
 
-        def asks(a, b, bank):
-            ts(T.AK2[:, 8 * a:8 * b], T[bank][:, 0:8 * (b - a)], 0.0, A.is_gt, bank, "AK" + bank)
+        def asks(p):
+            a, b, bank = PIECES[p][0:3]
+            ts(T.AK2[:, 8 * a:8 * b], T[bank][:, 0:8 * (b - a)], 0.0, A.is_gt, bank, "AK%d" % p)
 
         def patch():
             for r in (0, 1):
@@ -371,8 +412,7 @@ def rank_program(g, core, T, topo):
 
         def where(b):
             c, gr = b // 8, b % 8
-            bank = [p[2] for p in PIECES if p[0] <= c < p[1]][0]
-            return c, gr, 128 * c + 16 * gr + 15, bank
+            return c, gr, 128 * c + 16 * gr + 15, str([p[0] <= c < p[1] for p in PIECES].index(True))
 
         def far(b):
             c, gr, o, bank = where(b)
@@ -388,9 +428,12 @@ def rank_program(g, core, T, topo):
         def count(b):
             c, gr, o, bank = where(b)
             done.append(b)
-            mm(T.pH[0:W, 16 * gr + 2:16 * gr + 15], T.BB[:, W * b:W * b + W], T.AT[:, o - 13:o], False, len(done) == 64,
-               "BB%d AT%d" % (b, c // 4), "pH")
+            bank, a = HB[gr // 4], 16 * (gr % 4)
+            mm(T[bank][0:W, a + 2:a + 15], T.BB[:, W * b:W * b + W], T.AT[:, o - 13:o], False,
+               sum(d % 8 // 4 == gr // 4 for d in done) == 32, "BB%d AT%d" % (b, c // 4), bank)
 
+        if k == 0:
+            cp(T.GL16[:, 64:128], LN_, "NL", "L16")
         gat("v", T.GS[:, 0:512], T.SW[:, 0:3088], T.GL16[:, 0:32], SW + " G16", "GS0")
         gat("a", T.GS[:, 512:1024], T.SW[:, 0:3088], T.GL16[:, 32:64], SW + " G16", "GS1")
         ext("pS", "SELS", T.GS, "GS0 GS1")
@@ -404,7 +447,7 @@ def rank_program(g, core, T, topo):
             own_x("a", X, xk, 1)
             o_q()
         else:
-            own_x("a", X, xk, 1)
+            own_digits("a", 1)
             o_h(), o_q()
             o_ht(), o_ga(), o_tq()
             o_e1(), o_of()
@@ -414,94 +457,94 @@ def rank_program(g, core, T, topo):
             o_of16()
         else:
             o_tq()
-        ties(*p0), ties2(*p0), ties(*p1), ties2(*p1), ties(*p2)
+        ties(0), ties(1)
+        ties(2)
+        diff(0), diff(1)
         if k:
-            ties2(*p2)
-            patch()
-            minus_own()
-        diff(*p0)
-        gat("a", T.XS[:, 0:512], XW, T.S16[:, 32:64], xk + " S16", "XSa")
+            fetch(2)
+        fetch(3)
+        clip(0)
+        votes(0)
         turned("v", 0)
-        cp(T.LO[:, 0:ND], T.pT[:, 15:16 * ND:16], "pT", "LO")
-        clip(*p0)
-        votes(*p0)
-        diff(*p1)
+        clip(1)
         if k:
+            plus(2)
+            votes(1)
+            sign(2)
             turned("a", 1)
-            mm(T.pD[:], T.IDP[:], T.XS[:, 0:512], False, True, "IDP XSa", "pD")
-            for b in (s1 + s2)[:nb]:
-                far(b)
-            act(T.SG[:, 512:1024], T.pD[:], F.Sign, "pD", "SGpC")
-            for b in (s1 + s2)[nb:]:
-                far(b)
+            o_d(), o_s2()
+            asks(0)
+            o_el(), o_e2()
         else:
+            clear_counts(1)
+            votes(1)
             own_digits("a", 1)
-        o_d(), o_s2()
-        asks(*p0)
+            diff(2)
+            asks(0)
+            o_d(), o_s2()
+            clip(2)
         m = 16 * GP
-        mine = [b for b in range(64) if b not in s1 + s2]
         for i, b in enumerate(mine):
-            c, gr, o, bank = where(b)
-            if i == cl:
-                clip(*p1)
-            if i == pb:
-                votes(*p1)
+            c, gr, o, p = where(b)
+            if i == a1:
+                asks(1)
+            if i == p3:
                 if k == 0:
-                    minus_own()
-                    mm(T.pD[:], T.IDP[:], T.XS[:, 0:512], False, True, "IDP XSa", "pD")
-                    act(T.SG[:, 512:1024], T.pD[:], F.Sign, "pD", "SGpC")
+                    minus_own(3)
+                plus(3)
+                sign(3)
+                if k == 0:
                     turned("a", 1)
-                    for b2 in s1 + s2:
-                        far(b2)
-            if i == vb:
-                asks(*p1)
+                else:
+                    clear_counts(1)
+            if i == v2:
+                votes(2)
+            if i == a2:
+                asks(2)
+                for b2 in s1:
+                    far(b2)
                 for b2 in s1:
                     hit(b2)
-            if i == pc:
-                if k == 0:
-                    ties2(*p2)
-                    patch()
-                votes(*p2)
-            if i == vc:
-                asks(*p2)
+                for b2 in s2:
+                    far(b2)
+            if i == t3:
+                ties(3)
+                patch()
+            if i == v3:
+                votes(3)
+            if i == a3:
+                asks(3)
                 for b2 in s2:
                     hit(b2)
-            bb = T.BB[:, W * b:W * b + W]
-            if i < ND:
-                ts(bb, T.IO[:, 0:W], T.LO[:, b:b + 1], A.not_equal, "IO pA LO", "BB%d" % b, T.pA[:, b:b + 1], A.is_lt)
-            else:
-                ts(bb, T.IO[:, 0:W], T.AT[:, o:o + 1], A.is_equal, "IO AK%s AT%d" % (bank, c // 4), "BB%d" % b,
-                   T.AK2[:, b:b + 1], A.mult)
+            ts(T.BB[:, W * b:W * b + W], T.IO[:, 0:W], T.AT[:, o:o + 1], A.is_equal, "IO AK%s AT%d" % (p, c // 4), "BB%d" % b,
+               T.AK2[:, b:b + 1], A.mult)
             count(b)
             for j, his in ((j1, s1), (j2, s2)):
-                if 0 <= i - j < len(his):
-                    count(his[i - j])
+                if i >= j and (i - j) % 2 == 0 and (i - j) // 2 < len(his):
+                    count(his[(i - j) // 2])
         for b in s1 + s2:
             if b not in done:
                 count(b)
-        if k == 0:
-            o_h(), o_of()
-        o_el()
-        if k == 0:
-            o_ga(), o_of16(), o_ht()
-        else:
-            o_e2()
-        ext("pA", "SELM", T.SG, "SGpA SGpB SGpC")
-        if GP < 64:
-            act(T.GN[:, 0:1024 - m], T.GS[:, m:1024], F.Sign, "GS1", "GN")
-            mm(T.pD[:, 0:1024 - m], T.IDP[:], T.GN[:, 0:1024 - m], True, False, "IDP GN", "pD")
+        ext("pB", "SELM", T.SG, "SG0 SG1 SG2 SG3")
+        act(T.GN[:, 0:1024 - m], T.GS[:, m:1024], F.Sign, "GS1", "GN")
         if t == 0:
             act(T.SELF[:], T.SELM[:], F.Copy, "SELM", "SELF", scale=1.0 / 4096)
-        ts(T.RR[0:W, :], T.pH[0:W, 0:128], MAGIC, A.add, "pH", "RR", MAGIC, A.subtract)
-        ts(T.FL1[0:W, :], T.pH[0:W, 0:128], MAGIC, A.add, "pH", "FL1", MAGIC + 2048, A.is_equal)
-        o_bl()
-        tt(T.FL0[0:W, :], T.pH[0:W, 0:128], T.RR[0:W, :], A.is_equal, "pH RR", "FL0")
+        for h, bank in enumerate(HB):
+            P, a = T[bank][0:W, 0:64], 64 * h
+            ts(T.RR[0:W, a:a + 64], P, MAGIC, A.add, bank, "RR%d" % h, MAGIC, A.subtract)
+            ts(T.FL1[0:W, a:a + 64], P, MAGIC, A.add, bank, "+FL1", MAGIC + 2048, A.is_equal)
+            if k == 0:
+                (o_h(), o_of(), o_el()) if h == 0 else (o_ga(), o_of16())
+            elif h == 0:
+                o_bl()
+            tt(T.FL0[0:W, a:a + 64], P, T.RR[0:W, a:a + 64], A.is_equal, bank + " RR%d" % h, "+FL0")
         for f in (1, 0):
             em("p", lambda: g.tensor.transpose(T.pT[:, W * f:W * f + W], T["FL%d" % f][0:W, :], T.IDP[0:W, 0:W]),
                "IDP FL%d" % f, "pT")
+        mm(T.pD[:, 0:1024 - m], T.IDP[:], T.GN[:, 0:1024 - m], True, False, "IDP GN", "pD")
         if k == 0:
-            o_e1(), o_e2()
-        tt(AK, T.pA[:, 0:64], T.D[:], A.is_lt, "pA D pW", "wAK")
+            o_ht(), o_bl(), o_e1(), o_e2()
+        tt(AK, T.pB[:, 0:64], T.D[:], A.is_lt, "pB D pW", "wAK")
         win = T.FT[:, 0:2 * W]
         cp(win, T.pT[:, 0:2 * W], "pT", "FT")
         if not final:
@@ -530,25 +573,28 @@ def rank_program(g, core, T, topo):
             own_x("a", X, xk, 0)
             own_digits("a", 0)
             unsit()
-            own_digits("a", 1)
-            clear_counts()
+            own_x("a", X, xk, 1)
+            clear_counts(0)
+            minus_own(2, 1), minus_own(3, 1)
         if k == 0:
             dma("s", X[:, SELF:SELF + 3072], X[:, 0:3072], xk + " SC16", xk[0:2] + "h")
         em("v", lambda: g.vector.tensor_copy(T.SW[:].indirect(T.SC16[:]), T.GS[:]), "SC16 GS0 GS1", SW)
 
     def pass_on(n):
         yield ts(T.UP[:], LN_, float(ROOT), A.is_equal, "NL", "UP")
-        yield tt(T.PF2[:], T.EF[:], T.NEW[:, 64:192], A.subtract, "EF NG NL", "PF2")
+        yield tt(T.RR[:, 0:64], GN_, LN_, A.max, "NG NL", "RR0")
+        yield tt(T.RR[:, 64:128], GN_, LN_, A.min, "NG NL", "RR1")
+        yield tt(T.PF2[:], T.EF[:], T.RR[:], A.subtract, "EF RR0 RR1", "PF2")
         yield tt(T.P3[:, 0:64], T.PF2[:, 0:64], T.UP[:], A.mult, "PF2 UP", "+P3")
         yield tt(T.P3[:, 64:128], T.PF2[:, 64:128], T.UP[:], A.mult, "PF2 UP", "+P3")
-        yield tt(T.P4[:], T.P3[:], T.NEW[:, 64:192], A.add, "P3 NG NL", "P4")
+        yield tt(T.P4[:], T.P3[:], T.RR[:], A.add, "P3 RR0 RR1", "P4")
         sp = "SP%d" % n
         cp(T[sp][:], T.P4[:], "P4", sp)
         yield send(T["LP%d" % n][:], T[sp][:], "r%d" % n, "s%d" % n, sp)
 
     def round_end(n, X, xk, Y, yk):
         final = n == RO - 1
-        key, xh = "abcdfg", xk + " " + xk[0:2] + "h "
+        key, xh = "abcdfgi", xk + " " + xk[0:2] + "h "
         for a, b, e, bank in SEG:
             if e == "v":
                 act(T.XP[:, a:b], X[:, a:b], F.Identity, xk, "+XP", bias=1.0)
@@ -572,7 +618,7 @@ def rank_program(g, core, T, topo):
             a, b, e, bank = SEG[i]
             if e == "v":
                 tt(T.DD[:, a:b], X[:].indirect(T.SL16[:, a // 16:b // 16]), T.XP[:, a:b], A.min,
-                   xh + "XP " + lk(a, b), "DDpA DDpB DD" + key[i] if a < 1024 else "DD" + key[i])
+                   xh + "XP " + lk(a, b), "DD0 DD1 DD2 DD" + key[i] if a < 1024 else "DD" + key[i])
             else:
                 gat("a", T.XS[:, a:b], X[:], T.SL16[:, a // 16:b // 16], xh + lk(a, b), "XS" + key[i])
 
@@ -598,22 +644,22 @@ def rank_program(g, core, T, topo):
         def go(c):
             for _ in range(c):
                 next(on, None)
-        lists(0), go(2), listed(0), lists(1), fetch(0), go(2), fetch(1), listed(1), minus(0), lists(2), fetch(2), sign(0)
-        go(1), put(1), go(1), listed(2), minus(2), fetch(3), sign(2), fetch(4)
+        lists(0), go(4), listed(0), lists(1), fetch(0), fetch(1), go(4), listed(1), minus(0), lists(2), sign(0)
+        fetch(2), listed(2), minus(1), fetch(3), sign(1), put(2), fetch(4)
         if final:
             ts(T.D2[:], T.D0[:], SELF / 64, A.is_ge, "D0", "D2", -SELF / 64, A.mult)
             for i, (w, d) in enumerate((("ID6", "D0"), ("IDP", "D1"), ("ID6", "D2"))):
                 mm(T.pS[:, 0:192], T[w][:], T[d][:], i == 0, i == 2, w + " " + d, "pS")
-        minus(3), fetch(5), sign(3), minus(5)
+        minus(3), fetch(6), sign(3), minus(6)
         if final:
             act(T.Y3[:], T.pS[:, 0:192], F.Copy, "pS", "Y3")
             dma("a", T.ys[:], T.Y3[:], "Y3", "oy")
-        sign(5)
-        put(0), put(4), put(2), put(3), put(5)
+        sign(6)
+        put(0), fetch(5), put(4), put(1), put(5), put(3), put(6)
 
     X, Y, xk, yk = T.XA, T.XB, "X0", "X1"
     for n in range(RO):
-        xr = " ".join(xk + c for c in "abcdefg")
+        xr = " ".join(xk + c for c in "abcdefgi")
         round_start(n, X, xr)
         for k in range(ST):
             step(n, k, X, xr)

@@ -4,28 +4,27 @@ RO, ST, LB = 3, 4, 10
 TOP, ROOT, SELF, SIT = 3072, 3073, 3136, 8192.0
 MAGIC = 3.0 * 2 ** 33
 W = 120
-CUT = 4
-
-
-def pieces(k):
-    cut = CUT if k else 4
-    return (0, 1, "pA", ""), (1, 2, "pB", ""), (2, cut, "pS", "pC"), (cut, 8, "pA", "pD")
-
-
-GP = 50
+PIECES = ((0, 1, "pA", ""), (1, 2, "pB", ""), (2, 4, "pS", "pC"), (4, 8, "pA", "pD"))
 HB = ("pH", "pC")
+GP = 48
+G2 = 58
+LX = 20
 RV = 24
-RA = 52
 RS = 36
-AT0 = (0, 6, 0, 4, 2, 12, 4, 10, 24, 40, 41)
-ATK = (0, 9, 0, 3, 1, 13, 2, 12, 29, 30, 38)
-RC = 2656
-SEG = ((0, 512, "a", "pA"), (512, 1024, "a", "pB"), (1024, 1536, "v", "pW"), (1536, 2048, "a", "pC"),
-       (2048, 2560, "v", "pH"), (2560, RC, "v", "XM"), (RC, 3072, "a", "pD"))
+RA = 52
+QV = 6
+AT0 = (6, 4, 3, 12, 3, 10, 26, 41)
+ATK = (8, 4, 0, 13, 2, 10, 28, 39)
+RC = 2848
+RF = 2720
+SEGS = (((0, 512, "c", "pA"), (512, 1024, "a", "pB"), (1024, 1536, "v", "pW"), (1536, 2048, "a", "pC"),
+         (2048, 2560, "v", "pH"), (2560, RC, "v", "XM"), (RC, 3072, "a", "pD")),
+        ((0, 512, "a", "pA"), (512, 1024, "v", "pW"), (1024, 1536, "a", "pB"), (1536, 2048, "a", "pC"),
+         (2048, 2560, "v", "pH"), (2560, RF, "v", "XM"), (RF, 3072, "a", "pD")))
 DT = {"b": "bfloat16", "f": "float32", "i": "int32", "u": "uint16"}
 SCRATCH = {}
-for _t in ("b6208 XA XB;b3088 DG;b4112 SW;b1024 GS XL LD SG AT GF;b3072 DD XP XS;b7680 BB BT;b512 GN XM;"
-           "b64 AK2 S2G;b128 IO IDP IDN ID6 NEG FL0 FL1;b256 WR IH IL B2 FT;i128 EI;f128 RR EF PF2 P3 P4;"
+for _t in ("b6208 XA XB;b3088 DG;b4112 SW;b1024 SR GS XL LD SG AT GF;b3072 DD XP XS;b7680 BB BT;b512 GN XM;"
+           "b64 AK2 S2G;b128 IO IDP IDN ID6 NEG FL0 FL1 BD;b256 WR IH IL FT;i128 EI;f128 RR EF PF2 P3 P4;"
            "b2048 SELS SELM SELF;b8 M2 S2L;i1 PI GI QI;f1 GFC QF GC WT;b1 PF N1 N2;b16 EQ EC GQ KB;f16 E4;"
            "i4 BI;f4 BC;i192 UI W1 W2 SI;b192 D0 D1 D2;f192 Y3 NEW BASE DV;u192 SL16;i64 LV Q;"
            "u128 ED EDN LP0 LP1 SP0 SP1 GL16;f256 BW;"
@@ -36,7 +35,7 @@ PS = ("pS", "pA", "pB", "pC", "pD", "pH", "pW", "pT")
 for _n in PS[:-1]:
     SCRATCH[_n] = ("psum", [128, 512], "float32")
 SCRATCH["pT"] = ("psum", [128, 1024], "bfloat16")
-SEMAPHORES = ["cv", "ca", "cp", "cg", "se", "s0", "s1", "re", "r0", "r1"] + ["d%d" % i for i in range(48)]
+SEMAPHORES = ["cv", "ca", "cp", "cg", "se", "s0", "s1", "re", "r0", "r1"] + ["d%d" % i for i in range(64)]
 SW = "SW SW0 SW1"
 
 
@@ -143,10 +142,10 @@ def rank_program(g, core, T, topo):
         else:
             act(out, win.indirect(off), F.Copy, rd, wr)
 
-    def ext(key, sel, src, rd, o=0):
+    def ext(key, sel, src, rd, o=0, n=64):
         for q in range(16):
-            mm(T[key][:, 0:64], T[sel][:, q * 128:(q + 1) * 128], src[:, 16 * o + q:16 * (o + 64):16], q == 0, q == 15,
-               rd + " " + sel, key)
+            mm(T[key][:, 0:n], T[sel][:, q * 128:(q + 1) * 128], src[:, 16 * o + q:16 * (o + n):16], q == 0, q == 15,
+               rd + " SELG " + sel, key)
 
     def iota(nm, pat, cm, a=0, b=None):
         kw = {} if SCRATCH[nm][2] == "int32" else {"allow_small_or_imprecise_dtypes": True}
@@ -162,9 +161,10 @@ def rank_program(g, core, T, topo):
 
     iota("PI", [[1, 1]], 1)
     iota("IO", [[1, 128]], 0)
-    iota("UI", [[1, 192]], 192)
     iota("IH", [[1, 4], [0, 64]], 0)
     iota("IL", [[0, 4], [1, 64]], 0)
+    iota("BD", [[16, 8], [0, 16]], 0)
+    iota("UI", [[1, 192]], 192)
     for b in "AB":
         ms(T["X" + b][:, 3072:SELF], -1.0, "X%de" % (b == "B"))
     ms(T.SW[:, 3072:3088], 0.0, "SW")
@@ -177,33 +177,30 @@ def rank_program(g, core, T, topo):
         ms(T["X" + b][:, TOP:TOP + 1], 256.0, "X%de" % (b == "B"))
     cp(T.QF[:], T.QI[:], "QI", "QF")
     cp(T.GFC[:], T.GI[:], "GI", "GFC")
-    for nm, sc in (("IDN", -1.0), ("IDP", 1.0), ("ID6", 64.0)):
-        ts(T[nm][:], T.IO[:], T.PF[:], A.is_equal, "IO PF", nm, sc, A.mult)
     ts(T.EQ[:], T.IO[:, 0:16], T.QF[:], A.is_equal, "IO QF", "EQ")
+    for nm, sc in (("IDN", -1.0), ("IDP", 1.0)):
+        ts(T[nm][:], T.IO[:], T.PF[:], A.is_equal, "IO PF", nm, sc, A.mult)
     ts(T.GQ[:], T.IO[:, 0:16], T.GFC[:], A.add, "IO GFC", "GQ")
     ts(T.GC[:], T.GFC[:], -192.0, A.mult, "GFC", "GC")
-    for u in range(4):
-        ts(T.BI[:, u:u + 1], T.QI[:], u, A.arith_shift_right, "QI", "+BI", 1, A.bitwise_and)
     ts(T.N1[:], T.EQ[:, 15:16], -1.0, A.mult, "EQ", "N1", 1.0, A.add)
     ts(T.N2[:], T.EQ[:, 15:16], -2048.0, A.mult, "EQ", "N2", 2048.0, A.add)
     ts(T.EC[:], T.EQ[:], T.EQ[:, 15:16], A.max, "EQ", "EC")
     ts(T.KB[:], T.IO[:, 0:16], T.EQ[:, 0:1], A.mult, "IO EQ", "KB", 4.0, A.mult)
-    ts(T.pW[:, 0:192], T.UI[:], T.GC[:], A.add, "UI GC pW", "wT")
     ts(T.WR[:, 0:W], T.IO[:, 0:W], T.EQ[:, 15:16], A.mult, "IO EQ N1", "WR", T.N1[:], A.add)
     ts(T.WR[:, W:2 * W], T.IO[:, 0:W], T.EQ[:, 15:16], A.mult, "IO EQ N2", "+WR", T.N2[:], A.add)
     ts(T.E4[:], T.EQ[:], 1.0 / 4096, A.mult, "EQ", "E4")
-    ts(T.BC[:], T.BI[:], SIT, A.mult, "BI", "BC")
-    ts(T.B2[:], T.IH[:], T.EQ[:, 0:1], A.mult, "IH EQ", "B2")
+    for r, src in enumerate(("IH", "IL")):
+        ts(T["FL%d" % r][:], T.IDP[:], T.EQ[:, r:r + 1], A.mult, "IDP EQ", "FL%d" % r)
+        mm(T.pA[:, 0:256], T["FL%d" % r][:], T[src][:], r == 0, r == 1, "FL%d %s" % (r, src), "pA")
+    for k in range(13):
+        w = 256 if k < 12 else 16
+        act(T.DG[:, 256 * k:256 * k + w], T.pA[:, 0:w], F.Identity, "pA KB", "+DG", bias=T.KB[:, k:k + 1])
     for k in range(13):
         a, w = 2 * W * k, min(2 * W, 3072 - 2 * W * k)
         ts(T.SW[:, a:a + w], T.WR[:, 0:w], T.EC[:, k + 2:k + 3], A.mult, "WR EC", "+SW0 +SW1")
-        if k == 3:
-            ts(T.pW[:, 256:512], T.IL[:], T.EQ[:, 1:2], A.mult, "IL EQ pW", "wAK wH wGA wTQ wS")
         if k == 5:
-            tt(T.B2[:], T.pW[:, 256:512], T.B2[:], A.add, "B2 wAK pW", "B2")
-    for k in range(13):
-        w = 256 if k < 12 else 16
-        act(T.DG[:, 256 * k:256 * k + w], T.B2[:, 0:w], F.Identity, "B2 KB", "+DG", bias=T.KB[:, k:k + 1])
+            ts(T.BD[:], T.BD[:], T.GFC[:], A.is_equal, "BD GFC", "BD", 4096.0, A.mult)
+    ts(T.pW[:, 0:192], T.UI[:], T.GC[:], A.add, "UI GC pW", "wT")
     ts(T.WT[:], T.E4[:, 0:1], 64.0, A.mult, "E4", "WT", T.E4[:, 1:2], A.add)
     tt(T.P3[:, 0:64], T.EI[:, 0:64], T.EI[:, 64:128], A.max, "EIa EIb", "+P3")
     tt(T.P3[:, 64:128], T.EI[:, 0:64], T.EI[:, 64:128], A.min, "EIa EIb", "+P3")
@@ -216,12 +213,15 @@ def rank_program(g, core, T, topo):
     tt(T.D0[:], T.pW[:, 192:384], T.W1[:], A.add, "W1 wAK pW", "D0")
     dma("s", T.SW[0:128:16, 0:3072], T.D0[:], "D0", "SW0")
     cp(T.ED[:], T.P3[:], "P3", "ED")
-    send(T.EDN[:], T.ED[:], "re", "se", "ED")
+    for q in range(16):
+        sel = T.SELM[:, q * 128:(q + 1) * 128]
+        if q < QV:
+            ts(sel, T.IO[:], T.GQ[:, q:q + 1], A.is_equal, "IO GQ", "+SELM", 4096.0, A.mult)
+        else:
+            em("g", lambda: g.affine_select(sel, T.BD[:], [[0, 8], [1, 16]], A.is_equal, 0.0, -q, 0), "BD", "+SELG")
     iota("LV", [[16, 64]], 0)
     for i, b in enumerate((1, 2, 3, 5)):
         iota("BW", [[0, 32 >> b], [int(SIT), 2], [0, 1 << b]], 0, 64 * i, 64 * i + 64)
-    for q in range(16):
-        ts(T.SELM[:, q * 128:(q + 1) * 128], T.IO[:], T.GQ[:, q:q + 1], A.is_equal, "IO GQ", "+SELM", 4096.0, A.mult)
 
     def more_constants():
         sel = T.SELM[:, 0:128:16]
@@ -232,18 +232,19 @@ def rank_program(g, core, T, topo):
         ts(T.S2G[:, 0:8], sel, T.WT[:], A.mult, "SELM WT", "S2G", 2.0 ** -17, A.mult)
         ts(T.BASE[:, 0:64], T.LV[:], T.QF[:], A.add, "LV QF", "TR", 3088.0, A.add)
 
-    def turned(e, h):
-        o, i = T.AT[:, 512 * h:512 * h + 512], T.pT[:, 512 * h:512 * h + 512]
-        if e == "v":
-            cp(o, i, "pT", "AT%d" % h)
-        else:
-            act(o, i, F.Copy, "pT", "AT%d" % h)
+    def at(c):
+        return ("AT0", "AT2", "AT1", "AT1")[c // 2]
 
     def own_x(e, X, xk, h):
         gat(e, T.XL[:, 512 * h:512 * h + 512], X[:, 0:3088], T.GL16[:, 64 + 32 * h:96 + 32 * h], xk + " L16", "XL%d" % h)
 
-    def own_digits(e, h):
-        gat(e, T.LD[:, 512 * h:512 * h + 512], T.DG[:], T.GL16[:, 64 + 32 * h:96 + 32 * h], "DG L16", "LD%d" % h)
+    def own_digits(e, h, a=0, b=32):
+        a, b = 32 * h + a, 32 * h + b
+        gat(e, T.LD[:, 16 * a:16 * b], T.DG[:], T.GL16[:, 64 + a:64 + b], "DG L16", "LD2" if e == "v" else "+LD%d" % h)
+
+    def minus_own(p):
+        a, b, bank, db = PIECES[p]
+        mm(T[db][:, 0:128 * (b - a)], T.IDN[:], T.XL[:, 128 * a:128 * b], True, False, "IDN XL0 XL1", db)
 
     def clear_counts(h):
         mm(T[HB[h]][:, 0:64], T.IDP[:], T.NEG[:, 0:64], True, False, "IDP NEG", HB[h])
@@ -257,7 +258,7 @@ def rank_program(g, core, T, topo):
         else:
             lst, lk = T["LP%d" % (n - 1)], "LP%d" % (n - 1)
             landed("r%d" % (n - 1), lk)
-        m, w, X = 16 * RS, 1024 - 16 * RS, X[:, 0:3088]
+        m, X = 16 * RS, X[:, 0:3088]
         rd = xk + " " + lk
         vs, ss = ((0, RV, "0"), (RV, RS, "1 2")), ((RS, RA, "pC", "a"), (RA, 64, "pD", "b"))
         gat("a", T.XL[:, m:1024], X, lst[:, 64 + RS:128], rd, "XL1")
@@ -281,8 +282,10 @@ def rank_program(g, core, T, topo):
         tt(T.D[:], T.PF2[:, 0:64], T.PF2[:, 64:128], A.add, "PF2", "D")
         clear_counts(0)
         if n == 0:
-            act(T.SELS[:], T.SELM[:], F.Identity, "SELM WT", "SELS", scale=T.WT[:])
+            act(T.SELS[:], T.SELM[:], F.Identity, "SELM SELG WT", "SELS", scale=T.WT[:])
             more_constants()
+            before("g", ["SG3"], [])
+            send(T.EDN[:], T.ED[:], "re", "se", "ED")
         if n < 2:
             if n == 1:
                 landed("re", "EDN")
@@ -297,16 +300,9 @@ def rank_program(g, core, T, topo):
         t = ST * n + k
         last = k == ST - 1
         final = last and n == RO - 1
-        n1, n2, p3, a1, v2, a2, t3, v3, a3, j1, j2 = AT0 if k == 0 else ATK
-        PIECES = pieces(k)
-        cut = 8 * PIECES[3][0]
-        s1, s2 = list(range(cut - n1, cut)), [b for b in range(cut, 64) if b % 8 >= 4][:n2]
-
-        def minus_own(p, k=0):
-            a, b, bank, db = pieces(k)[p]
-            mm(T[db][:, 0:128 * (b - a)], T.IDN[:], T.XL[:, 128 * a:128 * b], True, False, "IDN XL0 XL1", db)
-
-        mine = sorted((b for b in range(64) if b not in s1 + s2), key=lambda b: (b >= 48 and b % 8 >= 4, b))
+        ns, a1, v2, a2, t3, v3, a3, js = AT0 if k == 0 else ATK
+        his = [b for b in range(32, 64) if b % 8 >= 4][:ns]
+        mine = sorted((b for b in range(64) if b not in his), key=lambda b: (b >= 48 and b % 8 >= 4, b))
         XW = X[:, 0:3088]
 
         def ties(p):
@@ -314,15 +310,15 @@ def rank_program(g, core, T, topo):
             for c in range(a, b):
                 w = 8 * (b - a) if c == a else 8
                 mm(T[bank][:, 8 * (c - a):8 * (c - a) + w], T.GS[:, 128 * c:128 * c + 128], T.S2G[:, 0:w], c == a, False,
-                   "GS%d S2G" % (c // 4), bank)
+                   "GS%d S2G" % (c // 2), bank)
             for c in range(a, b):
                 mm(T[bank][:, 8 * (c - a):8 * (c - a) + 8], T.LD[:, 128 * c:128 * c + 128], T.S2L[:], False, False,
-                   "LD%d S2L" % (c // 4), bank)
+                   "S2L " + ("LD0", "LD1 LD2")[c // 4], bank)
 
         def diff(p):
             a, b = PIECES[p][0:2]
             tt(T.DD[:, 128 * a:128 * b], XW.indirect(T.S16[:, 8 * a:8 * b]), T.XL[:, 128 * a:128 * b], A.subtract,
-               xk + " XL0 S16", "DD%d" % p)
+               xk + " S160 XL%d" % (p // 2 * 2), "DD%d" % p)
 
         def clip(p):
             a, b = PIECES[p][0:2]
@@ -330,7 +326,7 @@ def rank_program(g, core, T, topo):
 
         def fetch(p):
             a, b = PIECES[p][0:2]
-            gat("a", T.XS[:, 128 * a:128 * b], XW, T.S16[:, 8 * a:8 * b], xk + " S16", "XS" + "ab"[p - 2])
+            gat("a", T.XS[:, 128 * a:128 * b], XW, T.S16[:, 8 * a:8 * b], xk + " S16%d" % (p - 2), "XS" + "ab"[p - 2])
 
         def plus(p):
             a, b, bank, db = PIECES[p]
@@ -352,7 +348,7 @@ def rank_program(g, core, T, topo):
 
         def patch():
             for r in (0, 1):
-                dma("s", T.GS[r:128:16, :], T.LD[r:128:16, :], "LD0 LD1", "+GS0 +GS1")
+                dma("s", T.SR[r:128:16, :], T.LD[r:128:16, :], "LD0 LD1 LD2 SR", "SR%d" % r)
 
         def o_h():
             tt(H, GN_, T.K[:], A.min, "NG K pW", "wH")
@@ -389,7 +385,7 @@ def rank_program(g, core, T, topo):
                 tt(T.E1[:], LN_, ga, A.subtract, "NL pW " + gk, "E1")
 
         def o_s():
-            ts(S, T.pS[:, 0:64], float(ROOT), A.min, "pS pW", "wS")
+            cp(S, T.S16[:], "S160 S161 pW", "wS")
 
         def o_d():
             tt(T.D[:], S, LN_, A.subtract, "wS NL pW", "D")
@@ -416,7 +412,7 @@ def rank_program(g, core, T, topo):
 
         def far(b):
             c, gr, o, bank = where(b)
-            act(T.BT[:, W * b:W * b + W], T.IO[:, 0:W], F.Abs, "IO AT%d" % (c // 4), "BT%d" % b,
+            act(T.BT[:, W * b:W * b + W], T.IO[:, 0:W], F.Abs, "IO " + at(c), "BT%d" % b,
                 bias=T.AT[:, o:o + 1], scale=-1.0)
 
         def hit(b):
@@ -430,83 +426,87 @@ def rank_program(g, core, T, topo):
             done.append(b)
             bank, a = HB[gr // 4], 16 * (gr % 4)
             mm(T[bank][0:W, a + 2:a + 15], T.BB[:, W * b:W * b + W], T.AT[:, o - 13:o], False,
-               sum(d % 8 // 4 == gr // 4 for d in done) == 32, "BB%d AT%d" % (b, c // 4), bank)
+               sum(d % 8 // 4 == gr // 4 for d in done) == 32, "BB%d %s" % (b, at(c)), bank)
 
         if k == 0:
-            cp(T.GL16[:, 64:128], LN_, "NL", "L16")
-        gat("v", T.GS[:, 0:512], T.SW[:, 0:3088], T.GL16[:, 0:32], SW + " G16", "GS0")
-        gat("a", T.GS[:, 512:1024], T.SW[:, 0:3088], T.GL16[:, 32:64], SW + " G16", "GS1")
-        ext("pS", "SELS", T.GS, "GS0 GS1")
+            o_q()
+        for i in range(4):
+            gat("va"[i % 2], T.GS[:, 256 * i:256 * i + 256], T.SW[:, 0:3088], T.GL16[:, 16 * i:16 * i + 16], SW + " G16", "GS%d" % i)
+            if k == 0 and i == 0:
+                cp(T.GL16[:, 64:128], LN_, "NL", "L16")
+        dma("s", T.SR[:], T.GS[:], "GS0 GS1 GS2 GS3", "SR SR0 SR1")
+        ext("pS", "SELS", T.GS, "GS0 GS1", 0, 32)
+        ext("pB", "SELS", T.GS, "GS2 GS3", 32, 32)
+
+        def listed(h):
+            ts(T.S16[:, 32 * h:32 * h + 32], T["pB" if h else "pS"][:, 0:32], float(ROOT), A.min, "pB" if h else "pS", "S16%d" % h)
         for c in range(8):
             em("p", lambda: g.tensor.transpose(T.pT[:, 128 * c:128 * c + 128], T.GS[:, 128 * c:128 * c + 128], T.IDP[:]),
-               "IDP GS%d" % (c // 4), "pT")
+               "IDP GS%d" % (c // 2), "pT")
         if k == 0:
-            own_x("v", X, xk, 0)
+            gat("v", T.XL[:, 0:256], XW, T.GL16[:, 64:80], xk + " L16", "XL0")
+            cp(H, GN_, "NG pW", "wH")
+            o_tq()
             own_digits("a", 0)
             unsit()
             own_x("a", X, xk, 1)
+        else:
+            own_digits("v", 1, LX)
+            own_digits("a", 1, 0, LX)
             o_q()
-        else:
-            own_digits("a", 1)
-            o_h(), o_q()
-            o_ht(), o_ga(), o_tq()
-            o_e1(), o_of()
-        ts(T.S16[:], T.pS[:, 0:64], float(ROOT), A.min, "pS", "S16")
-        o_s()
+        listed(0)
         if k:
-            o_of16()
+            o_h(), o_tq()
         else:
-            o_tq()
-        ties(0), ties(1)
-        ties(2)
-        diff(0), diff(1)
+            gat("v", T.XL[:, 256:512], XW, T.GL16[:, 80:96], xk + " L16", "XL2")
+        ties(0)
+        diff(0)
         if k:
             fetch(2)
+        listed(1)
         fetch(3)
+        if k:
+            o_of()
         clip(0)
+        diff(1)
         votes(0)
-        turned("v", 0)
-        clip(1)
         if k:
             plus(2)
-            votes(1)
+        ties(1), ties(2)
+        cp(T.AT[:, 0:256], T.pT[:, 0:256], "pT", "AT0")
+        clip(1)
+        votes(1)
+        asks(0)
+        cp(T.AT[:, 256:512], T.pT[:, 256:512], "pT", "AT2")
+        if k:
             sign(2)
-            turned("a", 1)
-            o_d(), o_s2()
-            asks(0)
-            o_el(), o_e2()
+            act(T.AT[:, 512:1024], T.pT[:, 512:1024], F.Copy, "pT", "AT1")
+            o_s()
+            plus(3)
+            sign(3)
         else:
             clear_counts(1)
-            votes(1)
             own_digits("a", 1)
             diff(2)
-            asks(0)
-            o_d(), o_s2()
-            clip(2)
+            minus_own(3)
+            plus(3)
+            sign(3)
+            act(T.AT[:, 512:1024], T.pT[:, 512:1024], F.Copy, "pT", "AT1")
+        for b in his:
+            far(b)
         m = 16 * GP
         for i, b in enumerate(mine):
             c, gr, o, p = where(b)
             if i == a1:
                 asks(1)
-            if i == p3:
-                if k == 0:
-                    minus_own(3)
-                plus(3)
-                sign(3)
-                if k == 0:
-                    turned("a", 1)
-                else:
-                    clear_counts(1)
             if i == v2:
+                if k == 0:
+                    clip(2)
                 votes(2)
+                if k:
+                    clear_counts(1)
             if i == a2:
                 asks(2)
-                for b2 in s1:
-                    far(b2)
-                for b2 in s1:
-                    hit(b2)
-                for b2 in s2:
-                    far(b2)
             if i == t3:
                 ties(3)
                 patch()
@@ -514,48 +514,60 @@ def rank_program(g, core, T, topo):
                 votes(3)
             if i == a3:
                 asks(3)
-                for b2 in s2:
+                for b2 in his:
                     hit(b2)
-            ts(T.BB[:, W * b:W * b + W], T.IO[:, 0:W], T.AT[:, o:o + 1], A.is_equal, "IO AK%s AT%d" % (p, c // 4), "BB%d" % b,
-               T.AK2[:, b:b + 1], A.mult)
+            ts(T.BB[:, W * b:W * b + W], T.IO[:, 0:W], T.AT[:, o:o + 1], A.is_equal, "IO AK%s %s" % (p, at(c)),
+               "BB%d" % b, T.AK2[:, b:b + 1], A.mult)
             count(b)
-            for j, his in ((j1, s1), (j2, s2)):
-                if i >= j and (i - j) % 2 == 0 and (i - j) // 2 < len(his):
-                    count(his[(i - j) // 2])
-        for b in s1 + s2:
-            if b not in done:
-                count(b)
-        ext("pB", "SELM", T.SG, "SG0 SG1 SG2 SG3")
-        act(T.GN[:, 0:1024 - m], T.GS[:, m:1024], F.Sign, "GS1", "GN")
+            if i >= js and (i - js) % 2 == 0 and (i - js) // 2 < ns:
+                count(his[(i - js) // 2])
+        if k == 0:
+            o_s()
         if t == 0:
+            for u in range(4):
+                ts(T.BI[:, u:u + 1], T.QI[:], u, A.arith_shift_right, "QI", "+BI", 1, A.bitwise_and)
             act(T.SELF[:], T.SELM[:], F.Copy, "SELM", "SELF", scale=1.0 / 4096)
+        act(T.GN[:, 0:1024 - m], T.GS[:, m:1024], F.Sign, "GS2 GS3", "GN")
         for h, bank in enumerate(HB):
             P, a = T[bank][0:W, 0:64], 64 * h
             ts(T.RR[0:W, a:a + 64], P, MAGIC, A.add, bank, "RR%d" % h, MAGIC, A.subtract)
             ts(T.FL1[0:W, a:a + 64], P, MAGIC, A.add, bank, "+FL1", MAGIC + 2048, A.is_equal)
-            if k == 0:
-                (o_h(), o_of(), o_el()) if h == 0 else (o_ga(), o_of16())
-            elif h == 0:
-                o_bl()
+            if h:
+                o_d()
+            elif k:
+                o_of16()
+            else:
+                o_of()
             tt(T.FL0[0:W, a:a + 64], P, T.RR[0:W, a:a + 64], A.is_equal, bank + " RR%d" % h, "+FL0")
-        for f in (1, 0):
-            em("p", lambda: g.tensor.transpose(T.pT[:, W * f:W * f + W], T["FL%d" % f][0:W, :], T.IDP[0:W, 0:W]),
-               "IDP FL%d" % f, "pT")
-        mm(T.pD[:, 0:1024 - m], T.IDP[:], T.GN[:, 0:1024 - m], True, False, "IDP GN", "pD")
+        mm(T.pS[:, 0:W], T.FL1[0:W, :], T.IDP[0:W, 0:W], True, True, "IDP FL1", "pS")
+        act(T.FT[:, W:2 * W], T.pS[:, 0:W], F.Copy, "pS", "FT1")
+        em("p", lambda: g.tensor.transpose(T.pT[:, 0:W], T.FL0[0:W, :], T.IDP[0:W, 0:W]), "IDP FL0", "pT")
+        fl = ((GP, G2, "pD", "XSb"), (G2, 64, "pA", "XSj"))
+        for a, b, bank, key in fl:
+            mm(T[bank][:, 0:16 * (b - a)], T.IDP[:], T.GN[:, 16 * a - m:16 * b - m], True, False, "IDP GN", bank)
+        ext("pB", "SELM", T.SG, "SG0 SG1 SG2 SG3")
         if k == 0:
-            o_ht(), o_bl(), o_e1(), o_e2()
-        tt(AK, T.pB[:, 0:64], T.D[:], A.is_lt, "pB D pW", "wAK")
+            o_of16()
+        if t == 0:
+            ts(T.BC[:], T.BI[:], SIT, A.mult, "BI", "BC")
+        o_s2(), o_ht(), o_el(), o_ga()
         win = T.FT[:, 0:2 * W]
-        cp(win, T.pT[:, 0:2 * W], "pT", "FT")
+        cp(T.FT[:, 0:W], T.pT[:, 0:W], "pT", "FT")
+        o_bl(), o_e2()
+        tt(T.GF[:, 0:m], win.indirect(T.OF16[:, 0:GP]), T.GS[:, 0:m], A.min, "FT FT1 OF16 GS0 GS1 GS2 GS3", "GF0")
+        for a, b, bank, key in fl:
+            gat("a", T.XS[:, 16 * a:16 * b], win, T.OF16[:, a:b], "FT FT1 OF16", key)
+            mm(T[bank][:, 0:16 * (b - a)], T.IDP[:], T.XS[:, 16 * a:16 * b], False, True, "IDP " + key, bank)
+        for a, b, bank, key in fl:
+            act(T.GF[:, 16 * a:16 * b], T[bank][:, 0:16 * (b - a)], F.Relu, bank, "+GF1", bias=-1.0)
+        ext("pS", "SELF", T.GF, "GF0 GF1")
+        tt(AK, T.pB[:, 0:64], T.D[:], A.is_lt, "pB D pW", "wAK")
+        o_e1()
+        if t == 0:
+            ts(T.ID6[:], T.IO[:], T.PF[:], A.is_equal, "IO PF", "ID6", 64.0, A.mult)
         if not final:
             tt(TQ, AK, T.E2[:], A.mult, "wAK E2 pW", "wTQ")
         tt(T.DV[:, 0:64], AK, T.HT[:], A.mult, "wAK HT pW", "+DV")
-        tt(T.GF[:, 0:m], win.indirect(T.OF16[:, 0:GP]), T.GS[:, 0:m], A.min, "FT OF16 GS0 GS1", "GF0")
-        if GP < 64:
-            gat("a", T.XS[:, 512:1536 - m], win, T.OF16[:, GP:64], "FT OF16", "XSb")
-            mm(T.pD[:, 0:1024 - m], T.IDP[:], T.XS[:, 512:1536 - m], False, True, "IDP XSb", "pD")
-            act(T.GF[:, m:1024], T.pD[:, 0:1024 - m], F.Relu, "pD", "GF1", bias=-1.0)
-        ext("pS", "SELF", T.GF, "GF0 GF1")
         if not final:
             tt(T.DV[:, 64:128], AK, T.E1[:], A.mult, "wAK E1 pW", "+DV")
             tt(T.DV[:, 128:192], AK, T.D[:], A.mult, "wAK D pW", "+DV")
@@ -575,10 +587,10 @@ def rank_program(g, core, T, topo):
             unsit()
             own_x("a", X, xk, 1)
             clear_counts(0)
-            minus_own(2, 1), minus_own(3, 1)
+            minus_own(2), minus_own(3)
         if k == 0:
             dma("s", X[:, SELF:SELF + 3072], X[:, 0:3072], xk + " SC16", xk[0:2] + "h")
-        em("v", lambda: g.vector.tensor_copy(T.SW[:].indirect(T.SC16[:]), T.GS[:]), "SC16 GS0 GS1", SW)
+        em("v", lambda: g.vector.tensor_copy(T.SW[:].indirect(T.SC16[:]), T.SR[:]), "SC16 SR SR0 SR1", SW)
 
     def pass_on(n):
         yield ts(T.UP[:], LN_, float(ROOT), A.is_equal, "NL", "UP")
@@ -594,22 +606,27 @@ def rank_program(g, core, T, topo):
 
     def round_end(n, X, xk, Y, yk):
         final = n == RO - 1
-        key, xh = "abcdfgi", xk + " " + xk[0:2] + "h "
-        for a, b, e, bank in SEG:
+        key, xh, SEG = "abcdfgi", xk + " " + xk[0:2] + "h ", SEGS[final]
+
+        def ahead(i):
+            a, b, e, bank = SEG[i]
             if e == "v":
                 act(T.XP[:, a:b], X[:, a:b], F.Identity, xk, "+XP", bias=1.0)
                 act(T[bank][:, 0:b - a], X[:, a:b], F.Identity, xk, bank, bias=-1.0)
             else:
                 mm(T[bank][:, 0:b - a], T.IDN[:], X[:, a:b], True, False, "IDN " + xk, bank)
+        for i in range(6):
+            ahead(i)
         if final:
             dma("s", T.D0[:], T.SW[0:128:16, 0:3072], SW, "D0")
             dma("s", T.D1[:], T.SW[1:128:16, 0:3072], SW, "D1")
 
         def lists(c):
-            ext("pS", "SELS", T.SW, SW, 64 * c)
+            ext(("pS", "pD")[c % 2], "SELS", T.SW, SW, 64 * c)
 
         def listed(c):
-            cp(T.SL16[:, 64 * c:64 * c + 64], T.pS[:, 0:64], "pS", "SL%d" % c)
+            bank = ("pS", "pD")[c % 2]
+            cp(T.SL16[:, 64 * c:64 * c + 64], T[bank][:, 0:64], bank, "SL%d" % c)
 
         def lk(a, b):
             return " ".join("SL%d" % c for c in range(a // 1024, (b - 1) // 1024 + 1))
@@ -628,34 +645,45 @@ def rank_program(g, core, T, topo):
 
         def sign(i):
             a, b, e, bank = SEG[i]
-            act(T[bank][:, 0:b - a], T[bank][:, 0:b - a], F.Sign, bank, bank)
+            if e == "a":
+                act(T[bank][:, 0:b - a], T[bank][:, 0:b - a], F.Sign, bank, bank)
+            else:
+                act(T.GN[:, 0:b - a], T[bank][:, 0:b - a], F.Sign, bank, "GN")
+                mm(T[bank][:, 0:b - a], T.IDP[:], X[:, a:b], True, False, "IDP " + xk, bank)
+                mm(T[bank][:, 0:b - a], T.IDP[:], T.GN[:, 0:b - a], False, True, "IDP GN", bank)
 
         def put(i):
             a, b, e, bank = SEG[i]
-            if e == "v":
+            if e == "c":
+                act(Y[:, a:b], T[bank][:, 0:b - a], F.Copy, bank, yk + key[i])
+            elif e == "v":
                 tt(Y[:, a:b], T[bank][:, 0:b - a], T.DD[:, a:b], A.max, bank + " DD" + key[i], yk + key[i])
             else:
                 tt(Y[:, a:b], T[bank][:, 0:b - a], X[:, a:b], A.add, bank + " " + xk, yk + key[i])
             if final:
                 dma("s", T.yx[:, a:b], Y[:, a:b], yk + key[i], "ox" + key[i])
 
-        on = iter(()) if final else pass_on(n)
+        if final:
+            lists(0), lists(1), listed(0), lists(2), listed(1), ahead(6), fetch(0), fetch(1), listed(2), minus(0), fetch(2)
+            sign(0), fetch(4), put(1), minus(2), fetch(3), sign(2), put(0)
+            ts(T.D2[:], T.D0[:], SELF / 64, A.is_ge, "D0", "D2", -SELF / 64, A.mult)
+            minus(3), fetch(6), sign(3)
+            for i, (w, d) in enumerate((("ID6", "D0"), ("IDP", "D1"), ("ID6", "D2"))):
+                mm(T.pS[:, 0:192], T[w][:], T[d][:], i == 0, i == 2, w + " " + d, "pS")
+            minus(6), sign(6), put(4), fetch(5)
+            cp(T.Y3[:], T.pS[:, 0:192], "pS", "Y3")
+            dma("s", T.ys[:], T.Y3[:], "Y3", "oy")
+            put(2), put(3), put(6), put(5)
+            return
+        on = pass_on(n)
 
         def go(c):
             for _ in range(c):
-                next(on, None)
-        lists(0), go(4), listed(0), lists(1), fetch(0), fetch(1), go(4), listed(1), minus(0), lists(2), sign(0)
-        fetch(2), listed(2), minus(1), fetch(3), sign(1), put(2), fetch(4)
-        if final:
-            ts(T.D2[:], T.D0[:], SELF / 64, A.is_ge, "D0", "D2", -SELF / 64, A.mult)
-            for i, (w, d) in enumerate((("ID6", "D0"), ("IDP", "D1"), ("ID6", "D2"))):
-                mm(T.pS[:, 0:192], T[w][:], T[d][:], i == 0, i == 2, w + " " + d, "pS")
-        minus(3), fetch(6), sign(3), minus(6)
-        if final:
-            act(T.Y3[:], T.pS[:, 0:192], F.Copy, "pS", "Y3")
-            dma("a", T.ys[:], T.Y3[:], "Y3", "oy")
-        sign(6)
-        put(0), fetch(5), put(4), put(1), put(5), put(3), put(6)
+                next(on)
+        lists(0), lists(1), go(4), listed(0), lists(2), fetch(0), fetch(1), go(2), listed(1), ahead(6), go(1), fetch(2), go(1)
+        listed(2), minus(0), minus(1), sign(0)
+        fetch(3), sign(1), put(2), fetch(4), minus(3), fetch(6), sign(3), minus(6), put(0), sign(6)
+        fetch(5), put(4), put(1), put(5), put(3), put(6)
 
     X, Y, xk, yk = T.XA, T.XB, "X0", "X1"
     for n in range(RO):

from concourse.mybir import AluOpType as A, ActivationFunctionType as F

RO, ST, LB = 3, 4, 10
TOP, ROOT, SELF, SIT = 3072, 3073, 3136, 8192.0
MAGIC = 3.0 * 2 ** 33
W = 120
PIECES = ((0, 1, "pA", ""), (1, 2, "pB", ""), (2, 4, "pS", "pC"), (4, 8, "pA", "pD"))
HB = ("pH", "pC")
GP = 48
G2 = 58
LX = 20
RV = 24
RS = 36
RA = 52
QV = 6
AT0 = (6, 4, 3, 12, 3, 10, 26, 41)
ATK = (8, 4, 0, 13, 2, 10, 28, 39)
RC = 2848
RF = 2720
SEGS = (((0, 512, "c", "pA"), (512, 1024, "a", "pB"), (1024, 1536, "v", "pW"), (1536, 2048, "a", "pC"),
         (2048, 2560, "v", "pH"), (2560, RC, "v", "XM"), (RC, 3072, "a", "pD")),
        ((0, 512, "a", "pA"), (512, 1024, "v", "pW"), (1024, 1536, "a", "pB"), (1536, 2048, "a", "pC"),
         (2048, 2560, "v", "pH"), (2560, RF, "v", "XM"), (RF, 3072, "a", "pD")))
DT = {"b": "bfloat16", "f": "float32", "i": "int32", "u": "uint16"}
SCRATCH = {}
for _t in ("b6208 XA XB;b3088 DG;b4112 SW;b1024 SR GS XL LD SG AT GF;b3072 DD XP XS;b7680 BB BT;b512 GN XM;"
           "b64 AK2 S2G;b128 IO IDP IDN ID6 NEG FL0 FL1 BD;b256 WR IH IL FT;i128 EI;f128 RR EF PF2 P3 P4;"
           "b2048 SELS SELM SELF;b8 M2 S2L;i1 PI GI QI;f1 GFC QF GC WT;b1 PF N1 N2;b16 EQ EC GQ KB;f16 E4;"
           "i4 BI;f4 BC;i192 UI W1 W2 SI;b192 D0 D1 D2;f192 Y3 NEW BASE DV;u192 SL16;i64 LV Q;"
           "u128 ED EDN LP0 LP1 SP0 SP1 GL16;f256 BW;"
           "f64 D K HT E1 E2 S2 UP OF;u64 S16 OF16 SC16").split(";"):
    for _n in _t.split()[1:]:
        SCRATCH[_n] = ("sbuf", [128, int(_t.split()[0][1:])], DT[_t[0]])
PS = ("pS", "pA", "pB", "pC", "pD", "pH", "pW", "pT")
for _n in PS[:-1]:
    SCRATCH[_n] = ("psum", [128, 512], "float32")
SCRATCH["pT"] = ("psum", [128, 1024], "bfloat16")
SEMAPHORES = ["cv", "ca", "cp", "cg", "se", "s0", "s1", "re", "r0", "r1"] + ["d%d" % i for i in range(64)]
SW = "SW SW0 SW1"


def rank_program(g, core, T, topo):
    rank = T.rank_of(core)
    if rank is None:
        return
    N = len(T.cores)
    nxt, prv = T.cores[(rank + 1) % N], T.cores[(rank - 1) % N]
    eng = {"v": g.vector, "a": g.scalar, "p": g.tensor, "g": g, "s": g.sync}
    total, seen, wr_, rd_ = {}, {e: {} for e in eng}, {}, {}

    def need(e, toks):
        best = {}
        for t in toks:
            if t[0] not in best or best[t[0]][1] < t[1]:
                best[t[0]] = t
        for t in sorted(best.values(), key=lambda t: -len(t[3])):
            if seen[e].get(t[0], 0) < t[1]:
                eng[e].wait_ge(T.sem[t[0]], t[1])
                seen[e][t[0]] = t[1]
                for s, v in t[3].items():
                    seen[e][s] = max(seen[e].get(s, 0), v)

    def before(e, rd, wr):
        toks = []
        for k in rd:
            toks += wr_.get(k, {}).values()
            if k in PS:
                toks += [t for t in rd_.get(k, {}).values() if t[2] != e]
        for k in wr:
            part = k[0] == "+" or (e == "p" and k in PS)
            k = k.strip("+")
            toks += [t for t in wr_.get(k, {}).values() if not (part and t[2] == e)]
            toks += rd_.get(k, {}).values()
        need(e, toks)

    def after(tok, rd, wr):
        for k in wr:
            part = k[0] == "+"
            k = k.strip("+")
            if not part:
                wr_[k] = {}
            wr_.setdefault(k, {})[tok[0]] = tok
            rd_[k] = {}
        for k in rd:
            if k not in wr:
                rd_.setdefault(k, {})[tok[0]] = tok

    def em(e, fn, rd, wr):
        rd, wr = rd.split(), wr.split()
        before(e, rd, wr)
        s = "c" + e
        total[s] = total.get(s, 0) + 1
        fn().then_inc(T.sem[s], 1)
        after((s, total[s], e, dict(seen[e])), rd, wr)

    nd = [0]

    def dma(e, out, in_, rd, wr):
        rd, wr = rd.split(), wr.split()
        before(e, rd, wr)
        s = "d%d" % nd[0]
        nd[0] += 1
        total[s] = 16
        eng[e].dma_start(out, in_).then_inc(T.sem[s], 16)
        after((s, 16, e if e == "s" else "D", dict(seen[e])), rd, wr)

    def send(out, in_, rs, ls, rd):
        before("g", rd.split(), [])
        rid, pid = topo.addr(nxt, core)
        g.remote_dma(out, in_, T.sem[rs], T.sem[ls], pid, rid, topo.mask(core, nxt))
        total[ls] = len(topo.engines(core, nxt))
        total[rs] = len(topo.engines(prv, core))
        after((ls, total[ls], "D", {}), rd.split(), [])

    def landed(rs, key):
        wr_[key] = {rs: (rs, total[rs], "N", {})}

    def cp(out, in_, rd, wr):
        em("v", lambda: g.vector.tensor_copy(out, in_), rd, wr)

    def tt(out, a, b, op, rd, wr):
        em("v", lambda: g.vector.tensor_tensor(out, a, b, op), rd, wr)

    def ts(out, a, s1, op0, rd, wr, s2=None, op1=None):
        if op1 is None:
            em("v", lambda: g.vector.tensor_scalar(out, a, s1, None, op0), rd, wr)
        else:
            em("v", lambda: g.vector.tensor_scalar(out, a, s1, s2, op0, op1), rd, wr)

    def ms(ap, c, wr):
        em("v", lambda: g.vector.memset(ap, c), "", wr)

    def act(out, in_, fn, rd, wr, bias=0.0, scale=1.0):
        em("a", lambda: g.scalar.activation(out, in_, fn, bias=bias, scale=scale), rd, wr)

    def mm(out, l, r, start, stop, rd, wr):
        em("p", lambda: g.tensor.matmul(out, l, r, start, stop), rd, wr)

    def gat(e, out, win, off, rd, wr):
        if e == "v":
            cp(out, win.indirect(off), rd, wr)
        else:
            act(out, win.indirect(off), F.Copy, rd, wr)

    def ext(key, sel, src, rd, o=0, n=64):
        for q in range(16):
            mm(T[key][:, 0:n], T[sel][:, q * 128:(q + 1) * 128], src[:, 16 * o + q:16 * (o + n):16], q == 0, q == 15,
               rd + " SELG " + sel, key)

    def iota(nm, pat, cm, a=0, b=None):
        kw = {} if SCRATCH[nm][2] == "int32" else {"allow_small_or_imprecise_dtypes": True}
        em("g", lambda: g.iota(T[nm][:, a:b or SCRATCH[nm][1][1]], pat, 0, cm, **kw), "", "+" + nm)

    GN_, LN_ = T.NEW[:, 64:128], T.NEW[:, 128:192]
    AK, H, GA, TQ, S = [T.pW[:, 192 + 64 * i:256 + 64 * i] for i in range(5)]

    dma("s", T.SI[:], T.succ[:], "", "SI")
    dma("a", T.EI[:, 0:64], T.ea[:], "", "EIa")
    dma("a", T.EI[:, 64:128], T.eb[:], "", "EIb")
    dma("s", T.XA[:, 0:3072], T.x[:], "", "X0a X0b X0c X0d X0f X0g X0i")

    iota("PI", [[1, 1]], 1)
    iota("IO", [[1, 128]], 0)
    iota("IH", [[1, 4], [0, 64]], 0)
    iota("IL", [[0, 4], [1, 64]], 0)
    iota("BD", [[16, 8], [0, 16]], 0)
    iota("UI", [[1, 192]], 192)
    for b in "AB":
        ms(T["X" + b][:, 3072:SELF], -1.0, "X%de" % (b == "B"))
    ms(T.SW[:, 3072:3088], 0.0, "SW")
    ms(T.S2G[:], 0.0, "S2G")
    ms(T.NEG[:], -1.0, "NEG")
    ts(T.QI[:], T.PI[:], 15, A.bitwise_and, "PI", "QI")
    ts(T.GI[:], T.PI[:], 112, A.bitwise_and, "PI", "GI")
    cp(T.PF[:], T.PI[:], "PI", "PF")
    for b in "AB":
        ms(T["X" + b][:, TOP:TOP + 1], 256.0, "X%de" % (b == "B"))
    cp(T.QF[:], T.QI[:], "QI", "QF")
    cp(T.GFC[:], T.GI[:], "GI", "GFC")
    ts(T.EQ[:], T.IO[:, 0:16], T.QF[:], A.is_equal, "IO QF", "EQ")
    for nm, sc in (("IDN", -1.0), ("IDP", 1.0)):
        ts(T[nm][:], T.IO[:], T.PF[:], A.is_equal, "IO PF", nm, sc, A.mult)
    ts(T.GQ[:], T.IO[:, 0:16], T.GFC[:], A.add, "IO GFC", "GQ")
    ts(T.GC[:], T.GFC[:], -192.0, A.mult, "GFC", "GC")
    ts(T.N1[:], T.EQ[:, 15:16], -1.0, A.mult, "EQ", "N1", 1.0, A.add)
    ts(T.N2[:], T.EQ[:, 15:16], -2048.0, A.mult, "EQ", "N2", 2048.0, A.add)
    ts(T.EC[:], T.EQ[:], T.EQ[:, 15:16], A.max, "EQ", "EC")
    ts(T.KB[:], T.IO[:, 0:16], T.EQ[:, 0:1], A.mult, "IO EQ", "KB", 4.0, A.mult)
    ts(T.WR[:, 0:W], T.IO[:, 0:W], T.EQ[:, 15:16], A.mult, "IO EQ N1", "WR", T.N1[:], A.add)
    ts(T.WR[:, W:2 * W], T.IO[:, 0:W], T.EQ[:, 15:16], A.mult, "IO EQ N2", "+WR", T.N2[:], A.add)
    ts(T.E4[:], T.EQ[:], 1.0 / 4096, A.mult, "EQ", "E4")
    for r, src in enumerate(("IH", "IL")):
        ts(T["FL%d" % r][:], T.IDP[:], T.EQ[:, r:r + 1], A.mult, "IDP EQ", "FL%d" % r)
        mm(T.pA[:, 0:256], T["FL%d" % r][:], T[src][:], r == 0, r == 1, "FL%d %s" % (r, src), "pA")
    for k in range(13):
        w = 256 if k < 12 else 16
        act(T.DG[:, 256 * k:256 * k + w], T.pA[:, 0:w], F.Identity, "pA KB", "+DG", bias=T.KB[:, k:k + 1])
    for k in range(13):
        a, w = 2 * W * k, min(2 * W, 3072 - 2 * W * k)
        ts(T.SW[:, a:a + w], T.WR[:, 0:w], T.EC[:, k + 2:k + 3], A.mult, "WR EC", "+SW0 +SW1")
        if k == 5:
            ts(T.BD[:], T.BD[:], T.GFC[:], A.is_equal, "BD GFC", "BD", 4096.0, A.mult)
    ts(T.pW[:, 0:192], T.UI[:], T.GC[:], A.add, "UI GC pW", "wT")
    ts(T.WT[:], T.E4[:, 0:1], 64.0, A.mult, "E4", "WT", T.E4[:, 1:2], A.add)
    tt(T.P3[:, 0:64], T.EI[:, 0:64], T.EI[:, 64:128], A.max, "EIa EIb", "+P3")
    tt(T.P3[:, 64:128], T.EI[:, 0:64], T.EI[:, 64:128], A.min, "EIa EIb", "+P3")
    tt(T.Y3[:], T.pW[:, 0:192], T.SI[:], A.is_equal, "SI wT pW", "Y3")
    ts(T.W2[:], T.SI[:], 63, A.bitwise_and, "SI", "W2")
    ts(T.W1[:], T.SI[:], 6, A.arith_shift_right, "SI", "W1")
    ts(T.pW[:, 192:384], T.Y3[:], SELF / 64, A.mult, "Y3 pW", "wAK wH wGA")
    cp(T.D1[:], T.W2[:], "W2", "D1")
    dma("s", T.SW[1:128:16, 0:3072], T.D1[:], "D1", "SW1")
    tt(T.D0[:], T.pW[:, 192:384], T.W1[:], A.add, "W1 wAK pW", "D0")
    dma("s", T.SW[0:128:16, 0:3072], T.D0[:], "D0", "SW0")
    cp(T.ED[:], T.P3[:], "P3", "ED")
    for q in range(16):
        sel = T.SELM[:, q * 128:(q + 1) * 128]
        if q < QV:
            ts(sel, T.IO[:], T.GQ[:, q:q + 1], A.is_equal, "IO GQ", "+SELM", 4096.0, A.mult)
        else:
            em("g", lambda: g.affine_select(sel, T.BD[:], [[0, 8], [1, 16]], A.is_equal, 0.0, -q, 0), "BD", "+SELG")
    iota("LV", [[16, 64]], 0)
    for i, b in enumerate((1, 2, 3, 5)):
        iota("BW", [[0, 32 >> b], [int(SIT), 2], [0, 1 << b]], 0, 64 * i, 64 * i + 64)

    def more_constants():
        sel = T.SELM[:, 0:128:16]
        cp(T.SW[:, TOP:TOP + 1], T.DG[:, TOP:TOP + 1], "DG", "SW")
        ts(T.DG[:, ROOT:ROOT + 1], T.EQ[:, 0:1], 127.0, A.mult, "EQ", "DG")
        ts(T.M2[:], sel, -2.0 ** -17, A.mult, "SELM", "M2")
        ts(T.S2L[:], sel, T.WT[:], A.mult, "SELM WT", "S2L", -2.0 ** -17, A.mult)
        ts(T.S2G[:, 0:8], sel, T.WT[:], A.mult, "SELM WT", "S2G", 2.0 ** -17, A.mult)
        ts(T.BASE[:, 0:64], T.LV[:], T.QF[:], A.add, "LV QF", "TR", 3088.0, A.add)

    def at(c):
        return ("AT0", "AT2", "AT1", "AT1")[c // 2]

    def own_x(e, X, xk, h):
        gat(e, T.XL[:, 512 * h:512 * h + 512], X[:, 0:3088], T.GL16[:, 64 + 32 * h:96 + 32 * h], xk + " L16", "XL%d" % h)

    def own_digits(e, h, a=0, b=32):
        a, b = 32 * h + a, 32 * h + b
        gat(e, T.LD[:, 16 * a:16 * b], T.DG[:], T.GL16[:, 64 + a:64 + b], "DG L16", "LD2" if e == "v" else "+LD%d" % h)

    def minus_own(p):
        a, b, bank, db = PIECES[p]
        mm(T[db][:, 0:128 * (b - a)], T.IDN[:], T.XL[:, 128 * a:128 * b], True, False, "IDN XL0 XL1", db)

    def clear_counts(h):
        mm(T[HB[h]][:, 0:64], T.IDP[:], T.NEG[:, 0:64], True, False, "IDP NEG", HB[h])

    def unsit():
        act(T.K[:], GN_, F.Abs, "NG", "K", bias=-SIT)

    def round_start(n, X, xk):
        if n == 0:
            lst, lk = T.ED, "ED"
        else:
            lst, lk = T["LP%d" % (n - 1)], "LP%d" % (n - 1)
            landed("r%d" % (n - 1), lk)
        m, X = 16 * RS, X[:, 0:3088]
        rd = xk + " " + lk
        vs, ss = ((0, RV, "0"), (RV, RS, "1 2")), ((RS, RA, "pC", "a"), (RA, 64, "pD", "b"))
        gat("a", T.XL[:, m:1024], X, lst[:, 64 + RS:128], rd, "XL1")
        for a, b, bank, key in ss:
            mm(T[bank][:, 0:16 * (b - a)], T.IDN[:], T.XL[:, 16 * a:16 * b], True, False, "IDN XL1", bank)
        for a, b, bank, key in ss:
            gat("a", T.XS[:, 16 * a:16 * b], X, lst[:, a:b], rd, "XS" + key)
            mm(T[bank][:, 0:16 * (b - a)], T.IDP[:], T.XS[:, 16 * a:16 * b], False, True, "IDP XS" + key, bank)
        for a, b, bank, key in ss:
            act(T.SG[:, 16 * a:16 * b], T[bank][:, 0:16 * (b - a)], F.Sign, bank, "+SG3")
        gat("v", T.XL[:, 0:16 * RV], X, lst[:, 64:64 + RV], rd, "XL0")
        gat("v", T.XL[:, 16 * RV:m], X, lst[:, 64 + RV:64 + RS], rd, "XL2")
        for a, b, key in vs:
            tt(T.DD[:, 16 * a:16 * b], X.indirect(lst[:, a:b]), T.XL[:, 16 * a:16 * b], A.subtract,
               rd + (" XL2" if a else " XL0"), " ".join("DD" + c for c in key.split()))
        for a, b, key in vs:
            ts(T.SG[:, 16 * a:16 * b], T.DD[:, 16 * a:16 * b], 1.0, A.min, " ".join("DD" + c for c in key.split()),
               " ".join("SG" + c for c in key.split()), -1.0, A.max)
        ext("pA", "SELM", T.SG, "SG0 SG1 SG2 SG3")
        cp(T.PF2[:], lst[:], lk, "PF2")
        tt(T.D[:], T.PF2[:, 0:64], T.PF2[:, 64:128], A.add, "PF2", "D")
        clear_counts(0)
        if n == 0:
            act(T.SELS[:], T.SELM[:], F.Identity, "SELM SELG WT", "SELS", scale=T.WT[:])
            more_constants()
            before("g", ["SG3"], [])
            send(T.EDN[:], T.ED[:], "re", "se", "ED")
        if n < 2:
            if n == 1:
                landed("re", "EDN")
            e = T.ED if n == 0 else T.EDN
            cp(T.EF[:], e[:], "ED" if n == 0 else "EDN", "EF")
        tt(AK, T.pA[:, 0:64], T.PF2[:, 0:64], A.min, "pA PF2 pW", "wAK")
        tt(GN_, AK, T.PF2[:, 64:128], A.max, "wAK PF2 pW", "NG")
        cp(T.GL16[:, 0:64], GN_, "NG", "G16")
        tt(LN_, T.D[:], GN_, A.subtract, "D NG", "NL")

    def step(n, k, X, xk):
        t = ST * n + k
        last = k == ST - 1
        final = last and n == RO - 1
        ns, a1, v2, a2, t3, v3, a3, js = AT0 if k == 0 else ATK
        his = [b for b in range(32, 64) if b % 8 >= 4][:ns]
        mine = sorted((b for b in range(64) if b not in his), key=lambda b: (b >= 48 and b % 8 >= 4, b))
        XW = X[:, 0:3088]

        def ties(p):
            a, b, bank = PIECES[p][0:3]
            for c in range(a, b):
                w = 8 * (b - a) if c == a else 8
                mm(T[bank][:, 8 * (c - a):8 * (c - a) + w], T.GS[:, 128 * c:128 * c + 128], T.S2G[:, 0:w], c == a, False,
                   "GS%d S2G" % (c // 2), bank)
            for c in range(a, b):
                mm(T[bank][:, 8 * (c - a):8 * (c - a) + 8], T.LD[:, 128 * c:128 * c + 128], T.S2L[:], False, False,
                   "S2L " + ("LD0", "LD1 LD2")[c // 4], bank)

        def diff(p):
            a, b = PIECES[p][0:2]
            tt(T.DD[:, 128 * a:128 * b], XW.indirect(T.S16[:, 8 * a:8 * b]), T.XL[:, 128 * a:128 * b], A.subtract,
               xk + " S160 XL%d" % (p // 2 * 2), "DD%d" % p)

        def clip(p):
            a, b = PIECES[p][0:2]
            ts(T.SG[:, 128 * a:128 * b], T.DD[:, 128 * a:128 * b], 1.0, A.min, "DD%d" % p, "SG%d" % p, -1.0, A.max)

        def fetch(p):
            a, b = PIECES[p][0:2]
            gat("a", T.XS[:, 128 * a:128 * b], XW, T.S16[:, 8 * a:8 * b], xk + " S16%d" % (p - 2), "XS" + "ab"[p - 2])

        def plus(p):
            a, b, bank, db = PIECES[p]
            mm(T[db][:, 0:128 * (b - a)], T.IDP[:], T.XS[:, 128 * a:128 * b], False, True, "IDP XS" + "ab"[p - 2], db)

        def sign(p):
            a, b, bank, db = PIECES[p]
            act(T.SG[:, 128 * a:128 * b], T[db][:, 0:128 * (b - a)], F.Sign, db, "SG%d" % p)

        def votes(p):
            a, b, bank = PIECES[p][0:3]
            for c in range(a, b):
                mm(T[bank][:, 8 * (c - a):8 * (c - a) + 8], T.SG[:, 128 * c:128 * c + 128], T.M2[:], False, c == b - 1,
                   "M2 SG%d" % p, bank)

        def asks(p):
            a, b, bank = PIECES[p][0:3]
            ts(T.AK2[:, 8 * a:8 * b], T[bank][:, 0:8 * (b - a)], 0.0, A.is_gt, bank, "AK%d" % p)

        def patch():
            for r in (0, 1):
                dma("s", T.SR[r:128:16, :], T.LD[r:128:16, :], "LD0 LD1 LD2 SR", "SR%d" % r)

        def o_h():
            tt(H, GN_, T.K[:], A.min, "NG K pW", "wH")

        def o_q():
            ts(T.Q[:], GN_, 1.0 / (2 * W), A.mult, "NG", "Q", 0.25 / W - 0.5, A.add)

        def o_tq():
            ts(TQ, T.Q[:], -2.0 * W, A.mult, "Q pW", "wTQ")

        def o_of():
            tt(T.OF[:], TQ, GN_, A.add, "wTQ NG pW", "OF")

        def o_of16():
            cp(T.OF16[:], T.OF[:], "OF", "OF16")

        def o_ht():
            tt(T.HT[:], H, T.BASE[:, 0:64], A.subtract, "wH TR pW", "HT")

        def o_ga():
            u = (t + 1) % LB
            if last:
                pass
            elif u < 4:
                ts(GA, H, T.BC[:, u:u + 1], A.add, "wH BC pW", "wGA")
            else:
                i = (5, 6, 7, 9).index(u)
                tt(GA, H, T.BW[:, 64 * i:64 * i + 64], A.add, "wH BW pW", "wGA")

        ga, gk = (H, "wH") if last else (GA, "wGA")

        def o_e1():
            if not final:
                tt(T.E1[:], LN_, ga, A.subtract, "NL pW " + gk, "E1")

        def o_s():
            cp(S, T.S16[:], "S160 S161 pW", "wS")

        def o_d():
            tt(T.D[:], S, LN_, A.subtract, "wS NL pW", "D")

        def o_s2():
            if not final:
                tt(T.S2[:], S, T.K[:], A.min, "wS K pW", "S2")

        def o_el():
            if not final:
                ts(TQ, T.D[:], 0.0, A.is_equal, "D pW", "wTQ", float(ROOT), A.mult)

        def o_e2():
            if not final:
                tt(T.E2[:], ga, T.S2[:], A.subtract, "S2 pW " + gk, "E2")

        def o_bl():
            if not final:
                tt(T.BASE[:, 128:192], TQ, LN_, A.max, "NL wTQ pW", "BL")

        def where(b):
            c, gr = b // 8, b % 8
            return c, gr, 128 * c + 16 * gr + 15, str([p[0] <= c < p[1] for p in PIECES].index(True))

        def far(b):
            c, gr, o, bank = where(b)
            act(T.BT[:, W * b:W * b + W], T.IO[:, 0:W], F.Abs, "IO " + at(c), "BT%d" % b,
                bias=T.AT[:, o:o + 1], scale=-1.0)

        def hit(b):
            act(T.BB[:, W * b:W * b + W], T.BT[:, W * b:W * b + W], F.Relu, "BT%d AK%s" % (b, where(b)[3]), "BB%d" % b,
                bias=T.AK2[:, b:b + 1], scale=-1.0)

        done = []

        def count(b):
            c, gr, o, bank = where(b)
            done.append(b)
            bank, a = HB[gr // 4], 16 * (gr % 4)
            mm(T[bank][0:W, a + 2:a + 15], T.BB[:, W * b:W * b + W], T.AT[:, o - 13:o], False,
               sum(d % 8 // 4 == gr // 4 for d in done) == 32, "BB%d %s" % (b, at(c)), bank)

        if k == 0:
            o_q()
        for i in range(4):
            gat("va"[i % 2], T.GS[:, 256 * i:256 * i + 256], T.SW[:, 0:3088], T.GL16[:, 16 * i:16 * i + 16], SW + " G16", "GS%d" % i)
            if k == 0 and i == 0:
                cp(T.GL16[:, 64:128], LN_, "NL", "L16")
        dma("s", T.SR[:], T.GS[:], "GS0 GS1 GS2 GS3", "SR SR0 SR1")
        ext("pS", "SELS", T.GS, "GS0 GS1", 0, 32)
        ext("pB", "SELS", T.GS, "GS2 GS3", 32, 32)

        def listed(h):
            ts(T.S16[:, 32 * h:32 * h + 32], T["pB" if h else "pS"][:, 0:32], float(ROOT), A.min, "pB" if h else "pS", "S16%d" % h)
        for c in range(8):
            em("p", lambda: g.tensor.transpose(T.pT[:, 128 * c:128 * c + 128], T.GS[:, 128 * c:128 * c + 128], T.IDP[:]),
               "IDP GS%d" % (c // 2), "pT")
        if k == 0:
            gat("v", T.XL[:, 0:256], XW, T.GL16[:, 64:80], xk + " L16", "XL0")
            cp(H, GN_, "NG pW", "wH")
            o_tq()
            own_digits("a", 0)
            unsit()
            own_x("a", X, xk, 1)
        else:
            own_digits("v", 1, LX)
            own_digits("a", 1, 0, LX)
            o_q()
        listed(0)
        if k:
            o_h(), o_tq()
        else:
            gat("v", T.XL[:, 256:512], XW, T.GL16[:, 80:96], xk + " L16", "XL2")
        ties(0)
        diff(0)
        if k:
            fetch(2)
        listed(1)
        fetch(3)
        if k:
            o_of()
        clip(0)
        diff(1)
        votes(0)
        if k:
            plus(2)
        ties(1), ties(2)
        cp(T.AT[:, 0:256], T.pT[:, 0:256], "pT", "AT0")
        clip(1)
        votes(1)
        asks(0)
        cp(T.AT[:, 256:512], T.pT[:, 256:512], "pT", "AT2")
        if k:
            sign(2)
            act(T.AT[:, 512:1024], T.pT[:, 512:1024], F.Copy, "pT", "AT1")
            o_s()
            plus(3)
            sign(3)
        else:
            clear_counts(1)
            own_digits("a", 1)
            diff(2)
            minus_own(3)
            plus(3)
            sign(3)
            act(T.AT[:, 512:1024], T.pT[:, 512:1024], F.Copy, "pT", "AT1")
        for b in his:
            far(b)
        m = 16 * GP
        for i, b in enumerate(mine):
            c, gr, o, p = where(b)
            if i == a1:
                asks(1)
            if i == v2:
                if k == 0:
                    clip(2)
                votes(2)
                if k:
                    clear_counts(1)
            if i == a2:
                asks(2)
            if i == t3:
                ties(3)
                patch()
            if i == v3:
                votes(3)
            if i == a3:
                asks(3)
                for b2 in his:
                    hit(b2)
            ts(T.BB[:, W * b:W * b + W], T.IO[:, 0:W], T.AT[:, o:o + 1], A.is_equal, "IO AK%s %s" % (p, at(c)),
               "BB%d" % b, T.AK2[:, b:b + 1], A.mult)
            count(b)
            if i >= js and (i - js) % 2 == 0 and (i - js) // 2 < ns:
                count(his[(i - js) // 2])
        if k == 0:
            o_s()
        if t == 0:
            for u in range(4):
                ts(T.BI[:, u:u + 1], T.QI[:], u, A.arith_shift_right, "QI", "+BI", 1, A.bitwise_and)
            act(T.SELF[:], T.SELM[:], F.Copy, "SELM", "SELF", scale=1.0 / 4096)
        act(T.GN[:, 0:1024 - m], T.GS[:, m:1024], F.Sign, "GS2 GS3", "GN")
        for h, bank in enumerate(HB):
            P, a = T[bank][0:W, 0:64], 64 * h
            ts(T.RR[0:W, a:a + 64], P, MAGIC, A.add, bank, "RR%d" % h, MAGIC, A.subtract)
            ts(T.FL1[0:W, a:a + 64], P, MAGIC, A.add, bank, "+FL1", MAGIC + 2048, A.is_equal)
            if h:
                o_d()
            elif k:
                o_of16()
            else:
                o_of()
            tt(T.FL0[0:W, a:a + 64], P, T.RR[0:W, a:a + 64], A.is_equal, bank + " RR%d" % h, "+FL0")
        mm(T.pS[:, 0:W], T.FL1[0:W, :], T.IDP[0:W, 0:W], True, True, "IDP FL1", "pS")
        act(T.FT[:, W:2 * W], T.pS[:, 0:W], F.Copy, "pS", "FT1")
        em("p", lambda: g.tensor.transpose(T.pT[:, 0:W], T.FL0[0:W, :], T.IDP[0:W, 0:W]), "IDP FL0", "pT")
        fl = ((GP, G2, "pD", "XSb"), (G2, 64, "pA", "XSj"))
        for a, b, bank, key in fl:
            mm(T[bank][:, 0:16 * (b - a)], T.IDP[:], T.GN[:, 16 * a - m:16 * b - m], True, False, "IDP GN", bank)
        ext("pB", "SELM", T.SG, "SG0 SG1 SG2 SG3")
        if k == 0:
            o_of16()
        if t == 0:
            ts(T.BC[:], T.BI[:], SIT, A.mult, "BI", "BC")
        o_s2(), o_ht(), o_el(), o_ga()
        win = T.FT[:, 0:2 * W]
        cp(T.FT[:, 0:W], T.pT[:, 0:W], "pT", "FT")
        o_bl(), o_e2()
        tt(T.GF[:, 0:m], win.indirect(T.OF16[:, 0:GP]), T.GS[:, 0:m], A.min, "FT FT1 OF16 GS0 GS1 GS2 GS3", "GF0")
        for a, b, bank, key in fl:
            gat("a", T.XS[:, 16 * a:16 * b], win, T.OF16[:, a:b], "FT FT1 OF16", key)
            mm(T[bank][:, 0:16 * (b - a)], T.IDP[:], T.XS[:, 16 * a:16 * b], False, True, "IDP " + key, bank)
        for a, b, bank, key in fl:
            act(T.GF[:, 16 * a:16 * b], T[bank][:, 0:16 * (b - a)], F.Relu, bank, "+GF1", bias=-1.0)
        ext("pS", "SELF", T.GF, "GF0 GF1")
        tt(AK, T.pB[:, 0:64], T.D[:], A.is_lt, "pB D pW", "wAK")
        o_e1()
        if t == 0:
            ts(T.ID6[:], T.IO[:], T.PF[:], A.is_equal, "IO PF", "ID6", 64.0, A.mult)
        if not final:
            tt(TQ, AK, T.E2[:], A.mult, "wAK E2 pW", "wTQ")
        tt(T.DV[:, 0:64], AK, T.HT[:], A.mult, "wAK HT pW", "+DV")
        if not final:
            tt(T.DV[:, 64:128], AK, T.E1[:], A.mult, "wAK E1 pW", "+DV")
            tt(T.DV[:, 128:192], AK, T.D[:], A.mult, "wAK D pW", "+DV")
            tt(T.BASE[:, 64:128], TQ, T.S2[:], A.add, "wTQ S2 pW", "BG")
        parts = (0,) if final else (0, 2, 1)
        for i in parts:
            tt(T.pW[:, 64 * i:64 * i + 64], T.pS[:, 0:64], T.DV[:, 64 * i:64 * i + 64], A.mult, "pS DV pW wT", "wT%d" % i)
        for i in parts:
            tt(T.NEW[:, 64 * i:64 * i + 64], T.pW[:, 64 * i:64 * i + 64], T.BASE[:, 64 * i:64 * i + 64], A.add,
               "wT%d pW wT %s" % (i, ("TR", "BG", "BL")[i]), ("NC", "NG", "NL")[i])
        cp(T.SC16[:], T.NEW[:, 0:64], "NC", "SC16")
        if not last:
            cp(T.GL16[:, 64:128], LN_, "NL", "L16")
            ts(T.GL16[:, 0:64], GN_, float(TOP), A.min, "NG", "G16")
            own_x("a", X, xk, 0)
            own_digits("a", 0)
            unsit()
            own_x("a", X, xk, 1)
            clear_counts(0)
            minus_own(2), minus_own(3)
        if k == 0:
            dma("s", X[:, SELF:SELF + 3072], X[:, 0:3072], xk + " SC16", xk[0:2] + "h")
        em("v", lambda: g.vector.tensor_copy(T.SW[:].indirect(T.SC16[:]), T.SR[:]), "SC16 SR SR0 SR1", SW)

    def pass_on(n):
        yield ts(T.UP[:], LN_, float(ROOT), A.is_equal, "NL", "UP")
        yield tt(T.RR[:, 0:64], GN_, LN_, A.max, "NG NL", "RR0")
        yield tt(T.RR[:, 64:128], GN_, LN_, A.min, "NG NL", "RR1")
        yield tt(T.PF2[:], T.EF[:], T.RR[:], A.subtract, "EF RR0 RR1", "PF2")
        yield tt(T.P3[:, 0:64], T.PF2[:, 0:64], T.UP[:], A.mult, "PF2 UP", "+P3")
        yield tt(T.P3[:, 64:128], T.PF2[:, 64:128], T.UP[:], A.mult, "PF2 UP", "+P3")
        yield tt(T.P4[:], T.P3[:], T.RR[:], A.add, "P3 RR0 RR1", "P4")
        sp = "SP%d" % n
        cp(T[sp][:], T.P4[:], "P4", sp)
        yield send(T["LP%d" % n][:], T[sp][:], "r%d" % n, "s%d" % n, sp)

    def round_end(n, X, xk, Y, yk):
        final = n == RO - 1
        key, xh, SEG = "abcdfgi", xk + " " + xk[0:2] + "h ", SEGS[final]

        def ahead(i):
            a, b, e, bank = SEG[i]
            if e == "v":
                act(T.XP[:, a:b], X[:, a:b], F.Identity, xk, "+XP", bias=1.0)
                act(T[bank][:, 0:b - a], X[:, a:b], F.Identity, xk, bank, bias=-1.0)
            else:
                mm(T[bank][:, 0:b - a], T.IDN[:], X[:, a:b], True, False, "IDN " + xk, bank)
        for i in range(6):
            ahead(i)
        if final:
            dma("s", T.D0[:], T.SW[0:128:16, 0:3072], SW, "D0")
            dma("s", T.D1[:], T.SW[1:128:16, 0:3072], SW, "D1")

        def lists(c):
            ext(("pS", "pD")[c % 2], "SELS", T.SW, SW, 64 * c)

        def listed(c):
            bank = ("pS", "pD")[c % 2]
            cp(T.SL16[:, 64 * c:64 * c + 64], T[bank][:, 0:64], bank, "SL%d" % c)

        def lk(a, b):
            return " ".join("SL%d" % c for c in range(a // 1024, (b - 1) // 1024 + 1))

        def fetch(i):
            a, b, e, bank = SEG[i]
            if e == "v":
                tt(T.DD[:, a:b], X[:].indirect(T.SL16[:, a // 16:b // 16]), T.XP[:, a:b], A.min,
                   xh + "XP " + lk(a, b), "DD0 DD1 DD2 DD" + key[i] if a < 1024 else "DD" + key[i])
            else:
                gat("a", T.XS[:, a:b], X[:], T.SL16[:, a // 16:b // 16], xh + lk(a, b), "XS" + key[i])

        def minus(i):
            a, b, e, bank = SEG[i]
            mm(T[bank][:, 0:b - a], T.IDP[:], T.XS[:, a:b], False, True, "IDP XS" + key[i], bank)

        def sign(i):
            a, b, e, bank = SEG[i]
            if e == "a":
                act(T[bank][:, 0:b - a], T[bank][:, 0:b - a], F.Sign, bank, bank)
            else:
                act(T.GN[:, 0:b - a], T[bank][:, 0:b - a], F.Sign, bank, "GN")
                mm(T[bank][:, 0:b - a], T.IDP[:], X[:, a:b], True, False, "IDP " + xk, bank)
                mm(T[bank][:, 0:b - a], T.IDP[:], T.GN[:, 0:b - a], False, True, "IDP GN", bank)

        def put(i):
            a, b, e, bank = SEG[i]
            if e == "c":
                act(Y[:, a:b], T[bank][:, 0:b - a], F.Copy, bank, yk + key[i])
            elif e == "v":
                tt(Y[:, a:b], T[bank][:, 0:b - a], T.DD[:, a:b], A.max, bank + " DD" + key[i], yk + key[i])
            else:
                tt(Y[:, a:b], T[bank][:, 0:b - a], X[:, a:b], A.add, bank + " " + xk, yk + key[i])
            if final:
                dma("s", T.yx[:, a:b], Y[:, a:b], yk + key[i], "ox" + key[i])

        if final:
            lists(0), lists(1), listed(0), lists(2), listed(1), ahead(6), fetch(0), fetch(1), listed(2), minus(0), fetch(2)
            sign(0), fetch(4), put(1), minus(2), fetch(3), sign(2), put(0)
            ts(T.D2[:], T.D0[:], SELF / 64, A.is_ge, "D0", "D2", -SELF / 64, A.mult)
            minus(3), fetch(6), sign(3)
            for i, (w, d) in enumerate((("ID6", "D0"), ("IDP", "D1"), ("ID6", "D2"))):
                mm(T.pS[:, 0:192], T[w][:], T[d][:], i == 0, i == 2, w + " " + d, "pS")
            minus(6), sign(6), put(4), fetch(5)
            cp(T.Y3[:], T.pS[:, 0:192], "pS", "Y3")
            dma("s", T.ys[:], T.Y3[:], "Y3", "oy")
            put(2), put(3), put(6), put(5)
            return
        on = pass_on(n)

        def go(c):
            for _ in range(c):
                next(on)
        lists(0), lists(1), go(4), listed(0), lists(2), fetch(0), fetch(1), go(2), listed(1), ahead(6), go(1), fetch(2), go(1)
        listed(2), minus(0), minus(1), sign(0)
        fetch(3), sign(1), put(2), fetch(4), minus(3), fetch(6), sign(3), minus(6), put(0), sign(6)
        fetch(5), put(4), put(1), put(5), put(3), put(6)

    X, Y, xk, yk = T.XA, T.XB, "X0", "X1"
    for n in range(RO):
        xr = " ".join(xk + c for c in "abcdefgi")
        round_start(n, X, xr)
        for k in range(ST):
            step(n, k, X, xr)
        round_end(n, X, xr, Y, yk)
        X, Y, xk, yk = Y, X, yk, xk
    for s, v in total.items():
        if seen["g"].get(s, 0) < v:
            g.wait_ge(T.sem[s], v)
